import numpy as np
import ml_dtypes


def mxq(x, axis, fmt="e4m3"):
    dtype, down = {"e4m3": (ml_dtypes.float8_e4m3fn, 7), "e5m2": (ml_dtypes.float8_e5m2, 14)}[fmt]
    v = np.moveaxis(np.asarray(x, np.float32).astype(ml_dtypes.bfloat16).astype(np.float64), axis, -1)
    blocks = v.reshape(v.shape[:-1] + (-1, 32))
    amax = np.abs(blocks).max(-1, keepdims=True)
    byte = np.maximum(np.where(amax > 0, np.frexp(amax)[1] - 1 + 127, 0) - down, 1)
    scale = np.exp2(byte - 127.0)
    codes = (blocks / scale).astype(np.float32).astype(dtype).astype(np.float64)
    return np.moveaxis((codes * scale).reshape(v.shape), -1, axis)


WIDE = False


def mx_kscale(k):
    if not WIDE:
        return np.ones(k)
    levels = np.array([10, -10, 5, -5, 0])
    if k % 512:
        return np.exp2(np.random.permutation(np.resize(levels, k // 32))).repeat(32)
    a = np.empty((k // 512, 16))
    for p in range(k // 512):
        a[p, :8] = np.random.permutation(np.resize(levels, 8))
        for g in range(8):
            far = levels[np.abs(levels - a[p, g]) >= 10]
            a[p, g + 8] = far[np.random.randint(len(far))]
    return np.exp2(a.ravel()).repeat(32)


def f64(x):
    return np.asarray(x).astype(np.float64)


def striped(idx):
    return np.tile(idx.reshape(-1, 16).T, (8, 1)).astype(np.uint16)


def unstriped(offs):
    return offs[:16].T.reshape(-1).astype(np.int64)


E2M1 = np.array([0.0, 0.5, 1.0, 1.5, 2.0, 3.0, 4.0, 6.0, -0.0, -0.5, -1.0, -1.5, -2.0, -3.0, -4.0, -6.0])


def pack_weight(w, fmt):
    k, n = w.shape
    w = f64(np.asarray(w, np.float32).astype(ml_dtypes.bfloat16)).reshape(k // 32, 32, n)
    amax = np.abs(w).max(1)
    if fmt == "e4m3":
        byte = np.frexp(amax)[1] - 1 + 127 - 7
    else:
        mant, ex = np.frexp(amax / 6.0)
        byte = np.where(mant > 0.5, ex, ex - 1) + 127
    byte = np.clip(np.where(amax > 0, byte, 1), 1, 254)
    scaled = (w * np.exp2(127.0 - byte)[:, None, :]).reshape(k, n).astype(np.float32)
    by_word = np.ascontiguousarray(scaled.reshape(k // 512, 128, 4, n).transpose(0, 1, 3, 2))
    if fmt == "e4m3":
        words = by_word.astype(ml_dtypes.float8_e4m3fn).view(np.uint8)
    else:
        c = by_word.astype(ml_dtypes.float4_e2m1fn).view(np.uint8) & 0xF
        words = (c[..., 0::2] | (c[..., 1::2] << 4)).reshape(k // 512, 128, 2 * n)
    return np.ascontiguousarray(words), np.ascontiguousarray(byte.astype(np.uint8).reshape(k // 512, 16, n))


def unpack_weight(words, scales, fmt):
    g, _, n = scales.shape
    words = np.ascontiguousarray(words).reshape(g, 128, n, -1)
    if fmt == "e4m3":
        vals = words.view(ml_dtypes.float8_e4m3fn).astype(np.float64)
    else:
        nib = np.empty((g, 128, n, 4), np.uint8)
        nib[..., 0::2] = words & 0xF
        nib[..., 1::2] = words >> 4
        vals = E2M1[nib]
    vals = vals * np.repeat(np.exp2(scales.astype(np.float64) - 127.0), 8, axis=1)[..., None]
    return vals.transpose(0, 1, 3, 2).reshape(g * 512, n)


def gelu(v):
    return 0.5 * v * (1.0 + np.tanh(np.sqrt(2.0 / np.pi) * (v + 0.044715 * v**3)))


def striped8(idx):
    return np.concatenate([v.reshape(-1, 16).T for v in idx]).astype(np.uint16)


def unstriped8(offs):
    return np.stack([offs[16 * g:16 * g + 16].T.reshape(-1) for g in range(8)]).astype(np.int64)


def heads(xT, wgt, idx8):
    k = np.arange(xT.shape[0])
    return wgt[k // 4 % 128] * xT[k[:, None], idx8[k % 512 // 64]]


K, T, S, H, N, G, P = 1024, 2048, 1024, 512, 256, 8, 16

def setup_inputs():
    n = np.random.standard_normal
    s = mx_kscale(K)[:, None]
    u = mx_kscale(H)[:, None]
    wb_words, wb_scales = pack_weight(n((K, H)) / s * u.T / np.sqrt(K), "e2m1")
    wo_words, wo_scales = pack_weight(n((H, N)) / u / np.sqrt(H), "e4m3")
    return {
        "xT": (n((K, T)) * s).astype(np.float32),
        "wgt": np.repeat(np.random.uniform(0.5, 2.0, (G, S)), P, axis=0).astype(np.float32),
        "offs": striped8(np.stack([np.random.permutation(T)[:S] for _ in range(G)])),
        "wa": (n((K, H)) / s / np.sqrt(K)).astype(np.float32),
        "ba": (0.5 * n(H)).astype(np.float32),
        "wb_words": wb_words, "wb_scales": wb_scales,
        "wc": (n((K, H)) / s * u.T / np.sqrt(K)).astype(np.float32),
        "wo_words": wo_words, "wo_scales": wo_scales,
        "bo": (0.5 * n(N)).astype(np.float32),
    }

def reference(xT, wgt, offs, wa, ba, wb_words, wb_scales, wc, wo_words, wo_scales, bo):
    xg = heads(f64(xT), f64(wgt), unstriped8(offs))
    xq = mxq(xg, 0, "e4m3")
    wb = unpack_weight(wb_words, wb_scales, "e2m1")
    wo = unpack_weight(wo_words, wo_scales, "e4m3")
    a = mxq(f64(wa), 0, "e4m3").T @ xq
    b = wb.T @ xq
    c = mxq(f64(wc), 0, "e4m3").T @ xq
    gate = 1.0 / (1.0 + np.exp(-(a + f64(ba)[:, None])))
    h = gate * b + c
    return (wo.T @ mxq(h, 0, "e4m3")) + f64(bo)[:, None]

@@ -1,0 +1,254 @@
+from contextlib import ExitStack
+
+import concourse.mybir as mybir
+
+K, T, S, H, N = 1024, 2048, 1024, 512, 256
+FLOPS = 2 * S * (3 * K * H + H * N)
+
+F32 = mybir.dt.float32
+BF16 = mybir.dt.bfloat16
+I32 = mybir.dt.int32
+U32 = mybir.dt.uint32
+U16 = mybir.dt.uint16
+U8 = mybir.dt.uint8
+FP8X4 = mybir.dt.float8_e4m3fn_x4
+FP4X4 = mybir.dt.float4_e2m1fn_x4
+ALU = mybir.AluOpType
+ACT = mybir.ActivationFunctionType
+
+P = 128
+PACK = 4
+KP = P * PACK
+PASSES = K // KP
+CH = 512
+CHUNKS = S // CH
+BLK = 128
+OUTW = 256
+
+
+def tile_list_octant_voxel_fusion_kernel(tc, xT, wgt, offs, wa, ba, wb_words, wb_scales, wc, wo_words, wo_scales, bo, out):
+    nc = tc.nc
+    with ExitStack() as ctx:
+        keep = ctx.enter_context(tc.tile_pool(name="keep", bufs=1))
+        work = ctx.enter_context(tc.tile_pool(name="work", bufs=2))
+        psum = ctx.enter_context(tc.psum_pool(name="psum", bufs=1))
+
+        offsets = keep.tile([P, S // 16], U16, name="offsets")
+        nc.sync.dma_start(offsets[:], offs)
+
+        warm = keep.tile([P, 8], F32, name="warm")
+        nc.vector.memset(warm[:, 0:1], 0.0)
+        nc.scalar.activation(warm[:, 4:5], warm[:, 0:1], ACT.Sigmoid)
+
+        wb_raw = keep.tile([P, PASSES, 2 * H], U8, name="wb_raw", align_bytes=64)
+        wbs_raw = keep.tile([P, PASSES, H], U8, name="wbs_raw", align_bytes=64)
+        wos = keep.tile([P, N], U8, name="wos", align_bytes=64)
+        nc.vector.memset(wbs_raw[:].rearrange("p a e -> p (a e)").bitcast(I32), 0)
+        nc.vector.memset(wos[:].bitcast(I32), 0)
+        nc.sync.dma_start(wb_raw[:].bitcast(I32), wb_words.rearrange("a p e -> p a e").bitcast(I32))
+        for q in range(4):
+            nc.sync.dma_start(wbs_raw[32 * q : 32 * q + 4, :, :].bitcast(I32),
+                              wb_scales[:, 4 * q : 4 * q + 4, :].rearrange("a r e -> r a e").bitcast(I32))
+
+        x_rows = xT.rearrange("(a p i) t -> a i p t", a=PASSES, i=PACK)
+        planes = {}
+        wg = []
+
+        def load_plane(a, i):
+            planes[a, i] = keep.tile([P, T], F32, name=f"x{a}{i}")
+            nc.sync.dma_start(planes[a, i][:], x_rows[a, i])
+
+        w_raw = {}
+
+        def load_w(name, w, a):
+            w_raw[name, a] = keep.tile([P, PACK, H], F32, name=f"raw_{name}{a}")
+            nc.sync.dma_start(w_raw[name, a][:], w[a * KP : (a + 1) * KP, :].rearrange("(p j) c -> p j c", j=PACK))
+
+        load_plane(0, 0)
+        for c in range(CHUNKS):
+            wg.append(keep.tile([P, CH], F32, name=f"wg{c}", tag=f"wg{c}", align_bytes=64))
+            nc.sync.dma_start(wg[c][:], wgt[:, c * CH : (c + 1) * CH])
+        load_plane(0, 1)
+        load_plane(0, 2)
+        load_plane(0, 3)
+        load_plane(1, 0)
+        load_plane(1, 1)
+        load_w("a", wa, 0)
+        load_w("a", wa, 1)
+        ba_t = keep.tile([P, PACK], F32, name="ba_t")
+        nc.sync.dma_start(ba_t[:], ba.rearrange("(p t) -> p t", t=PACK))
+        load_plane(1, 2)
+        load_plane(1, 3)
+        load_w("c", wc, 0)
+        load_w("c", wc, 1)
+        wo_c = keep.tile([P, 4 * N], U8, name="wo_c", align_bytes=64)
+        nc.sync.dma_start(wo_c[:].bitcast(I32), wo_words[0].rearrange("p e i -> p (e i)").bitcast(I32))
+        for q in range(4):
+            nc.sync.dma_start(wos[32 * q : 32 * q + 4, :].bitcast(I32), wo_scales[0, 4 * q : 4 * q + 4, :].bitcast(I32))
+        bo_t = keep.tile([P, N // P], F32, name="bo_t")
+        with nc.allow_non_contiguous_dma(reason="one bias value a partition"):
+            nc.sync.dma_start(bo_t[:], bo.rearrange("(u p) -> p u", p=P))
+
+        wb_c = keep.tile([P, PASSES, 2 * H], U8, name="wb_c", align_bytes=64)
+        wb_s = keep.tile([P, PASSES, H], U8, name="wb_s", align_bytes=64)
+        nc.vector.tensor_copy(wb_c[:].bitcast(U16).rearrange("p a (t m) -> p a t m", t=PACK),
+                              wb_raw[:].bitcast(U16).rearrange("p a (m t) -> p a t m", t=PACK))
+        nc.vector.tensor_copy(wb_s[:].rearrange("p a (t m) -> p a t m", t=PACK),
+                              wbs_raw[:].rearrange("p a (m t) -> p a t m", t=PACK))
+
+        xq, xs = {}, {}
+
+        g = {}
+        for a in range(PASSES):
+            for c in range(CHUNKS):
+                g[a, c] = keep.tile([P, PACK, CH], F32, name=f"g{a}{c}")
+                xq[a, c] = keep.tile([P, CH], U32, name=f"xq{a}{c}", align_bytes=64)
+                xs[a, c] = keep.tile([P, CH], U8, name=f"xs{a}{c}", align_bytes=64)
+
+        def gather(a, i, j0, w):
+            c, l = divmod(j0, CH)
+            nc.vector.tensor_tensor(g[a, c][:, i, l : l + w], planes[a, i][:].indirect(offsets[:, j0 // 16 : (j0 + w) // 16]),
+                                    wg[c][:, l : l + w], ALU.mult)
+
+        def weave_x(a, j0, w, copy):
+            c, l = divmod(j0, CH)
+            xb = work.tile([P, w, PACK], BF16, name="xb", tag="xb", bufs=3, align_bytes=64)
+            copy(xb[:].rearrange("p (c i) t -> p c t i", i=4), g[a, c][:, :, l : l + w].rearrange("p t (c i) -> p c t i", i=4))
+            return xb
+
+        def quant_x(a, j0, w, xb):
+            c, l = divmod(j0, CH)
+            nc.vector.quantize_mx(xq[a, c][:, l : l + w].bitcast(FP8X4), xs[a, c][:, l : l + w], xb[:].rearrange("p c t -> p (c t)"))
+
+        wq, ws, w16 = {}, {}, {}
+
+        def pool_cast(dst, src):
+            nc.gpsimd.tensor_scalar(dst, src, 1.0, 0.0, ALU.mult, ALU.add)
+
+        def cast_w(name, a, copy, part, parts):
+            if part == 0:
+                w16[name, a] = keep.tile([P, PACK, P, PACK], BF16, name=f"w16{name}{a}", align_bytes=64)
+            m = slice(part * P // parts, (part + 1) * P // parts)
+            copy(w16[name, a][:].rearrange("p t m j -> p m j t")[:, m], w_raw[name, a][:].rearrange("p j (m t) -> p m j t", t=PACK)[:, m])
+
+        def quant_w(name, a, tag):
+            wq[name, a] = keep.tile([P, H], U32, name=f"wq{name}{a}", tag=tag, align_bytes=64)
+            ws[name, a] = keep.tile([P, H], U8, name=f"ws{name}{a}", align_bytes=64)
+            nc.vector.quantize_mx(wq[name, a][:].bitcast(FP8X4), ws[name, a][:], w16[name, a][:].rearrange("p t m j -> p (t m j)"))
+
+        for i in range(PACK):
+            for c in range(CHUNKS):
+                gather(0, i, c * CH, CH)
+        woven = [weave_x(0, c * CH, CH, nc.scalar.copy) for c in range(CHUNKS)]
+        for c in range(CHUNKS):
+            gather(1, 0, c * CH, CH)
+        for c in range(CHUNKS):
+            quant_x(0, c * CH, CH, woven[c])
+        for c in range(CHUNKS):
+            gather(1, 1, c * CH, CH)
+        cast_w("a", 0, nc.scalar.copy, 0, 1)
+        quant_w("a", 0, "wqa0")
+        cast_w("a", 1, nc.scalar.copy, 0, 1)
+        for c in range(CHUNKS):
+            gather(1, 2, c * CH, CH)
+        Q = 256
+        VW = []
+        woven = []
+        for n in range(S // Q):
+            gather(1, PACK - 1, n * Q, Q)
+            woven.append(weave_x(1, n * Q, Q, nc.vector.tensor_copy if n in VW else nc.scalar.copy))
+            if n == 1:
+                quant_w("a", 1, "wg0")
+            if n >= 1:
+                quant_x(1, (n - 1) * Q, Q, woven[n - 1])
+        quant_x(1, S - Q, Q, woven[-1])
+
+        def bank():
+            return psum.tile([P, 512], F32, name="bank", tag="bank", bufs=8)
+
+        def mm_ab(c, t, a, pa, pb):
+            m = slice(t * P, (t + 1) * P)
+            nc.tensor.matmul_mx(pa[:], lhsT=wq["a", a][:, m].bitcast(FP8X4), lhsT_scale=ws["a", a][:, m],
+                                rhs=xq[a, c][:].bitcast(FP8X4), rhs_scale=xs[a, c][:], start=a == 0, stop=a == PASSES - 1)
+            nc.tensor.matmul_mx(pb[:], lhsT=wb_c[:, a, 2 * t * P : 2 * (t + 1) * P].bitcast(FP4X4), lhsT_scale=wb_s[:, a, m],
+                                rhs=xq[a, c][:].bitcast(FP8X4), rhs_scale=xs[a, c][:], start=a == 0, stop=a == PASSES - 1)
+
+        gbs = [keep.tile([P, PACK, CH], F32, name=f"gb{c}") for c in range(CHUNKS)]
+
+        def gate_b(c, t, pa, pb):
+            gate = work.tile([P, CH], F32, name="gate", bufs=3)
+            nc.scalar.activation(gate[:], pa[:], ACT.Sigmoid, bias=ba_t[:, t : t + 1])
+            nc.vector.tensor_tensor(gbs[c][:, t, :], pb[:], gate[:], ALU.mult)
+
+        PIECES = 2
+        COPY = {"scalar": nc.scalar.copy, "vector": nc.vector.tensor_copy, "gpsimd": pool_cast}
+        first = [(bank(), bank()) for t in range(PACK)]
+        for t in range(PACK):
+            mm_ab(0, t, 0, *first[t])
+        for t in range(PACK):
+            mm_ab(0, t, 1, *first[t])
+            gate_b(0, t, *first[t])
+            if t % (PACK // PIECES) == PACK // PIECES - 1:
+                cast_w("c", 0, COPY["scalar"], t // (PACK // PIECES), PIECES)
+        quant_w("c", 0, "wqc0")
+        for part in range(PIECES):
+            cast_w("c", 1, COPY["vector"], part, PIECES)
+        for t in range(PACK):
+            pa, pb = bank(), bank()
+            for a in range(PASSES):
+                mm_ab(1, t, a, pa, pb)
+            gate_b(1, t, pa, pb)
+            if t == 0:
+                quant_w("c", 1, "wqc1")
+
+        def mm_c(j0):
+            c, l = divmod(j0, CH)
+            pc = bank()
+            for t in range(PACK):
+                m = slice(t * P, (t + 1) * P)
+                for a in range(PASSES):
+                    nc.tensor.matmul_mx(pc[:, m], lhsT=wq["c", a][:, m].bitcast(FP8X4), lhsT_scale=ws["c", a][:, m],
+                                        rhs=xq[a, c][:, l : l + BLK].bitcast(FP8X4), rhs_scale=xs[a, c][:, l : l + BLK],
+                                        start=a == 0, stop=a == PASSES - 1)
+            return pc
+
+        def add_c(j0, pc, dst):
+            c, l = divmod(j0, CH)
+            nc.vector.tensor_tensor(dst.rearrange("p (c i t) -> p c t i", i=4, t=PACK), pc[:].rearrange("p (t c i) -> p c t i", i=4, t=PACK),
+                                    gbs[c][:, :, l : l + BLK].rearrange("p t (c i) -> p c t i", i=4), ALU.add)
+
+        def quant_h(w, hb):
+            hq = work.tile([P, w], U32, name="hq", tag="hq", bufs=3, align_bytes=64)
+            hs = work.tile([P, w], U8, name="hs", tag="hs", bufs=3, align_bytes=64)
+            nc.vector.quantize_mx(hq[:].bitcast(FP8X4), hs[:], hb[:])
+            return hq, hs
+
+        def finish(j0, w, hq, hs):
+            po = bank()
+            res = work.tile([P, N // P, w], F32, name="res", tag="res", bufs=5)
+            for u in range(N // P):
+                nc.tensor.matmul_mx(po[:, u * w : (u + 1) * w], lhsT=wo_c[:, 4 * u * P : 4 * (u + 1) * P].bitcast(FP8X4),
+                                    lhsT_scale=wos[:, u * P : (u + 1) * P], rhs=hq[:].bitcast(FP8X4), rhs_scale=hs[:], start=True, stop=True)
+            for u in range(N // P):
+                nc.scalar.activation(res[:, u, :], po[:, u * w : (u + 1) * w], ACT.Identity, bias=bo_t[:, u : u + 1])
+            nc.sync.dma_start(out.rearrange("(u p) j -> p u j", p=P)[:, :, j0 : j0 + w], res[:])
+
+        UNITS = [256,256,256,128,128]
+        j0 = 0
+        to_quant, to_finish = None, None
+        for w in UNITS:
+            hb = work.tile([P, w * PACK], BF16, name="hb", tag="hb", bufs=3, align_bytes=64)
+            for b in range(w // BLK):
+                pc = mm_c(j0 + b * BLK)
+                if to_finish:
+                    finish(*to_finish)
+                    to_finish = None
+                add_c(j0 + b * BLK, pc, hb[:, b * BLK * PACK : (b + 1) * BLK * PACK])
+                if to_quant:
+                    to_finish = to_quant[:2] + quant_h(to_quant[1], to_quant[2])
+                    to_quant = None
+            to_quant = (j0, w, hb)
+            j0 = j0 + w
+        if to_finish:
+            finish(*to_finish)
+        finish(*(to_quant[:2] + quant_h(to_quant[1], to_quant[2])))

@@ -23,191 +23,183 @@ PASSES = K // KP
 CH = 512
 CHUNKS = S // CH
 BLK = 128
-OUTW = 256
+CFG = {"head":256,"qs":[256,256,512],"hold":{},"units":[256,256,256,128,128],"gatebufs":3,"resbufs":5,"order":"wb wbs x00 wgh wgr x01 x02 x03 x10 x11 x12 wa0 ba x13 wa1 wc0 wc1 wo","at":{"p2":"Sa00 Sa01 qa00 qa01","l3":"Va11 qa11","l4":"","g1":"Sc00","g3":"Sc01 Vc10 qc00 Vc11","g4":"qc01 qc10 qc11","l2":"Va10 qa10"},"qlag":2,"weave":"SSS","bfirst":0,"look":4,"hlag":1,"flag":1}
 
 
 def tile_list_octant_voxel_fusion_kernel(tc, xT, wgt, offs, wa, ba, wb_words, wb_scales, wc, wo_words, wo_scales, bo, out):
     nc = tc.nc
+    HEAD, QS, HOLD, UNITS = CFG["head"], CFG["qs"], CFG["hold"], CFG["units"]
+    BUFS = {"gate": CFG["gatebufs"], "xb": 4}
     with ExitStack() as ctx:
         keep = ctx.enter_context(tc.tile_pool(name="keep", bufs=1))
-        work = ctx.enter_context(tc.tile_pool(name="work", bufs=2))
         psum = ctx.enter_context(tc.psum_pool(name="psum", bufs=1))
+
+        def sb(shape, dtype, name, tag=None, bufs=None):
+            tag = HOLD.get(name, tag or name)
+            return keep.tile(shape, dtype, name=name, tag=tag, bufs=bufs or BUFS.get(tag, 1), align_bytes=64)
 
         offsets = keep.tile([P, S // 16], U16, name="offsets")
         nc.sync.dma_start(offsets[:], offs)
 
-        warm = keep.tile([P, 8], F32, name="warm")
+        warm = sb([P, 8], F32, "warm")
         nc.vector.memset(warm[:, 0:1], 0.0)
         nc.scalar.activation(warm[:, 4:5], warm[:, 0:1], ACT.Sigmoid)
 
-        wb_raw = keep.tile([P, PASSES, 2 * H], U8, name="wb_raw", align_bytes=64)
-        wbs_raw = keep.tile([P, PASSES, H], U8, name="wbs_raw", align_bytes=64)
-        wos = keep.tile([P, N], U8, name="wos", align_bytes=64)
+        wb_raw = sb([P, PASSES, 2 * H], U8, "wb_raw")
+        wbs_raw = sb([P, PASSES, H], U8, "wbs_raw")
+        wos = sb([P, N], U8, "wos")
         nc.vector.memset(wbs_raw[:].rearrange("p a e -> p (a e)").bitcast(I32), 0)
         nc.vector.memset(wos[:].bitcast(I32), 0)
-        nc.sync.dma_start(wb_raw[:].bitcast(I32), wb_words.rearrange("a p e -> p a e").bitcast(I32))
-        for q in range(4):
-            nc.sync.dma_start(wbs_raw[32 * q : 32 * q + 4, :, :].bitcast(I32),
-                              wb_scales[:, 4 * q : 4 * q + 4, :].rearrange("a r e -> r a e").bitcast(I32))
-
         x_rows = xT.rearrange("(a p i) t -> a i p t", a=PASSES, i=PACK)
-        planes = {}
-        wg = []
+        planes, w_raw = {}, {}
+        wg = sb([P, S], F32, "wg")
+        ba_t = sb([P, PACK], F32, "ba_t")
+        bo_t = sb([P, N // P], F32, "bo_t")
+        wo_c = sb([P, 4 * N], U8, "wo_c")
+        for item in CFG["order"].split():
+            if item[0] == "x":
+                a, i = int(item[1]), int(item[2])
+                planes[a, i] = sb([P, T], F32, item)
+                nc.sync.dma_start(planes[a, i][:], x_rows[a, i])
+            elif item == "wgh":
+                nc.sync.dma_start(wg[:, :HEAD], wgt[:, :HEAD])
+            elif item == "wgr":
+                nc.sync.dma_start(wg[:, HEAD:], wgt[:, HEAD:])
+            elif item == "wb":
+                nc.sync.dma_start(wb_raw[:].bitcast(I32), wb_words.rearrange("a p e -> p a e").bitcast(I32))
+            elif item == "wbs":
+                for q in range(4):
+                    nc.sync.dma_start(wbs_raw[32 * q : 32 * q + 4, :, :].bitcast(I32),
+                                      wb_scales[:, 4 * q : 4 * q + 4, :].rearrange("a r e -> r a e").bitcast(I32))
+            elif item == "ba":
+                nc.sync.dma_start(ba_t[:], ba.rearrange("(p t) -> p t", t=PACK))
+            elif item == "wo":
+                nc.sync.dma_start(wo_c[:].bitcast(I32), wo_words[0].rearrange("p e i -> p (e i)").bitcast(I32))
+                for q in range(4):
+                    nc.sync.dma_start(wos[32 * q : 32 * q + 4, :].bitcast(I32), wo_scales[0, 4 * q : 4 * q + 4, :].bitcast(I32))
+                with nc.allow_non_contiguous_dma(reason="one bias value a partition"):
+                    nc.sync.dma_start(bo_t[:], bo.rearrange("(u p) -> p u", p=P))
+            else:
+                name, a = item[1], int(item[2])
+                w_raw[name, a] = sb([P, PACK, H], F32, f"raw_{name}{a}")
+                nc.sync.dma_start(w_raw[name, a][:], {"a": wa, "c": wc}[name][a * KP : (a + 1) * KP, :].rearrange("(p j) c -> p j c", j=PACK))
 
-        def load_plane(a, i):
-            planes[a, i] = keep.tile([P, T], F32, name=f"x{a}{i}")
-            nc.sync.dma_start(planes[a, i][:], x_rows[a, i])
-
-        w_raw = {}
-
-        def load_w(name, w, a):
-            w_raw[name, a] = keep.tile([P, PACK, H], F32, name=f"raw_{name}{a}")
-            nc.sync.dma_start(w_raw[name, a][:], w[a * KP : (a + 1) * KP, :].rearrange("(p j) c -> p j c", j=PACK))
-
-        load_plane(0, 0)
-        for c in range(CHUNKS):
-            wg.append(keep.tile([P, CH], F32, name=f"wg{c}", tag=f"wg{c}", align_bytes=64))
-            nc.sync.dma_start(wg[c][:], wgt[:, c * CH : (c + 1) * CH])
-        load_plane(0, 1)
-        load_plane(0, 2)
-        load_plane(0, 3)
-        load_plane(1, 0)
-        load_plane(1, 1)
-        load_w("a", wa, 0)
-        load_w("a", wa, 1)
-        ba_t = keep.tile([P, PACK], F32, name="ba_t")
-        nc.sync.dma_start(ba_t[:], ba.rearrange("(p t) -> p t", t=PACK))
-        load_plane(1, 2)
-        load_plane(1, 3)
-        load_w("c", wc, 0)
-        load_w("c", wc, 1)
-        wo_c = keep.tile([P, 4 * N], U8, name="wo_c", align_bytes=64)
-        nc.sync.dma_start(wo_c[:].bitcast(I32), wo_words[0].rearrange("p e i -> p (e i)").bitcast(I32))
-        for q in range(4):
-            nc.sync.dma_start(wos[32 * q : 32 * q + 4, :].bitcast(I32), wo_scales[0, 4 * q : 4 * q + 4, :].bitcast(I32))
-        bo_t = keep.tile([P, N // P], F32, name="bo_t")
-        with nc.allow_non_contiguous_dma(reason="one bias value a partition"):
-            nc.sync.dma_start(bo_t[:], bo.rearrange("(u p) -> p u", p=P))
-
-        wb_c = keep.tile([P, PASSES, 2 * H], U8, name="wb_c", align_bytes=64)
-        wb_s = keep.tile([P, PASSES, H], U8, name="wb_s", align_bytes=64)
+        wb_c = sb([P, PASSES, 2 * H], U8, "wb_c")
+        wb_s = sb([P, PASSES, H], U8, "wb_s")
         nc.vector.tensor_copy(wb_c[:].bitcast(U16).rearrange("p a (t m) -> p a t m", t=PACK),
                               wb_raw[:].bitcast(U16).rearrange("p a (m t) -> p a t m", t=PACK))
         nc.vector.tensor_copy(wb_s[:].rearrange("p a (t m) -> p a t m", t=PACK),
                               wbs_raw[:].rearrange("p a (m t) -> p a t m", t=PACK))
 
-        xq, xs = {}, {}
+        def pool_cast(dst, src):
+            nc.gpsimd.tensor_scalar(dst, src, 1.0, 0.0, ALU.mult, ALU.add)
 
-        g = {}
-        for a in range(PASSES):
-            for c in range(CHUNKS):
-                g[a, c] = keep.tile([P, PACK, CH], F32, name=f"g{a}{c}")
-                xq[a, c] = keep.tile([P, CH], U32, name=f"xq{a}{c}", align_bytes=64)
-                xs[a, c] = keep.tile([P, CH], U8, name=f"xs{a}{c}", align_bytes=64)
+        COPY = {"S": nc.scalar.copy, "V": nc.vector.tensor_copy, "G": pool_cast}
+        starts = [sum(QS[:n]) for n in range(len(QS))]
+        g0 = sb([P, PACK, S], F32, "g0")
+        g1 = [sb([P, PACK, w], F32, f"g1{n}") for n, w in enumerate(QS)]
+        xq, xs, wq, ws, w16, woven = {}, {}, {}, {}, {}, {}
 
-        def gather(a, i, j0, w):
-            c, l = divmod(j0, CH)
-            nc.vector.tensor_tensor(g[a, c][:, i, l : l + w], planes[a, i][:].indirect(offsets[:, j0 // 16 : (j0 + w) // 16]),
-                                    wg[c][:, l : l + w], ALU.mult)
+        def gather(dst, a, i, j0, w):
+            nc.vector.tensor_tensor(dst, planes[a, i][:].indirect(offsets[:, j0 // 16 : (j0 + w) // 16]), wg[:, j0 : j0 + w], ALU.mult)
 
-        def weave_x(a, j0, w, copy):
-            c, l = divmod(j0, CH)
-            xb = work.tile([P, w, PACK], BF16, name="xb", tag="xb", bufs=3, align_bytes=64)
-            copy(xb[:].rearrange("p (c i) t -> p c t i", i=4), g[a, c][:, :, l : l + w].rearrange("p t (c i) -> p c t i", i=4))
+        def weave_x(src, w, eng):
+            xb = sb([P, w, PACK], BF16, "xb")
+            COPY[eng](xb[:].rearrange("p (c i) t -> p c t i", i=4), src.rearrange("p t (c i) -> p c t i", i=4))
             return xb
 
         def quant_x(a, j0, w, xb):
             c, l = divmod(j0, CH)
+            if l == 0:
+                xq[a, c] = sb([P, CH], U32, f"xq{a}{c}")
+                xs[a, c] = sb([P, CH], U8, f"xs{a}{c}")
             nc.vector.quantize_mx(xq[a, c][:, l : l + w].bitcast(FP8X4), xs[a, c][:, l : l + w], xb[:].rearrange("p c t -> p (c t)"))
 
-        wq, ws, w16 = {}, {}, {}
+        def cast_w(name, a, h, eng):
+            w16[name, a, h] = sb([P, 2, P, PACK], BF16, f"w16{name}{a}{h}")
+            COPY[eng](w16[name, a, h][:].rearrange("p t m j -> p m j t"),
+                      w_raw[name, a][:].rearrange("p j (m t) -> p m j t", t=PACK)[:, :, :, 2 * h : 2 * h + 2])
 
-        def pool_cast(dst, src):
-            nc.gpsimd.tensor_scalar(dst, src, 1.0, 0.0, ALU.mult, ALU.add)
+        def quant_w(name, a, h):
+            wq[name, a, h] = sb([P, 2 * P], U32, f"wq{name}{a}{h}")
+            ws[name, a, h] = sb([P, 2 * P], U8, f"ws{name}{a}{h}")
+            nc.vector.quantize_mx(wq[name, a, h][:].bitcast(FP8X4), ws[name, a, h][:], w16[name, a, h][:].rearrange("p t m j -> p (t m j)"))
 
-        def cast_w(name, a, copy, part, parts):
-            if part == 0:
-                w16[name, a] = keep.tile([P, PACK, P, PACK], BF16, name=f"w16{name}{a}", align_bytes=64)
-            m = slice(part * P // parts, (part + 1) * P // parts)
-            copy(w16[name, a][:].rearrange("p t m j -> p m j t")[:, m], w_raw[name, a][:].rearrange("p j (m t) -> p m j t", t=PACK)[:, m])
+        def w_op(name, a, t):
+            m = slice(t % 2 * P, (t % 2 + 1) * P)
+            return dict(lhsT=wq[name, a, t // 2][:, m].bitcast(FP8X4), lhsT_scale=ws[name, a, t // 2][:, m])
 
-        def quant_w(name, a, tag):
-            wq[name, a] = keep.tile([P, H], U32, name=f"wq{name}{a}", tag=tag, align_bytes=64)
-            ws[name, a] = keep.tile([P, H], U8, name=f"ws{name}{a}", align_bytes=64)
-            nc.vector.quantize_mx(wq[name, a][:].bitcast(FP8X4), ws[name, a][:], w16[name, a][:].rearrange("p t m j -> p (t m j)"))
+        def extra(where):
+            for step in CFG["at"].get(where, "").split():
+                if step[0] == "q":
+                    quant_w(step[1], int(step[2]), int(step[3]))
+                else:
+                    cast_w(step[1], int(step[2]), int(step[3]), step[0])
 
-        for i in range(PACK):
-            for c in range(CHUNKS):
-                gather(0, i, c * CH, CH)
-        woven = [weave_x(0, c * CH, CH, nc.scalar.copy) for c in range(CHUNKS)]
-        for c in range(CHUNKS):
-            gather(1, 0, c * CH, CH)
-        for c in range(CHUNKS):
-            quant_x(0, c * CH, CH, woven[c])
-        for c in range(CHUNKS):
-            gather(1, 1, c * CH, CH)
-        cast_w("a", 0, nc.scalar.copy, 0, 1)
-        quant_w("a", 0, "wqa0")
-        cast_w("a", 1, nc.scalar.copy, 0, 1)
-        for c in range(CHUNKS):
-            gather(1, 2, c * CH, CH)
-        Q = 256
-        VW = []
-        woven = []
-        for n in range(S // Q):
-            gather(1, PACK - 1, n * Q, Q)
-            woven.append(weave_x(1, n * Q, Q, nc.vector.tensor_copy if n in VW else nc.scalar.copy))
-            if n == 1:
-                quant_w("a", 1, "wg0")
-            if n >= 1:
-                quant_x(1, (n - 1) * Q, Q, woven[n - 1])
-        quant_x(1, S - Q, Q, woven[-1])
+        gather(g0[:, 0, :HEAD], 0, 0, 0, HEAD)
+        gather(g0[:, 0, HEAD:], 0, 0, HEAD, S - HEAD)
+        for i in range(1, PACK):
+            gather(g0[:, i, :], 0, i, 0, S)
+        early = [weave_x(g0[:, :, c * CH : (c + 1) * CH], CH, "S") for c in range(CHUNKS)]
+        for i in range(PACK - 1):
+            for n, w in enumerate(QS):
+                gather(g1[n][:, i, :], 1, i, starts[n], w)
+            if i < CHUNKS:
+                quant_x(0, i * CH, CH, early[i])
+            extra(f"p{i}")
+        QL = CFG["qlag"]
+        for n in range(len(QS) + QL):
+            if n < len(QS):
+                gather(g1[n][:, 3, :], 1, 3, starts[n], QS[n])
+                woven[n] = weave_x(g1[n][:], QS[n], CFG["weave"][n])
+            if n >= QL:
+                quant_x(1, starts[n - QL], QS[n - QL], woven[n - QL])
+            extra(f"l{n}")
 
         def bank():
             return psum.tile([P, 512], F32, name="bank", tag="bank", bufs=8)
 
-        def mm_ab(c, t, a, pa, pb):
-            m = slice(t * P, (t + 1) * P)
-            nc.tensor.matmul_mx(pa[:], lhsT=wq["a", a][:, m].bitcast(FP8X4), lhsT_scale=ws["a", a][:, m],
-                                rhs=xq[a, c][:].bitcast(FP8X4), rhs_scale=xs[a, c][:], start=a == 0, stop=a == PASSES - 1)
-            nc.tensor.matmul_mx(pb[:], lhsT=wb_c[:, a, 2 * t * P : 2 * (t + 1) * P].bitcast(FP4X4), lhsT_scale=wb_s[:, a, m],
+        def mm_a(c, t, a, pa):
+            nc.tensor.matmul_mx(pa[:], **w_op("a", a, t), rhs=xq[a, c][:].bitcast(FP8X4), rhs_scale=xs[a, c][:], start=a == 0, stop=a == PASSES - 1)
+
+        def mm_b(c, t, a, pb):
+            nc.tensor.matmul_mx(pb[:], lhsT=wb_c[:, a, 2 * t * P : 2 * (t + 1) * P].bitcast(FP4X4), lhsT_scale=wb_s[:, a, t * P : (t + 1) * P],
                                 rhs=xq[a, c][:].bitcast(FP8X4), rhs_scale=xs[a, c][:], start=a == 0, stop=a == PASSES - 1)
 
-        gbs = [keep.tile([P, PACK, CH], F32, name=f"gb{c}") for c in range(CHUNKS)]
+        gbs = [sb([P, PACK, CH], F32, f"gb{c}") for c in range(CHUNKS)]
 
         def gate_b(c, t, pa, pb):
-            gate = work.tile([P, CH], F32, name="gate", bufs=3)
+            gate = sb([P, CH], F32, "gate")
             nc.scalar.activation(gate[:], pa[:], ACT.Sigmoid, bias=ba_t[:, t : t + 1])
             nc.vector.tensor_tensor(gbs[c][:, t, :], pb[:], gate[:], ALU.mult)
 
-        PIECES = 2
-        COPY = {"scalar": nc.scalar.copy, "vector": nc.vector.tensor_copy, "gpsimd": pool_cast}
         first = [(bank(), bank()) for t in range(PACK)]
         for t in range(PACK):
-            mm_ab(0, t, 0, *first[t])
+            mm_a(0, t, 0, first[t][0])
+            mm_b(0, t, 0, first[t][1])
+        for t in range(CFG["bfirst"]):
+            mm_b(0, t, 1, first[t][1])
         for t in range(PACK):
-            mm_ab(0, t, 1, *first[t])
+            mm_a(0, t, 1, first[t][0])
+            if t >= CFG["bfirst"]:
+                mm_b(0, t, 1, first[t][1])
             gate_b(0, t, *first[t])
-            if t % (PACK // PIECES) == PACK // PIECES - 1:
-                cast_w("c", 0, COPY["scalar"], t // (PACK // PIECES), PIECES)
-        quant_w("c", 0, "wqc0")
-        for part in range(PIECES):
-            cast_w("c", 1, COPY["vector"], part, PIECES)
+            extra(f"g{t}")
         for t in range(PACK):
             pa, pb = bank(), bank()
             for a in range(PASSES):
-                mm_ab(1, t, a, pa, pb)
+                mm_a(1, t, a, pa)
+            for a in range(PASSES):
+                mm_b(1, t, a, pb)
             gate_b(1, t, pa, pb)
-            if t == 0:
-                quant_w("c", 1, "wqc1")
+            extra(f"g{4 + t}")
 
         def mm_c(j0):
             c, l = divmod(j0, CH)
             pc = bank()
             for t in range(PACK):
-                m = slice(t * P, (t + 1) * P)
                 for a in range(PASSES):
-                    nc.tensor.matmul_mx(pc[:, m], lhsT=wq["c", a][:, m].bitcast(FP8X4), lhsT_scale=ws["c", a][:, m],
+                    nc.tensor.matmul_mx(pc[:, t * P : (t + 1) * P], **w_op("c", a, t),
                                         rhs=xq[a, c][:, l : l + BLK].bitcast(FP8X4), rhs_scale=xs[a, c][:, l : l + BLK],
                                         start=a == 0, stop=a == PASSES - 1)
             return pc
@@ -218,37 +210,42 @@ def tile_list_octant_voxel_fusion_kernel(tc, xT, wgt, offs, wa, ba, wb_words, wb
                                     gbs[c][:, :, l : l + BLK].rearrange("p t (c i) -> p c t i", i=4), ALU.add)
 
         def quant_h(w, hb):
-            hq = work.tile([P, w], U32, name="hq", tag="hq", bufs=3, align_bytes=64)
-            hs = work.tile([P, w], U8, name="hs", tag="hs", bufs=3, align_bytes=64)
+            hq = sb([P, w], U32, "hq", bufs=3)
+            hs = sb([P, w], U8, "hs", bufs=3)
             nc.vector.quantize_mx(hq[:].bitcast(FP8X4), hs[:], hb[:])
             return hq, hs
 
         def finish(j0, w, hq, hs):
-            po = bank()
-            res = work.tile([P, N // P, w], F32, name="res", tag="res", bufs=5)
+            pos = [bank() for u in range(N // P)] if w > 256 else [bank()]
+            res = sb([P, N // P, w], F32, "res", bufs=CFG["resbufs"])
+            outs = [pos[u][:] if w > 256 else pos[0][:, u * w : (u + 1) * w] for u in range(N // P)]
             for u in range(N // P):
-                nc.tensor.matmul_mx(po[:, u * w : (u + 1) * w], lhsT=wo_c[:, 4 * u * P : 4 * (u + 1) * P].bitcast(FP8X4),
+                nc.tensor.matmul_mx(outs[u], lhsT=wo_c[:, 4 * u * P : 4 * (u + 1) * P].bitcast(FP8X4),
                                     lhsT_scale=wos[:, u * P : (u + 1) * P], rhs=hq[:].bitcast(FP8X4), rhs_scale=hs[:], start=True, stop=True)
             for u in range(N // P):
-                nc.scalar.activation(res[:, u, :], po[:, u * w : (u + 1) * w], ACT.Identity, bias=bo_t[:, u : u + 1])
+                nc.scalar.activation(res[:, u, :], outs[u], ACT.Identity, bias=bo_t[:, u : u + 1])
             nc.sync.dma_start(out.rearrange("(u p) j -> p u j", p=P)[:, :, j0 : j0 + w], res[:])
 
-        UNITS = [256,256,256,128,128]
+        LOOK, HL, FL = CFG["look"], CFG["hlag"], CFG["flag"]
+        nblk = S // BLK
+        ends = {}
         j0 = 0
-        to_quant, to_finish = None, None
         for w in UNITS:
-            hb = work.tile([P, w * PACK], BF16, name="hb", tag="hb", bufs=3, align_bytes=64)
-            for b in range(w // BLK):
-                pc = mm_c(j0 + b * BLK)
-                if to_finish:
-                    finish(*to_finish)
-                    to_finish = None
-                add_c(j0 + b * BLK, pc, hb[:, b * BLK * PACK : (b + 1) * BLK * PACK])
-                if to_quant:
-                    to_finish = to_quant[:2] + quant_h(to_quant[1], to_quant[2])
-                    to_quant = None
-            to_quant = (j0, w, hb)
+            ends[(j0 + w) // BLK - 1] = (j0, w)
             j0 = j0 + w
-        if to_finish:
-            finish(*to_finish)
-        finish(*(to_quant[:2] + quant_h(to_quant[1], to_quant[2])))
+        unit_of = {b: u for u in ends.values() for b in range(u[0] // BLK, (u[0] + u[1]) // BLK)}
+        pcs = {b: mm_c(b * BLK) for b in range(LOOK)}
+        hbs, hqs = {}, {}
+        for b in range(nblk + HL + FL):
+            if b < nblk:
+                u = unit_of[b]
+                if u not in hbs:
+                    hbs[u] = sb([P, u[1] * PACK], BF16, "hb", bufs=3)
+                l = (b * BLK - u[0]) * PACK
+                add_c(b * BLK, pcs[b], hbs[u][:, l : l + BLK * PACK])
+            if b - HL in ends:
+                hqs[b - HL] = quant_h(ends[b - HL][1], hbs[ends[b - HL]])
+            if b + LOOK < nblk:
+                pcs[b + LOOK] = mm_c((b + LOOK) * BLK)
+            if b - HL - FL in ends:
+                finish(*ends[b - HL - FL], *hqs[b - HL - FL])

@@ -23,7 +23,7 @@ PASSES = K // KP
 CH = 512
 CHUNKS = S // CH
 BLK = 128
-CFG = {"head":256,"qs":[256,256,512],"hold":{},"units":[256,256,256,128,128],"gatebufs":3,"resbufs":5,"order":"wb wbs x00 wgh wgr x01 x02 x03 x10 x11 x12 wa0 ba x13 wa1 wc0 wc1 wo","at":{"p2":"Sa00 Sa01 qa00 qa01","l3":"Va11 qa11","l4":"","g1":"Sc00","g3":"Sc01 Vc10 qc00 Vc11","g4":"qc01 qc10 qc11","l2":"Va10 qa10"},"qlag":2,"weave":"SSS","bfirst":0,"look":4,"hlag":1,"flag":1}
+CFG = {"head":256,"qs":[256,256,512],"hold":{},"units":[256,256,256,128,128],"gatebufs":3,"resbufs":5,"order":"wbs wb offs wgh x00 wgr x01 x02 x03 x10 x11 x12 wa0 ba x13 wa1 wc0 wc1 wo","script":"g00 g01 g02 x00 g10 g11 g12 x01 g20 g21 g22 Sa00 Sa01 qa00 qa01 g30 wS0 g31 wS1 g32 wS2 x10 Va10 qa10 x11 Va11 qa11 x12 F m00 e00 m01 e01 Sc00 m02 e02 m03 e03 Sc01 Vc10 qc00 Vc11 m10 e10 qc01 qc10 qc11 m11 e11 m12 e12 m13 e13","look":4,"hlag":1,"flag":1,"wi":2,"ai":2}
 
 
 def tile_list_octant_voxel_fusion_kernel(tc, xT, wgt, offs, wa, ba, wb_words, wb_scales, wc, wo_words, wo_scales, bo, out):
@@ -39,7 +39,6 @@ def tile_list_octant_voxel_fusion_kernel(tc, xT, wgt, offs, wa, ba, wb_words, wb
             return keep.tile(shape, dtype, name=name, tag=tag, bufs=bufs or BUFS.get(tag, 1), align_bytes=64)
 
         offsets = keep.tile([P, S // 16], U16, name="offsets")
-        nc.sync.dma_start(offsets[:], offs)
 
         warm = sb([P, 8], F32, "warm")
         nc.vector.memset(warm[:, 0:1], 0.0)
@@ -48,8 +47,8 @@ def tile_list_octant_voxel_fusion_kernel(tc, xT, wgt, offs, wa, ba, wb_words, wb
         wb_raw = sb([P, PASSES, 2 * H], U8, "wb_raw")
         wbs_raw = sb([P, PASSES, H], U8, "wbs_raw")
         wos = sb([P, N], U8, "wos")
-        nc.vector.memset(wbs_raw[:].rearrange("p a e -> p (a e)").bitcast(I32), 0)
-        nc.vector.memset(wos[:].bitcast(I32), 0)
+        nc.gpsimd.memset(wbs_raw[:].rearrange("p a e -> p (a e)").bitcast(I32), 0)
+        nc.gpsimd.memset(wos[:].bitcast(I32), 0)
         x_rows = xT.rearrange("(a p i) t -> a i p t", a=PASSES, i=PACK)
         planes, w_raw = {}, {}
         wg = sb([P, S], F32, "wg")
@@ -61,6 +60,8 @@ def tile_list_octant_voxel_fusion_kernel(tc, xT, wgt, offs, wa, ba, wb_words, wb
                 a, i = int(item[1]), int(item[2])
                 planes[a, i] = sb([P, T], F32, item)
                 nc.sync.dma_start(planes[a, i][:], x_rows[a, i])
+            elif item == "offs":
+                nc.sync.dma_start(offsets[:], offs)
             elif item == "wgh":
                 nc.sync.dma_start(wg[:, :HEAD], wgt[:, :HEAD])
             elif item == "wgr":
@@ -105,7 +106,7 @@ def tile_list_octant_voxel_fusion_kernel(tc, xT, wgt, offs, wa, ba, wb_words, wb
 
         def weave_x(src, w, eng):
             xb = sb([P, w, PACK], BF16, "xb")
-            COPY[eng](xb[:].rearrange("p (c i) t -> p c t i", i=4), src.rearrange("p t (c i) -> p c t i", i=4))
+            COPY[eng](xb[:].rearrange("p (c i) t -> p c t i", i=CFG["wi"]), src.rearrange("p t (c i) -> p c t i", i=CFG["wi"]))
             return xb
 
         def quant_x(a, j0, w, xb):
@@ -123,7 +124,7 @@ def tile_list_octant_voxel_fusion_kernel(tc, xT, wgt, offs, wa, ba, wb_words, wb
         def quant_w(name, a, h):
             wq[name, a, h] = sb([P, 2 * P], U32, f"wq{name}{a}{h}")
             ws[name, a, h] = sb([P, 2 * P], U8, f"ws{name}{a}{h}")
-            nc.vector.quantize_mx(wq[name, a, h][:].bitcast(FP8X4), ws[name, a, h][:], w16[name, a, h][:].rearrange("p t m j -> p (t m j)"))
+            nc.vector.quantize_mx(wq[name, a, h][:].bitcast(FP8X4), ws[name, a, h][:], w16[name, a, h][:, :, :, :].rearrange("p t m j -> p (t m j)"))
 
         def w_op(name, a, t):
             m = slice(t % 2 * P, (t % 2 + 1) * P)
@@ -141,20 +142,6 @@ def tile_list_octant_voxel_fusion_kernel(tc, xT, wgt, offs, wa, ba, wb_words, wb
         for i in range(1, PACK):
             gather(g0[:, i, :], 0, i, 0, S)
         early = [weave_x(g0[:, :, c * CH : (c + 1) * CH], CH, "S") for c in range(CHUNKS)]
-        for i in range(PACK - 1):
-            for n, w in enumerate(QS):
-                gather(g1[n][:, i, :], 1, i, starts[n], w)
-            if i < CHUNKS:
-                quant_x(0, i * CH, CH, early[i])
-            extra(f"p{i}")
-        QL = CFG["qlag"]
-        for n in range(len(QS) + QL):
-            if n < len(QS):
-                gather(g1[n][:, 3, :], 1, 3, starts[n], QS[n])
-                woven[n] = weave_x(g1[n][:], QS[n], CFG["weave"][n])
-            if n >= QL:
-                quant_x(1, starts[n - QL], QS[n - QL], woven[n - QL])
-            extra(f"l{n}")
 
         def bank():
             return psum.tile([P, 512], F32, name="bank", tag="bank", bufs=8)
@@ -173,26 +160,86 @@ def tile_list_octant_voxel_fusion_kernel(tc, xT, wgt, offs, wa, ba, wb_words, wb
             nc.scalar.activation(gate[:], pa[:], ACT.Sigmoid, bias=ba_t[:, t : t + 1])
             nc.vector.tensor_tensor(gbs[c][:, t, :], pb[:], gate[:], ALU.mult)
 
-        first = [(bank(), bank()) for t in range(PACK)]
-        for t in range(PACK):
-            mm_a(0, t, 0, first[t][0])
-            mm_b(0, t, 0, first[t][1])
-        for t in range(CFG["bfirst"]):
-            mm_b(0, t, 1, first[t][1])
-        for t in range(PACK):
-            mm_a(0, t, 1, first[t][0])
-            if t >= CFG["bfirst"]:
-                mm_b(0, t, 1, first[t][1])
-            gate_b(0, t, *first[t])
-            extra(f"g{t}")
-        for t in range(PACK):
-            pa, pb = bank(), bank()
-            for a in range(PASSES):
-                mm_a(1, t, a, pa)
-            for a in range(PASSES):
-                mm_b(1, t, a, pb)
-            gate_b(1, t, pa, pb)
-            extra(f"g{4 + t}")
+        banks = {}
+
+        def unit_banks(c, t):
+            if (c, t) not in banks:
+                banks[c, t] = (bank(), bank())
+            return banks[c, t]
+
+        def step(w):
+            k = w[0]
+            if k == "g":
+                i, n = int(w[1]), int(w[2])
+                gather(g1[n][:, i, :], 1, i, starts[n], QS[n])
+            elif k == "w":
+                n = int(w[2])
+                woven[n] = weave_x(g1[n][:], QS[n], w[1])
+            elif k == "x":
+                n = int(w[2])
+                if w[1] == "0":
+                    quant_x(0, n * CH, CH, early[n])
+                else:
+                    quant_x(1, starts[n], QS[n], woven[n])
+            elif k == "P":
+                name, a, h = w[1], int(w[2]), int(w[3])
+                if h == 0:
+                    full[name, a] = sb([P, PACK, P, PACK], BF16, f"w16{name}{a}")
+                    for u in range(2):
+                        w16[name, a, u] = full[name, a][:, 2 * u : 2 * u + 2, :, :]
+                ms = slice(h * P // 2, (h + 1) * P // 2)
+                pool_cast(full[name, a][:].rearrange("p t m j -> p m t j")[:, ms, :, :],
+                          w_raw[name, a][:].rearrange("p j (m t) -> p m t j", t=PACK)[:, ms, :, :])
+            elif k == "q":
+                quant_w(w[1], int(w[2]), int(w[3]))
+            elif k == "B":
+                fb = [bank() for t in range(PACK)]
+                fa = [bank() for t in range(PACK)]
+                for t in range(PACK):
+                    banks[0, t] = (fa[t], fb[t])
+                    mm_b(0, t, 0, fb[t])
+            elif k == "F":
+                for t in range(PACK):
+                    pa, pb = unit_banks(0, t)
+                    mm_a(0, t, 0, pa)
+                    mm_b(0, t, 0, pb)
+            elif k == "A":
+                for t in range(PACK):
+                    mm_a(0, t, 0, banks[0, t][0])
+            elif k == "m":
+                c, t = int(w[1]), int(w[2])
+                pa, pb = unit_banks(c, t)
+                for a in range(1 - c, PASSES):
+                    mm_a(c, t, a, pa)
+                for a in range(1 - c, PASSES):
+                    mm_b(c, t, a, pb)
+            elif k == "e":
+                c, t = int(w[1]), int(w[2])
+                gate_b(c, t, *banks[c, t])
+            elif k == "k":
+                clocks.append(w)
+                if w[1] == "s":
+                    nc.gpsimd.tensor_copy(clk[:, 8 * len(clocks) : 8 * len(clocks) + 1], w16[w[2], int(w[3]), int(w[4])][:, 0, 0, 0:1])
+                    return
+                if w[1] == "q":
+                    nc.gpsimd.tensor_copy(clk[:, 8 * len(clocks) : 8 * len(clocks) + 1].bitcast(U32), wq[w[2], int(w[3]), int(w[4])][:, 0:1])
+                    return
+                if w[1] == "x":
+                    n = int(w[2])
+                    c, l = divmod(starts[n], CH)
+                    nc.gpsimd.tensor_copy(clk[:, 8 * len(clocks) : 8 * len(clocks) + 1].bitcast(U32), xq[1, c][:, l : l + 1])
+                    return
+                src = {"g": lambda: g1[int(w[3])][:, int(w[2]), 0:1], "e": lambda: gbs[int(w[2])][:, int(w[3]), 0:1],
+                       "w": lambda: woven[int(w[2])][:, 0, 0:1], "z": lambda: g0[:, int(w[2]), S - 1 : S]}[w[1]]()
+                nc.gpsimd.tensor_copy(clk[:, 8 * len(clocks) : 8 * len(clocks) + 1], src)
+            else:
+                cast_w(w[1], int(w[2]), int(w[3]), w[0])
+
+        full = {}
+        clocks = []
+        clk = sb([P, 32], F32, "clk")
+        for w in CFG["script"].split():
+            step(w)
 
         def mm_c(j0):
             c, l = divmod(j0, CH)
@@ -206,8 +253,8 @@ def tile_list_octant_voxel_fusion_kernel(tc, xT, wgt, offs, wa, ba, wb_words, wb
 
         def add_c(j0, pc, dst):
             c, l = divmod(j0, CH)
-            nc.vector.tensor_tensor(dst.rearrange("p (c i t) -> p c t i", i=4, t=PACK), pc[:].rearrange("p (t c i) -> p c t i", i=4, t=PACK),
-                                    gbs[c][:, :, l : l + BLK].rearrange("p t (c i) -> p c t i", i=4), ALU.add)
+            nc.vector.tensor_tensor(dst.rearrange("p (c i t) -> p c t i", i=CFG["ai"], t=PACK), pc[:].rearrange("p (t c i) -> p c t i", i=CFG["ai"], t=PACK),
+                                    gbs[c][:, :, l : l + BLK].rearrange("p t (c i) -> p c t i", i=CFG["ai"]), ALU.add)
 
         def quant_h(w, hb):
             hq = sb([P, w], U32, "hq", bufs=3)

@@ -1,6 +1,7 @@
 from contextlib import ExitStack
 
 import concourse.mybir as mybir
+from concourse.masks import make_identity
 
 K, T, S, H, N = 1024, 2048, 1024, 512, 256
 FLOPS = 2 * S * (3 * K * H + H * N)
@@ -18,281 +19,264 @@ ACT = mybir.ActivationFunctionType
 
 P = 128
 PACK = 4
-KP = P * PACK
-PASSES = K // KP
-CH = 512
-CHUNKS = S // CH
-BLK = 128
-CFG = {"head":256,"qs":[256,256,512],"hold":{},"units":[256,256,256,128,128],"gatebufs":3,"resbufs":5,"order":"wbs wb offs wgh x00 wgr x01 x02 x03 x10 x11 x12 wa0 ba x13 wa1 wc0 wc1 wo","script":"g00 g01 g02 x00 g10 g11 g12 x01 g20 g21 g22 Sa00 Sa01 qa00 qa01 g30 wS0 g31 wS1 g32 wS2 x10 Va10 qa10 x11 Va11 qa11 x12 F m00 e00 m01 e01 Sc00 m02 e02 m03 e03 Sc01 Vc10 qc00 Vc11 m10 e10 qc01 qc10 qc11 m11 e11 m12 e12 m13 e13","look":4,"hlag":1,"flag":1,"wi":2,"ai":2}
+K_PASS = P * PACK
+PASSES = K // K_PASS
+GROUP = 16
+HALF = 512
+HALVES = S // HALF
+BLOCK = 128
+LINE = 4
+PIECES = (256, 256, 512)
+STORES = (256, 256, 256, 128, 128)
+C_AHEAD = 2
 
 
 def tile_list_octant_voxel_fusion_kernel(tc, xT, wgt, offs, wa, ba, wb_words, wb_scales, wc, wo_words, wo_scales, bo, out):
     nc = tc.nc
-    HEAD, QS, HOLD, UNITS = CFG["head"], CFG["qs"], CFG["hold"], CFG["units"]
-    BUFS = {"gate": CFG["gatebufs"], "xb": 4}
     with ExitStack() as ctx:
         keep = ctx.enter_context(tc.tile_pool(name="keep", bufs=1))
         psum = ctx.enter_context(tc.psum_pool(name="psum", bufs=1))
 
-        def sb(shape, dtype, name, tag=None, bufs=None):
-            tag = HOLD.get(name, tag or name)
-            return keep.tile(shape, dtype, name=name, tag=tag, bufs=bufs or BUFS.get(tag, 1), align_bytes=64)
+        def sb(shape, dtype, name, tag=None, bufs=1):
+            return keep.tile(shape, dtype, name=name, tag=tag or name, bufs=bufs, align_bytes=64)
 
-        offsets = keep.tile([P, S // 16], U16, name="offsets")
+        def bank():
+            return psum.tile([P, HALF], F32, name="bank", tag="bank", bufs=8)
+
+        offsets = keep.tile([P, S // GROUP], U16, name="offsets")
 
         warm = sb([P, 8], F32, "warm")
         nc.vector.memset(warm[:, 0:1], 0.0)
         nc.scalar.activation(warm[:, 4:5], warm[:, 0:1], ACT.Sigmoid)
 
-        wb_raw = sb([P, PASSES, 2 * H], U8, "wb_raw")
-        wbs_raw = sb([P, PASSES, H], U8, "wbs_raw")
-        wos = sb([P, N], U8, "wos")
-        nc.gpsimd.memset(wbs_raw[:].rearrange("p a e -> p (a e)").bitcast(I32), 0)
-        nc.gpsimd.memset(wos[:].bitcast(I32), 0)
-        x_rows = xT.rearrange("(a p i) t -> a i p t", a=PASSES, i=PACK)
+        wb_words_raw = sb([P, PASSES, 2 * H], U8, "wb_words_raw")
+        wb_scales_raw = sb([P, PASSES, H], U8, "wb_scales_raw")
+        wo_scale = sb([P, N], U8, "wo_scale")
+        nc.vector.memset(wb_scales_raw[:].rearrange("p s e -> p (s e)").bitcast(I32), 0)
+        nc.vector.memset(wo_scale[:].bitcast(I32), 0)
+        weight = sb([P, S], F32, "weight")
+        ba_sb = sb([P, PACK], F32, "ba_sb")
+        bo_sb = sb([P, N // P], F32, "bo_sb")
+        wo_code = sb([P, PACK * N], U8, "wo_code")
+        ident = sb([P, P], F32, "ident")
+        make_identity(nc, ident[:])
+        two_rows = sb([P, P], F32, "two_rows")
+
+        x_rows = xT.rearrange("(s p i) t -> s i p t", s=PASSES, i=PACK)
         planes, w_raw = {}, {}
-        wg = sb([P, S], F32, "wg")
-        ba_t = sb([P, PACK], F32, "ba_t")
-        bo_t = sb([P, N // P], F32, "bo_t")
-        wo_c = sb([P, 4 * N], U8, "wo_c")
-        for item in CFG["order"].split():
-            if item[0] == "x":
-                a, i = int(item[1]), int(item[2])
-                planes[a, i] = sb([P, T], F32, item)
-                nc.sync.dma_start(planes[a, i][:], x_rows[a, i])
-            elif item == "offs":
-                nc.sync.dma_start(offsets[:], offs)
-            elif item == "wgh":
-                nc.sync.dma_start(wg[:, :HEAD], wgt[:, :HEAD])
-            elif item == "wgr":
-                nc.sync.dma_start(wg[:, HEAD:], wgt[:, HEAD:])
-            elif item == "wb":
-                nc.sync.dma_start(wb_raw[:].bitcast(I32), wb_words.rearrange("a p e -> p a e").bitcast(I32))
-            elif item == "wbs":
-                for q in range(4):
-                    nc.sync.dma_start(wbs_raw[32 * q : 32 * q + 4, :, :].bitcast(I32),
-                                      wb_scales[:, 4 * q : 4 * q + 4, :].rearrange("a r e -> r a e").bitcast(I32))
-            elif item == "ba":
-                nc.sync.dma_start(ba_t[:], ba.rearrange("(p t) -> p t", t=PACK))
-            elif item == "wo":
-                nc.sync.dma_start(wo_c[:].bitcast(I32), wo_words[0].rearrange("p e i -> p (e i)").bitcast(I32))
-                for q in range(4):
-                    nc.sync.dma_start(wos[32 * q : 32 * q + 4, :].bitcast(I32), wo_scales[0, 4 * q : 4 * q + 4, :].bitcast(I32))
-                with nc.allow_non_contiguous_dma(reason="one bias value a partition"):
-                    nc.sync.dma_start(bo_t[:], bo.rearrange("(u p) -> p u", p=P))
-            else:
-                name, a = item[1], int(item[2])
-                w_raw[name, a] = sb([P, PACK, H], F32, f"raw_{name}{a}")
-                nc.sync.dma_start(w_raw[name, a][:], {"a": wa, "c": wc}[name][a * KP : (a + 1) * KP, :].rearrange("(p j) c -> p j c", j=PACK))
 
-        wb_c = sb([P, PASSES, 2 * H], U8, "wb_c")
-        wb_s = sb([P, PASSES, H], U8, "wb_s")
-        nc.vector.tensor_copy(wb_c[:].bitcast(U16).rearrange("p a (t m) -> p a t m", t=PACK),
-                              wb_raw[:].bitcast(U16).rearrange("p a (m t) -> p a t m", t=PACK))
-        nc.vector.tensor_copy(wb_s[:].rearrange("p a (t m) -> p a t m", t=PACK),
-                              wbs_raw[:].rearrange("p a (m t) -> p a t m", t=PACK))
+        def load_plane(s, i):
+            planes[s, i] = sb([P, T], F32, f"plane{s}{i}")
+            nc.sync.dma_start(planes[s, i][:], x_rows[s, i])
 
-        def pool_cast(dst, src):
-            nc.gpsimd.tensor_scalar(dst, src, 1.0, 0.0, ALU.mult, ALU.add)
+        def load_weight(name, w, s):
+            w_raw[name, s] = sb([P, PACK, H], F32, f"raw_{name}{s}")
+            nc.sync.dma_start(w_raw[name, s][:], w[s * K_PASS : (s + 1) * K_PASS, :].rearrange("(p i) c -> p i c", i=PACK))
 
-        COPY = {"S": nc.scalar.copy, "V": nc.vector.tensor_copy, "G": pool_cast}
-        starts = [sum(QS[:n]) for n in range(len(QS))]
-        g0 = sb([P, PACK, S], F32, "g0")
-        g1 = [sb([P, PACK, w], F32, f"g1{n}") for n, w in enumerate(QS)]
-        xq, xs, wq, ws, w16, woven = {}, {}, {}, {}, {}, {}
+        nc.sync.dma_start(two_rows[:], wgt.rearrange("(g r) (c j) -> g (r c) j", r=GROUP, j=P)[:, 0:GROUP, :])
+        nc.sync.dma_start(offsets[:], offs)
+        nc.sync.dma_start(wb_words_raw[:].bitcast(I32), wb_words.rearrange("s p e -> p s e").bitcast(I32))
+        for q in range(4):
+            nc.sync.dma_start(wb_scales_raw[32 * q : 32 * q + 4, :, :].bitcast(I32),
+                              wb_scales[:, 4 * q : 4 * q + 4, :].rearrange("s r e -> r s e").bitcast(I32))
+        for s in range(PASSES):
+            for i in range(PACK):
+                if (s, i) == (PASSES - 1, PACK - 1):
+                    load_weight("a", wa, 0)
+                load_plane(s, i)
+        load_weight("a", wa, 1)
+        nc.sync.dma_start(ba_sb[:], ba.rearrange("(p t) -> p t", t=PACK))
+        for s in range(PASSES):
+            load_weight("c", wc, s)
+        nc.sync.dma_start(wo_code[:].bitcast(I32), wo_words[0].rearrange("p e i -> p (e i)").bitcast(I32))
+        for q in range(4):
+            nc.sync.dma_start(wo_scale[32 * q : 32 * q + 4, :].bitcast(I32), wo_scales[0, 4 * q : 4 * q + 4, :].bitcast(I32))
+        with nc.allow_non_contiguous_dma(reason="one bias value a partition"):
+            nc.sync.dma_start(bo_sb[:], bo.rearrange("(u p) -> p u", p=P))
 
-        def gather(dst, a, i, j0, w):
-            nc.vector.tensor_tensor(dst, planes[a, i][:].indirect(offsets[:, j0 // 16 : (j0 + w) // 16]), wg[:, j0 : j0 + w], ALU.mult)
+        starts = [sum(PIECES[:n]) for n in range(len(PIECES))]
 
-        def weave_x(src, w, eng):
-            xb = sb([P, w, PACK], BF16, "xb")
-            COPY[eng](xb[:].rearrange("p (c i) t -> p c t i", i=CFG["wi"]), src.rearrange("p t (c i) -> p c t i", i=CFG["wi"]))
-            return xb
+        def scratch(shape, name):
+            return sb(shape, F32, name, tag="scratch", bufs=3)
 
-        def quant_x(a, j0, w, xb):
-            c, l = divmod(j0, CH)
-            if l == 0:
-                xq[a, c] = sb([P, CH], U32, f"xq{a}{c}")
-                xs[a, c] = sb([P, CH], U8, f"xs{a}{c}")
-            nc.vector.quantize_mx(xq[a, c][:, l : l + w].bitcast(FP8X4), xs[a, c][:, l : l + w], xb[:].rearrange("p c t -> p (c t)"))
+        runs = S // P
+        by_column = bank()
+        nc.tensor.transpose(by_column[:, :P], two_rows[:], ident[:])
+        by_run = by_column[:, :P].rearrange("j (g d c) -> j c g d", d=2, c=runs)
+        for j0, width in zip(starts, PIECES):
+            first, count = j0 // P, width // P
+            repeated = scratch([P, count, P], f"repeated{first}")
+            nc.scalar.copy(repeated[:].rearrange("j c (g d e) -> j c g d e", d=2, e=GROUP // 2),
+                           by_run[:, first : first + count, :, :].unsqueeze(4).to_broadcast([P, count, P // GROUP, 2, GROUP // 2]))
+            back = bank()
+            for c in range(count):
+                nc.tensor.transpose(back[:, c * P : (c + 1) * P], repeated[:, c, :], ident[:])
+            nc.scalar.copy(weight[:, j0 : j0 + width], back[:, :width])
 
-        def cast_w(name, a, h, eng):
-            w16[name, a, h] = sb([P, 2, P, PACK], BF16, f"w16{name}{a}{h}")
-            COPY[eng](w16[name, a, h][:].rearrange("p t m j -> p m j t"),
-                      w_raw[name, a][:].rearrange("p j (m t) -> p m j t", t=PACK)[:, :, :, 2 * h : 2 * h + 2])
+        wb_code = sb([P, PASSES, 2 * H], U8, "wb_code")
+        wb_scale = sb([P, PASSES, H], U8, "wb_scale")
+        nc.vector.tensor_copy(wb_code[:].bitcast(U16).rearrange("p s (t m) -> p s t m", t=PACK),
+                              wb_words_raw[:].bitcast(U16).rearrange("p s (m t) -> p s t m", t=PACK))
+        nc.vector.tensor_copy(wb_scale[:].rearrange("p s (t m) -> p s t m", t=PACK),
+                              wb_scales_raw[:].rearrange("p s (m t) -> p s t m", t=PACK))
 
-        def quant_w(name, a, h):
-            wq[name, a, h] = sb([P, 2 * P], U32, f"wq{name}{a}{h}")
-            ws[name, a, h] = sb([P, 2 * P], U8, f"ws{name}{a}{h}")
-            nc.vector.quantize_mx(wq[name, a, h][:].bitcast(FP8X4), ws[name, a, h][:], w16[name, a, h][:, :, :, :].rearrange("p t m j -> p (t m j)"))
+        picked0 = sb([P, PACK, S], F32, "picked0")
+        picked1 = [sb([P, PACK, width], F32, f"picked1{n}") for n, width in enumerate(PIECES)]
+        x_code, x_scale, w_code, w_scale, w_round = {}, {}, {}, {}, {}
 
-        def w_op(name, a, t):
-            m = slice(t % 2 * P, (t % 2 + 1) * P)
-            return dict(lhsT=wq[name, a, t // 2][:, m].bitcast(FP8X4), lhsT_scale=ws[name, a, t // 2][:, m])
+        def gather(dst, s, i, j0, width):
+            nc.vector.tensor_tensor(dst, planes[s, i][:].indirect(offsets[:, j0 // GROUP : (j0 + width) // GROUP]),
+                                    weight[:, j0 : j0 + width], ALU.mult)
 
-        def extra(where):
-            for step in CFG["at"].get(where, "").split():
-                if step[0] == "q":
-                    quant_w(step[1], int(step[2]), int(step[3]))
-                else:
-                    cast_w(step[1], int(step[2]), int(step[3]), step[0])
+        def round_x(src, width):
+            x_round = sb([P, width, PACK], BF16, "x_round", bufs=4)
+            nc.scalar.copy(x_round[:].rearrange("p (c l) i -> p c i l", l=LINE), src.rearrange("p i (c l) -> p c i l", l=LINE))
+            return x_round
 
-        gather(g0[:, 0, :HEAD], 0, 0, 0, HEAD)
-        gather(g0[:, 0, HEAD:], 0, 0, HEAD, S - HEAD)
+        def quantise_x(s, j0, width, x_round):
+            half, at = divmod(j0, HALF)
+            if at == 0:
+                x_code[s, half] = sb([P, HALF], U32, f"x_code{s}{half}")
+                x_scale[s, half] = sb([P, HALF], U8, f"x_scale{s}{half}")
+            nc.vector.quantize_mx(x_code[s, half][:, at : at + width].bitcast(FP8X4), x_scale[s, half][:, at : at + width],
+                                  x_round[:].rearrange("p c i -> p (c i)"))
+
+        def round_w(copy, name, s, pair):
+            w_round[name, s, pair] = sb([P, 2, P, PACK], BF16, f"w_round{name}{s}{pair}")
+            copy(w_round[name, s, pair][:].rearrange("p t m i -> p m i t"),
+                 w_raw[name, s][:].rearrange("p i (m t) -> p m i t", t=PACK)[:, :, :, 2 * pair : 2 * pair + 2])
+
+        def quantise_w(name, s, pair):
+            w_code[name, s, pair] = sb([P, 2 * P], U32, f"w_code{name}{s}{pair}")
+            w_scale[name, s, pair] = sb([P, 2 * P], U8, f"w_scale{name}{s}{pair}")
+            nc.vector.quantize_mx(w_code[name, s, pair][:].bitcast(FP8X4), w_scale[name, s, pair][:],
+                                  w_round[name, s, pair][:].rearrange("p t m i -> p (t m i)"))
+
+        def row_set(name, s, t):
+            cols = slice(t % 2 * P, (t % 2 + 1) * P)
+            return dict(lhsT=w_code[name, s, t // 2][:, cols].bitcast(FP8X4), lhsT_scale=w_scale[name, s, t // 2][:, cols])
+
+        for j0, width in zip(starts, PIECES):
+            gather(picked0[:, 0, j0 : j0 + width], 0, 0, j0, width)
         for i in range(1, PACK):
-            gather(g0[:, i, :], 0, i, 0, S)
-        early = [weave_x(g0[:, :, c * CH : (c + 1) * CH], CH, "S") for c in range(CHUNKS)]
+            gather(picked0[:, i, :], 0, i, 0, S)
+        rounded0 = [round_x(picked0[:, :, half * HALF : (half + 1) * HALF], HALF) for half in range(HALVES)]
 
-        def bank():
-            return psum.tile([P, 512], F32, name="bank", tag="bank", bufs=8)
+        for i in range(PACK - 1):
+            for n, width in enumerate(PIECES):
+                gather(picked1[n][:, i, :], 1, i, starts[n], width)
+            if i < HALVES:
+                quantise_x(0, i * HALF, HALF, rounded0[i])
+        for pair in range(2):
+            round_w(nc.scalar.copy, "a", 0, pair)
+        for pair in range(2):
+            quantise_w("a", 0, pair)
+        rounded1 = []
+        for n, width in enumerate(PIECES):
+            gather(picked1[n][:, PACK - 1, :], 1, PACK - 1, starts[n], width)
+            rounded1.append(round_x(picked1[n][:], width))
+        for n, width in enumerate(PIECES):
+            quantise_x(1, starts[n], width, rounded1[n])
+            if n < 2:
+                round_w(nc.vector.tensor_copy, "a", 1, n)
+                quantise_w("a", 1, n)
 
-        def mm_a(c, t, a, pa):
-            nc.tensor.matmul_mx(pa[:], **w_op("a", a, t), rhs=xq[a, c][:].bitcast(FP8X4), rhs_scale=xs[a, c][:], start=a == 0, stop=a == PASSES - 1)
+        def product_a(half, t, s, acc):
+            nc.tensor.matmul_mx(acc[:], **row_set("a", s, t), rhs=x_code[s, half][:].bitcast(FP8X4), rhs_scale=x_scale[s, half][:],
+                                start=s == 0, stop=s == PASSES - 1)
 
-        def mm_b(c, t, a, pb):
-            nc.tensor.matmul_mx(pb[:], lhsT=wb_c[:, a, 2 * t * P : 2 * (t + 1) * P].bitcast(FP4X4), lhsT_scale=wb_s[:, a, t * P : (t + 1) * P],
-                                rhs=xq[a, c][:].bitcast(FP8X4), rhs_scale=xs[a, c][:], start=a == 0, stop=a == PASSES - 1)
+        def product_b(half, t, s, acc):
+            nc.tensor.matmul_mx(acc[:], lhsT=wb_code[:, s, 2 * t * P : 2 * (t + 1) * P].bitcast(FP4X4),
+                                lhsT_scale=wb_scale[:, s, t * P : (t + 1) * P],
+                                rhs=x_code[s, half][:].bitcast(FP8X4), rhs_scale=x_scale[s, half][:], start=s == 0, stop=s == PASSES - 1)
 
-        gbs = [sb([P, PACK, CH], F32, f"gb{c}") for c in range(CHUNKS)]
+        gated = [sb([P, PACK, HALF], F32, f"gated{half}") for half in range(HALVES)]
 
-        def gate_b(c, t, pa, pb):
-            gate = sb([P, CH], F32, "gate")
-            nc.scalar.activation(gate[:], pa[:], ACT.Sigmoid, bias=ba_t[:, t : t + 1])
-            nc.vector.tensor_tensor(gbs[c][:, t, :], pb[:], gate[:], ALU.mult)
+        def gate_times_b(half, t, acc_a, acc_b):
+            gate = scratch([P, HALF], "gate")
+            nc.scalar.activation(gate[:], acc_a[:], ACT.Sigmoid, bias=ba_sb[:, t : t + 1])
+            nc.vector.tensor_tensor(gated[half][:, t, :], acc_b[:], gate[:], ALU.mult)
 
-        banks = {}
+        open_banks = []
+        for t in range(PACK):
+            open_banks.append((bank(), bank()))
+            product_a(0, t, 0, open_banks[t][0])
+            product_b(0, t, 0, open_banks[t][1])
+        for t in range(PACK):
+            product_a(0, t, 1, open_banks[t][0])
+            product_b(0, t, 1, open_banks[t][1])
+            gate_times_b(0, t, *open_banks[t])
+            if t % 2:
+                round_w(nc.scalar.copy, "c", 0, t // 2)
+        round_w(nc.vector.tensor_copy, "c", 1, 0)
+        quantise_w("c", 0, 0)
+        round_w(nc.vector.tensor_copy, "c", 1, 1)
 
-        def unit_banks(c, t):
-            if (c, t) not in banks:
-                banks[c, t] = (bank(), bank())
-            return banks[c, t]
+        for t in range(PACK):
+            acc_a, acc_b = bank(), bank()
+            for s in range(PASSES):
+                product_a(1, t, s, acc_a)
+            for s in range(PASSES):
+                product_b(1, t, s, acc_b)
+            gate_times_b(1, t, acc_a, acc_b)
+            if t == 0:
+                quantise_w("c", 0, 1)
+                for pair in range(2):
+                    quantise_w("c", 1, pair)
 
-        def step(w):
-            k = w[0]
-            if k == "g":
-                i, n = int(w[1]), int(w[2])
-                gather(g1[n][:, i, :], 1, i, starts[n], QS[n])
-            elif k == "w":
-                n = int(w[2])
-                woven[n] = weave_x(g1[n][:], QS[n], w[1])
-            elif k == "x":
-                n = int(w[2])
-                if w[1] == "0":
-                    quant_x(0, n * CH, CH, early[n])
-                else:
-                    quant_x(1, starts[n], QS[n], woven[n])
-            elif k == "P":
-                name, a, h = w[1], int(w[2]), int(w[3])
-                if h == 0:
-                    full[name, a] = sb([P, PACK, P, PACK], BF16, f"w16{name}{a}")
-                    for u in range(2):
-                        w16[name, a, u] = full[name, a][:, 2 * u : 2 * u + 2, :, :]
-                ms = slice(h * P // 2, (h + 1) * P // 2)
-                pool_cast(full[name, a][:].rearrange("p t m j -> p m t j")[:, ms, :, :],
-                          w_raw[name, a][:].rearrange("p j (m t) -> p m t j", t=PACK)[:, ms, :, :])
-            elif k == "q":
-                quant_w(w[1], int(w[2]), int(w[3]))
-            elif k == "B":
-                fb = [bank() for t in range(PACK)]
-                fa = [bank() for t in range(PACK)]
-                for t in range(PACK):
-                    banks[0, t] = (fa[t], fb[t])
-                    mm_b(0, t, 0, fb[t])
-            elif k == "F":
-                for t in range(PACK):
-                    pa, pb = unit_banks(0, t)
-                    mm_a(0, t, 0, pa)
-                    mm_b(0, t, 0, pb)
-            elif k == "A":
-                for t in range(PACK):
-                    mm_a(0, t, 0, banks[0, t][0])
-            elif k == "m":
-                c, t = int(w[1]), int(w[2])
-                pa, pb = unit_banks(c, t)
-                for a in range(1 - c, PASSES):
-                    mm_a(c, t, a, pa)
-                for a in range(1 - c, PASSES):
-                    mm_b(c, t, a, pb)
-            elif k == "e":
-                c, t = int(w[1]), int(w[2])
-                gate_b(c, t, *banks[c, t])
-            elif k == "k":
-                clocks.append(w)
-                if w[1] == "s":
-                    nc.gpsimd.tensor_copy(clk[:, 8 * len(clocks) : 8 * len(clocks) + 1], w16[w[2], int(w[3]), int(w[4])][:, 0, 0, 0:1])
-                    return
-                if w[1] == "q":
-                    nc.gpsimd.tensor_copy(clk[:, 8 * len(clocks) : 8 * len(clocks) + 1].bitcast(U32), wq[w[2], int(w[3]), int(w[4])][:, 0:1])
-                    return
-                if w[1] == "x":
-                    n = int(w[2])
-                    c, l = divmod(starts[n], CH)
-                    nc.gpsimd.tensor_copy(clk[:, 8 * len(clocks) : 8 * len(clocks) + 1].bitcast(U32), xq[1, c][:, l : l + 1])
-                    return
-                src = {"g": lambda: g1[int(w[3])][:, int(w[2]), 0:1], "e": lambda: gbs[int(w[2])][:, int(w[3]), 0:1],
-                       "w": lambda: woven[int(w[2])][:, 0, 0:1], "z": lambda: g0[:, int(w[2]), S - 1 : S]}[w[1]]()
-                nc.gpsimd.tensor_copy(clk[:, 8 * len(clocks) : 8 * len(clocks) + 1], src)
-            else:
-                cast_w(w[1], int(w[2]), int(w[3]), w[0])
-
-        full = {}
-        clocks = []
-        clk = sb([P, 32], F32, "clk")
-        for w in CFG["script"].split():
-            step(w)
-
-        def mm_c(j0):
-            c, l = divmod(j0, CH)
-            pc = bank()
+        def product_c(j0):
+            half, at = divmod(j0, HALF)
+            acc = bank()
             for t in range(PACK):
-                for a in range(PASSES):
-                    nc.tensor.matmul_mx(pc[:, t * P : (t + 1) * P], **w_op("c", a, t),
-                                        rhs=xq[a, c][:, l : l + BLK].bitcast(FP8X4), rhs_scale=xs[a, c][:, l : l + BLK],
-                                        start=a == 0, stop=a == PASSES - 1)
-            return pc
+                for s in range(PASSES):
+                    nc.tensor.matmul_mx(acc[:, t * P : (t + 1) * P], **row_set("c", s, t),
+                                        rhs=x_code[s, half][:, at : at + BLOCK].bitcast(FP8X4), rhs_scale=x_scale[s, half][:, at : at + BLOCK],
+                                        start=s == 0, stop=s == PASSES - 1)
+            return acc
 
-        def add_c(j0, pc, dst):
-            c, l = divmod(j0, CH)
-            nc.vector.tensor_tensor(dst.rearrange("p (c i t) -> p c t i", i=CFG["ai"], t=PACK), pc[:].rearrange("p (t c i) -> p c t i", i=CFG["ai"], t=PACK),
-                                    gbs[c][:, :, l : l + BLK].rearrange("p t (c i) -> p c t i", i=CFG["ai"]), ALU.add)
+        def add_c(j0, acc, dst):
+            half, at = divmod(j0, HALF)
+            nc.vector.tensor_tensor(dst.rearrange("p (c l t) -> p c t l", l=LINE, t=PACK), acc[:].rearrange("p (t c l) -> p c t l", l=LINE, t=PACK),
+                                    gated[half][:, :, at : at + BLOCK].rearrange("p t (c l) -> p c t l", l=LINE), ALU.add)
 
-        def quant_h(w, hb):
-            hq = sb([P, w], U32, "hq", bufs=3)
-            hs = sb([P, w], U8, "hs", bufs=3)
-            nc.vector.quantize_mx(hq[:].bitcast(FP8X4), hs[:], hb[:])
-            return hq, hs
+        def quantise_h(width, h_round):
+            h_code = sb([P, width], U32, "h_code", bufs=3)
+            h_scale = sb([P, width], U8, "h_scale", bufs=3)
+            nc.vector.quantize_mx(h_code[:].bitcast(FP8X4), h_scale[:], h_round[:])
+            return h_code, h_scale
 
-        def finish(j0, w, hq, hs):
-            pos = [bank() for u in range(N // P)] if w > 256 else [bank()]
-            res = sb([P, N // P, w], F32, "res", bufs=CFG["resbufs"])
-            outs = [pos[u][:] if w > 256 else pos[0][:, u * w : (u + 1) * w] for u in range(N // P)]
+        def finish(j0, width, h_code, h_scale):
+            acc = bank()
+            result = sb([P, N // P, width], F32, "result", bufs=len(STORES))
             for u in range(N // P):
-                nc.tensor.matmul_mx(outs[u], lhsT=wo_c[:, 4 * u * P : 4 * (u + 1) * P].bitcast(FP8X4),
-                                    lhsT_scale=wos[:, u * P : (u + 1) * P], rhs=hq[:].bitcast(FP8X4), rhs_scale=hs[:], start=True, stop=True)
+                nc.tensor.matmul_mx(acc[:, u * width : (u + 1) * width], lhsT=wo_code[:, PACK * u * P : PACK * (u + 1) * P].bitcast(FP8X4),
+                                    lhsT_scale=wo_scale[:, u * P : (u + 1) * P], rhs=h_code[:].bitcast(FP8X4), rhs_scale=h_scale[:],
+                                    start=True, stop=True)
             for u in range(N // P):
-                nc.scalar.activation(res[:, u, :], outs[u], ACT.Identity, bias=bo_t[:, u : u + 1])
-            nc.sync.dma_start(out.rearrange("(u p) j -> p u j", p=P)[:, :, j0 : j0 + w], res[:])
+                nc.scalar.activation(result[:, u, :], acc[:, u * width : (u + 1) * width], ACT.Identity, bias=bo_sb[:, u : u + 1])
+            nc.sync.dma_start(out.rearrange("(u p) j -> p u j", p=P)[:, :, j0 : j0 + width], result[:])
 
-        LOOK, HL, FL = CFG["look"], CFG["hlag"], CFG["flag"]
-        nblk = S // BLK
-        ends = {}
-        j0 = 0
-        for w in UNITS:
-            ends[(j0 + w) // BLK - 1] = (j0, w)
-            j0 = j0 + w
-        unit_of = {b: u for u in ends.values() for b in range(u[0] // BLK, (u[0] + u[1]) // BLK)}
-        pcs = {b: mm_c(b * BLK) for b in range(LOOK)}
-        hbs, hqs = {}, {}
-        for b in range(nblk + HL + FL):
-            if b < nblk:
-                u = unit_of[b]
-                if u not in hbs:
-                    hbs[u] = sb([P, u[1] * PACK], BF16, "hb", bufs=3)
-                l = (b * BLK - u[0]) * PACK
-                add_c(b * BLK, pcs[b], hbs[u][:, l : l + BLK * PACK])
-            if b - HL in ends:
-                hqs[b - HL] = quant_h(ends[b - HL][1], hbs[ends[b - HL]])
-            if b + LOOK < nblk:
-                pcs[b + LOOK] = mm_c((b + LOOK) * BLK)
-            if b - HL - FL in ends:
-                finish(*ends[b - HL - FL], *hqs[b - HL - FL])
+        blocks = S // BLOCK
+        store_of, completed_by = {}, {}
+        for n, width in enumerate(STORES):
+            j0 = sum(STORES[:n])
+            for b in range(j0 // BLOCK, (j0 + width) // BLOCK):
+                store_of[b] = (j0, width)
+            completed_by[(j0 + width) // BLOCK - 1] = (j0, width)
+        c_banks = {b: product_c(b * BLOCK) for b in range(C_AHEAD)}
+        h_rounds, h_quantised = {}, {}
+        for b in range(blocks + 2):
+            if b < blocks:
+                j0, width = store_of[b]
+                if j0 not in h_rounds:
+                    h_rounds[j0] = sb([P, width * PACK], BF16, "h_round", bufs=3)
+                at = (b * BLOCK - j0) * PACK
+                add_c(b * BLOCK, c_banks[b], h_rounds[j0][:, at : at + BLOCK * PACK])
+            if b - 1 in completed_by:
+                j0, width = completed_by[b - 1]
+                h_quantised[j0] = quantise_h(width, h_rounds[j0])
+            if b + C_AHEAD < blocks:
+                c_banks[b + C_AHEAD] = product_c((b + C_AHEAD) * BLOCK)
+            if b - 2 in completed_by:
+                j0, width = completed_by[b - 2]
+                finish(j0, width, *h_quantised[j0])

@@ -28,7 +28,7 @@ BLOCK = 128
 LINE = 4
 PIECES = (256, 256, 512)
 STORES = (256, 256, 256, 128, 128)
-C_AHEAD = 2
+C_AHEAD = 3
 
 
 def tile_list_octant_voxel_fusion_kernel(tc, xT, wgt, offs, wa, ba, wb_words, wb_scales, wc, wo_words, wo_scales, bo, out):
@@ -120,6 +120,7 @@ def tile_list_octant_voxel_fusion_kernel(tc, xT, wgt, offs, wa, ba, wb_words, wb
         nc.vector.tensor_copy(wb_scale[:].rearrange("p s (t m) -> p s t m", t=PACK),
                               wb_scales_raw[:].rearrange("p s (m t) -> p s t m", t=PACK))
 
+        shared = sb([P, 3072], F32, "shared")
         picked0 = sb([P, PACK, S], F32, "picked0")
         picked1 = [sb([P, PACK, width], F32, f"picked1{n}") for n, width in enumerate(PIECES)]
         x_code, x_scale, w_code, w_scale, w_round = {}, {}, {}, {}, {}
@@ -128,8 +129,11 @@ def tile_list_octant_voxel_fusion_kernel(tc, xT, wgt, offs, wa, ba, wb_words, wb
             nc.vector.tensor_tensor(dst, planes[s, i][:].indirect(offsets[:, j0 // GROUP : (j0 + width) // GROUP]),
                                     weight[:, j0 : j0 + width], ALU.mult)
 
-        def round_x(src, width):
-            x_round = sb([P, width, PACK], BF16, "x_round", bufs=4)
+        def round_x(src, width, last=False):
+            if last:
+                x_round = shared[:, 1536:2560].bitcast(BF16).rearrange("p (c i) -> p c i", i=PACK)
+            else:
+                x_round = sb([P, width, PACK], BF16, "x_round", bufs=4)
             nc.scalar.copy(x_round[:].rearrange("p (c l) i -> p c i l", l=LINE), src.rearrange("p i (c l) -> p c i l", l=LINE))
             return x_round
 
@@ -174,12 +178,17 @@ def tile_list_octant_voxel_fusion_kernel(tc, xT, wgt, offs, wa, ba, wb_words, wb
         rounded1 = []
         for n, width in enumerate(PIECES):
             gather(picked1[n][:, PACK - 1, :], 1, PACK - 1, starts[n], width)
-            rounded1.append(round_x(picked1[n][:], width))
+            rounded1.append(round_x(picked1[n][:], width, n == len(PIECES) - 1))
         for n, width in enumerate(PIECES):
             quantise_x(1, starts[n], width, rounded1[n])
             if n < 2:
                 round_w(nc.vector.tensor_copy, "a", 1, n)
                 quantise_w("a", 1, n)
+            if n == 1:
+                quarter = 2 * P * PACK
+                late = shared[:, 1024:].bitcast(BF16)
+                nc.vector.tensor_copy(late[:, :quarter].rearrange("p (t m i) -> p m i t", t=2, i=PACK),
+                                      w_raw["c", 0][:].rearrange("p i (m t) -> p m i t", t=PACK)[:, :, :, 0:2])
 
         def product_a(half, t, s, acc):
             nc.tensor.matmul_mx(acc[:], **row_set("a", s, t), rhs=x_code[s, half][:].bitcast(FP8X4), rhs_scale=x_scale[s, half][:],
@@ -190,7 +199,7 @@ def tile_list_octant_voxel_fusion_kernel(tc, xT, wgt, offs, wa, ba, wb_words, wb
                                 lhsT_scale=wb_scale[:, s, t * P : (t + 1) * P],
                                 rhs=x_code[s, half][:].bitcast(FP8X4), rhs_scale=x_scale[s, half][:], start=s == 0, stop=s == PASSES - 1)
 
-        gated = [sb([P, PACK, HALF], F32, f"gated{half}") for half in range(HALVES)]
+        gated = [sb([P, PACK, HALF], F32, "gated0"), shared[:, :2048].rearrange("p (t j) -> p t j", t=PACK)]
 
         def gate_times_b(half, t, acc_a, acc_b):
             gate = scratch([P, HALF], "gate")
@@ -206,11 +215,15 @@ def tile_list_octant_voxel_fusion_kernel(tc, xT, wgt, offs, wa, ba, wb_words, wb
             product_a(0, t, 1, open_banks[t][0])
             product_b(0, t, 1, open_banks[t][1])
             gate_times_b(0, t, *open_banks[t])
-            if t % 2:
-                round_w(nc.scalar.copy, "c", 0, t // 2)
-        round_w(nc.vector.tensor_copy, "c", 1, 0)
-        quantise_w("c", 0, 0)
-        round_w(nc.vector.tensor_copy, "c", 1, 1)
+        nc.gpsimd.tensor_scalar(late[:, quarter : 2 * quarter].rearrange("p (t m i) -> p m t i", t=2, i=PACK),
+                                w_raw["c", 0][:].rearrange("p i (m t) -> p m t i", t=PACK)[:, :, 2:4, :], 1.0, 0.0, ALU.mult, ALU.add)
+        nc.gpsimd.tensor_scalar(late[:, 2 * quarter :].rearrange("p (t m i) -> p m t i", t=PACK, i=PACK),
+                                w_raw["c", 1][:].rearrange("p i (m t) -> p m t i", t=PACK), 1.0, 0.0, ALU.mult, ALU.add)
+        late_code = sb([P, 8 * P], U32, "late_code")
+        late_scale = sb([P, 8 * P], U8, "late_scale")
+        for n, (s, pair) in enumerate(((0, 0), (0, 1), (1, 0), (1, 1))):
+            w_code["c", s, pair] = late_code[:, n * 2 * P : (n + 1) * 2 * P]
+            w_scale["c", s, pair] = late_scale[:, n * 2 * P : (n + 1) * 2 * P]
 
         for t in range(PACK):
             acc_a, acc_b = bank(), bank()
@@ -219,10 +232,8 @@ def tile_list_octant_voxel_fusion_kernel(tc, xT, wgt, offs, wa, ba, wb_words, wb
             for s in range(PASSES):
                 product_b(1, t, s, acc_b)
             gate_times_b(1, t, acc_a, acc_b)
-            if t == 0:
-                quantise_w("c", 0, 1)
-                for pair in range(2):
-                    quantise_w("c", 1, pair)
+            if t == 1:
+                nc.vector.quantize_mx(late_code[:].bitcast(FP8X4), late_scale[:], late[:])
 
         def product_c(j0):
             half, at = divmod(j0, HALF)

@@ -86,8 +86,11 @@ def tile_list_octant_voxel_fusion_kernel(tc, xT, wgt, offs, wa, ba, wb_words, wb
                 load_plane(s, i)
         load_weight("a", wa, 1)
         nc.sync.dma_start(ba_sb[:], ba.rearrange("(p t) -> p t", t=PACK))
-        for s in range(PASSES):
-            load_weight("c", wc, s)
+        c_half = []
+        for u in range(2):
+            c_half.append(sb([P, PACK, H // 2], F32, f"raw_c0{u}"))
+            nc.sync.dma_start(c_half[u][:], wc[:K_PASS, u * H // 2 : (u + 1) * H // 2].rearrange("(p i) c -> p i c", i=PACK))
+        load_weight("c", wc, 1)
         nc.sync.dma_start(wo_code[:].bitcast(I32), wo_words[0].rearrange("p e i -> p (e i)").bitcast(I32))
         for q in range(4):
             nc.sync.dma_start(wo_scale[32 * q : 32 * q + 4, :].bitcast(I32), wo_scales[0, 4 * q : 4 * q + 4, :].bitcast(I32))
@@ -131,7 +134,7 @@ def tile_list_octant_voxel_fusion_kernel(tc, xT, wgt, offs, wa, ba, wb_words, wb
 
         def round_x(src, width, last=False):
             if last:
-                x_round = shared[:, 1536:2560].bitcast(BF16).rearrange("p (c i) -> p c i", i=PACK)
+                x_round = shared[:, 1920:2944].bitcast(BF16).rearrange("p (c i) -> p c i", i=PACK)
             else:
                 x_round = sb([P, width, PACK], BF16, "x_round", bufs=4)
             nc.scalar.copy(x_round[:].rearrange("p (c l) i -> p c i l", l=LINE), src.rearrange("p i (c l) -> p c i l", l=LINE))
@@ -140,7 +143,7 @@ def tile_list_octant_voxel_fusion_kernel(tc, xT, wgt, offs, wa, ba, wb_words, wb
         def quantise_x(s, j0, width, x_round):
             half, at = divmod(j0, HALF)
             if at == 0:
-                x_code[s, half] = sb([P, HALF], U32, f"x_code{s}{half}")
+                x_code[s, half] = sb([P, HALF], U32, f"x_code{s}{half}", tag="raw_c00" if (s, half) == (1, 1) else None)
                 x_scale[s, half] = sb([P, HALF], U8, f"x_scale{s}{half}")
             nc.vector.quantize_mx(x_code[s, half][:, at : at + width].bitcast(FP8X4), x_scale[s, half][:, at : at + width],
                                   x_round[:].rearrange("p c i -> p (c i)"))
@@ -187,8 +190,10 @@ def tile_list_octant_voxel_fusion_kernel(tc, xT, wgt, offs, wa, ba, wb_words, wb
             if n == 1:
                 quarter = 2 * P * PACK
                 late = shared[:, 1024:].bitcast(BF16)
-                nc.vector.tensor_copy(late[:, :quarter].rearrange("p (t m i) -> p m i t", t=2, i=PACK),
-                                      w_raw["c", 0][:].rearrange("p i (m t) -> p m i t", t=PACK)[:, :, :, 0:2])
+                first = late[:, : 2 * quarter].rearrange("p (t m i) -> p m i t", t=PACK, i=PACK)
+                for pair in range(2):
+                    nc.vector.tensor_copy(first[:, : P // 2, :, 2 * pair : 2 * pair + 2],
+                                          c_half[0][:].rearrange("p i (m t) -> p m i t", t=PACK)[:, :, :, 2 * pair : 2 * pair + 2])
 
         def product_a(half, t, s, acc):
             nc.tensor.matmul_mx(acc[:], **row_set("a", s, t), rhs=x_code[s, half][:].bitcast(FP8X4), rhs_scale=x_scale[s, half][:],
@@ -215,8 +220,8 @@ def tile_list_octant_voxel_fusion_kernel(tc, xT, wgt, offs, wa, ba, wb_words, wb
             product_a(0, t, 1, open_banks[t][0])
             product_b(0, t, 1, open_banks[t][1])
             gate_times_b(0, t, *open_banks[t])
-        nc.gpsimd.tensor_scalar(late[:, quarter : 2 * quarter].rearrange("p (t m i) -> p m t i", t=2, i=PACK),
-                                w_raw["c", 0][:].rearrange("p i (m t) -> p m t i", t=PACK)[:, :, 2:4, :], 1.0, 0.0, ALU.mult, ALU.add)
+        nc.gpsimd.tensor_scalar(late[:, : 2 * quarter].rearrange("p (t m i) -> p m t i", t=PACK, i=PACK)[:, P // 2 :, :, :],
+                                c_half[1][:].rearrange("p i (m t) -> p m t i", t=PACK), 1.0, 0.0, ALU.mult, ALU.add)
         nc.gpsimd.tensor_scalar(late[:, 2 * quarter :].rearrange("p (t m i) -> p m t i", t=PACK, i=PACK),
                                 w_raw["c", 1][:].rearrange("p i (m t) -> p m t i", t=PACK), 1.0, 0.0, ALU.mult, ALU.add)
         late_code = sb([P, 8 * P], U32, "late_code")

@@ -73,7 +73,7 @@ def tile_list_octant_voxel_fusion_kernel(tc, xT, wgt, offs, wa, ba, wb_words, wb
             w_raw[name, s] = sb([P, PACK, H], F32, f"raw_{name}{s}")
             nc.sync.dma_start(w_raw[name, s][:], w[s * K_PASS : (s + 1) * K_PASS, :].rearrange("(p i) c -> p i c", i=PACK))
 
-        nc.sync.dma_start(two_rows[:], wgt.rearrange("(g r) (c j) -> g (r c) j", r=GROUP, j=P)[:, 0:GROUP, :])
+        nc.sync.dma_start(two_rows[:], wgt.rearrange("(u r) (c j) -> u (r c) j", r=GROUP // 2, j=P)[:, 0 : S // P, :])
         nc.sync.dma_start(offsets[:], offs)
         nc.sync.dma_start(wb_words_raw[:].bitcast(I32), wb_words.rearrange("s p e -> p s e").bitcast(I32))
         for q in range(4):
@@ -125,7 +125,8 @@ def tile_list_octant_voxel_fusion_kernel(tc, xT, wgt, offs, wa, ba, wb_words, wb
 
         shared = sb([P, 3072], F32, "shared")
         picked0 = sb([P, PACK, S], F32, "picked0")
-        picked1 = [sb([P, PACK, width], F32, f"picked1{n}") for n, width in enumerate(PIECES)]
+        picked1_row = sb([P, PACK * S], F32, "picked1")
+        picked1 = [picked1_row[:].rearrange("p (i j) -> p i j", i=PACK)[:, :, j0 : j0 + width] for j0, width in zip(starts, PIECES)]
         x_code, x_scale, w_code, w_scale, w_round = {}, {}, {}, {}, {}
 
         def gather(dst, s, i, j0, width):
@@ -170,8 +171,7 @@ def tile_list_octant_voxel_fusion_kernel(tc, xT, wgt, offs, wa, ba, wb_words, wb
         rounded0 = [round_x(picked0[:, :, half * HALF : (half + 1) * HALF], HALF) for half in range(HALVES)]
 
         for i in range(PACK - 1):
-            for n, width in enumerate(PIECES):
-                gather(picked1[n][:, i, :], 1, i, starts[n], width)
+            gather(picked1_row[:, i * S : (i + 1) * S], 1, i, 0, S)
             if i < HALVES:
                 quantise_x(0, i * HALF, HALF, rounded0[i])
         for pair in range(2):
@@ -181,7 +181,7 @@ def tile_list_octant_voxel_fusion_kernel(tc, xT, wgt, offs, wa, ba, wb_words, wb
         rounded1 = []
         for n, width in enumerate(PIECES):
             gather(picked1[n][:, PACK - 1, :], 1, PACK - 1, starts[n], width)
-            rounded1.append(round_x(picked1[n][:], width, n == len(PIECES) - 1))
+            rounded1.append(round_x(picked1[n], width, n == len(PIECES) - 1))
         for n, width in enumerate(PIECES):
             quantise_x(1, starts[n], width, rounded1[n])
             if n < 2:
@@ -204,7 +204,11 @@ def tile_list_octant_voxel_fusion_kernel(tc, xT, wgt, offs, wa, ba, wb_words, wb
                                 lhsT_scale=wb_scale[:, s, t * P : (t + 1) * P],
                                 rhs=x_code[s, half][:].bitcast(FP8X4), rhs_scale=x_scale[s, half][:], start=s == 0, stop=s == PASSES - 1)
 
-        gated = [sb([P, PACK, HALF], F32, "gated0"), shared[:, :2048].rearrange("p (t j) -> p t j", t=PACK)]
+        gated = [sb([P, PACK, HALF], F32, "gated0"), shared[:, 512:2560].rearrange("p (t j) -> p t j", t=PACK)]
+
+        def round_rest(pair):
+            nc.scalar.copy(first[:, P // 2 :, :, 2 * pair : 2 * pair + 2],
+                           c_half[1][:].rearrange("p i (m t) -> p m i t", t=PACK)[:, :, :, 2 * pair : 2 * pair + 2])
 
         def gate_times_b(half, t, acc_a, acc_b):
             gate = scratch([P, HALF], "gate")
@@ -220,8 +224,8 @@ def tile_list_octant_voxel_fusion_kernel(tc, xT, wgt, offs, wa, ba, wb_words, wb
             product_a(0, t, 1, open_banks[t][0])
             product_b(0, t, 1, open_banks[t][1])
             gate_times_b(0, t, *open_banks[t])
-        nc.gpsimd.tensor_scalar(late[:, : 2 * quarter].rearrange("p (t m i) -> p m t i", t=PACK, i=PACK)[:, P // 2 :, :, :],
-                                c_half[1][:].rearrange("p i (m t) -> p m t i", t=PACK), 1.0, 0.0, ALU.mult, ALU.add)
+            if t == 2:
+                round_rest(0)
         nc.gpsimd.tensor_scalar(late[:, 2 * quarter :].rearrange("p (t m i) -> p m t i", t=PACK, i=PACK),
                                 w_raw["c", 1][:].rearrange("p i (m t) -> p m t i", t=PACK), 1.0, 0.0, ALU.mult, ALU.add)
         late_code = sb([P, 8 * P], U32, "late_code")
@@ -237,7 +241,9 @@ def tile_list_octant_voxel_fusion_kernel(tc, xT, wgt, offs, wa, ba, wb_words, wb
             for s in range(PASSES):
                 product_b(1, t, s, acc_b)
             gate_times_b(1, t, acc_a, acc_b)
-            if t == 1:
+            if t == 0:
+                round_rest(1)
+            if t == 0:
                 nc.vector.quantize_mx(late_code[:].bitcast(FP8X4), late_scale[:], late[:])
 
         def product_c(j0):

@@ -28,7 +28,7 @@ BLOCK = 128
 LINE = 4
 PIECES = (256, 256, 512)
 STORES = (256, 256, 256, 128, 128)
-C_AHEAD = 3
+C_AHEAD = 4
 
 
 def tile_list_octant_voxel_fusion_kernel(tc, xT, wgt, offs, wa, ba, wb_words, wb_scales, wc, wo_words, wo_scales, bo, out):
@@ -213,7 +213,12 @@ def tile_list_octant_voxel_fusion_kernel(tc, xT, wgt, offs, wa, ba, wb_words, wb
         def gate_times_b(half, t, acc_a, acc_b):
             gate = scratch([P, HALF], "gate")
             nc.scalar.activation(gate[:], acc_a[:], ACT.Sigmoid, bias=ba_sb[:, t : t + 1])
-            nc.vector.tensor_tensor(gated[half][:, t, :], acc_b[:], gate[:], ALU.mult)
+            if (half, t) == (HALVES - 1, PACK - 1):
+                b_copy = sb([P, HALF], F32, "b_copy")
+                nc.scalar.copy(b_copy[:], acc_b[:])
+                nc.gpsimd.tensor_tensor(gated[half][:, t, :], b_copy[:], gate[:], ALU.mult)
+            else:
+                nc.vector.tensor_tensor(gated[half][:, t, :], acc_b[:], gate[:], ALU.mult)
 
         open_banks = []
         for t in range(PACK):

@@ -27,7 +27,7 @@ HALVES = S // HALF
 BLOCK = 128
 LINE = 4
 PIECES = (256, 256, 512)
-STORES = (256, 256, 256, 128, 128)
+STORES = (512, 256, 128, 128)
 C_AHEAD = 4
 
 
@@ -115,6 +115,9 @@ def tile_list_octant_voxel_fusion_kernel(tc, xT, wgt, offs, wa, ba, wb_words, wb
             for c in range(count):
                 nc.tensor.transpose(back[:, c * P : (c + 1) * P], repeated[:, c, :], ident[:])
             nc.scalar.copy(weight[:, j0 : j0 + width], back[:, :width])
+            if j0 == starts[1]:
+                weight_piece = sb([P, width], F32, "weight_piece")
+                nc.scalar.copy(weight_piece[:], back[:, :width])
 
         wb_code = sb([P, PASSES, 2 * H], U8, "wb_code")
         wb_scale = sb([P, PASSES, H], U8, "wb_scale")
@@ -131,7 +134,7 @@ def tile_list_octant_voxel_fusion_kernel(tc, xT, wgt, offs, wa, ba, wb_words, wb
 
         def gather(dst, s, i, j0, width):
             nc.vector.tensor_tensor(dst, planes[s, i][:].indirect(offsets[:, j0 // GROUP : (j0 + width) // GROUP]),
-                                    weight[:, j0 : j0 + width], ALU.mult)
+                                    weight_piece[:] if (s, i, j0) == (1, PACK - 1, starts[1]) else weight[:, j0 : j0 + width], ALU.mult)
 
         def round_x(src, width, last=False):
             if last:
@@ -155,7 +158,7 @@ def tile_list_octant_voxel_fusion_kernel(tc, xT, wgt, offs, wa, ba, wb_words, wb
                  w_raw[name, s][:].rearrange("p i (m t) -> p m i t", t=PACK)[:, :, :, 2 * pair : 2 * pair + 2])
 
         def quantise_w(name, s, pair):
-            w_code[name, s, pair] = sb([P, 2 * P], U32, f"w_code{name}{s}{pair}")
+            w_code[name, s, pair] = sb([P, 2 * P], U32, f"w_code{name}{s}{pair}", tag="weight_piece" if (name, s, pair) == ("a", 0, 1) else None)
             w_scale[name, s, pair] = sb([P, 2 * P], U8, f"w_scale{name}{s}{pair}")
             nc.vector.quantize_mx(w_code[name, s, pair][:].bitcast(FP8X4), w_scale[name, s, pair][:],
                                   w_round[name, s, pair][:].rearrange("p t m i -> p (t m i)"))
@@ -176,11 +179,12 @@ def tile_list_octant_voxel_fusion_kernel(tc, xT, wgt, offs, wa, ba, wb_words, wb
                 quantise_x(0, i * HALF, HALF, rounded0[i])
         for pair in range(2):
             round_w(nc.scalar.copy, "a", 0, pair)
-        for pair in range(2):
-            quantise_w("a", 0, pair)
+        quantise_w("a", 0, 0)
         rounded1 = []
         for n, width in enumerate(PIECES):
             gather(picked1[n][:, PACK - 1, :], 1, PACK - 1, starts[n], width)
+            if n == 1:
+                quantise_w("a", 0, 1)
             rounded1.append(round_x(picked1[n], width, n == len(PIECES) - 1))
         for n, width in enumerate(PIECES):
             quantise_x(1, starts[n], width, rounded1[n])
@@ -213,12 +217,13 @@ def tile_list_octant_voxel_fusion_kernel(tc, xT, wgt, offs, wa, ba, wb_words, wb
         def gate_times_b(half, t, acc_a, acc_b):
             gate = scratch([P, HALF], "gate")
             nc.scalar.activation(gate[:], acc_a[:], ACT.Sigmoid, bias=ba_sb[:, t : t + 1])
-            if (half, t) == (HALVES - 1, PACK - 1):
-                b_copy = sb([P, HALF], F32, "b_copy")
-                nc.scalar.copy(b_copy[:], acc_b[:])
-                nc.gpsimd.tensor_tensor(gated[half][:, t, :], b_copy[:], gate[:], ALU.mult)
-            else:
-                nc.vector.tensor_tensor(gated[half][:, t, :], acc_b[:], gate[:], ALU.mult)
+            mine = HALF if half == 0 or t < PACK - 2 else (HALF // 2 if t == PACK - 2 else 0)
+            if mine:
+                nc.vector.tensor_tensor(gated[half][:, t, :mine], acc_b[:, :mine], gate[:, :mine], ALU.mult)
+            if mine < HALF:
+                b_copy = sb([P, HALF - mine], F32, f"b_copy{t}")
+                nc.scalar.copy(b_copy[:], acc_b[:, mine:])
+                nc.gpsimd.tensor_tensor(gated[half][:, t, mine:], b_copy[:], gate[:, mine:], ALU.mult)
 
         open_banks = []
         for t in range(PACK):
@@ -233,11 +238,12 @@ def tile_list_octant_voxel_fusion_kernel(tc, xT, wgt, offs, wa, ba, wb_words, wb
                 round_rest(0)
         nc.gpsimd.tensor_scalar(late[:, 2 * quarter :].rearrange("p (t m i) -> p m t i", t=PACK, i=PACK),
                                 w_raw["c", 1][:].rearrange("p i (m t) -> p m t i", t=PACK), 1.0, 0.0, ALU.mult, ALU.add)
-        late_code = sb([P, 8 * P], U32, "late_code")
-        late_scale = sb([P, 8 * P], U8, "late_scale")
-        for n, (s, pair) in enumerate(((0, 0), (0, 1), (1, 0), (1, 1))):
-            w_code["c", s, pair] = late_code[:, n * 2 * P : (n + 1) * 2 * P]
-            w_scale["c", s, pair] = late_scale[:, n * 2 * P : (n + 1) * 2 * P]
+        late_code = [sb([P, 4 * P], U32, "late_code0", tag="raw_c1"), sb([P, 4 * P], U32, "late_code1")]
+        late_scale = [sb([P, 4 * P], U8, f"late_scale{s}") for s in range(PASSES)]
+        for s in range(PASSES):
+            for pair in range(2):
+                w_code["c", s, pair] = late_code[s][:, pair * 2 * P : (pair + 1) * 2 * P]
+                w_scale["c", s, pair] = late_scale[s][:, pair * 2 * P : (pair + 1) * 2 * P]
 
         for t in range(PACK):
             acc_a, acc_b = bank(), bank()
@@ -249,16 +255,17 @@ def tile_list_octant_voxel_fusion_kernel(tc, xT, wgt, offs, wa, ba, wb_words, wb
             if t == 0:
                 round_rest(1)
             if t == 0:
-                nc.vector.quantize_mx(late_code[:].bitcast(FP8X4), late_scale[:], late[:])
+                for s in range(PASSES):
+                    nc.vector.quantize_mx(late_code[s][:].bitcast(FP8X4), late_scale[s][:], late[:, s * 2 * quarter : (s + 1) * 2 * quarter])
 
         def product_c(j0):
             half, at = divmod(j0, HALF)
             acc = bank()
-            for t in range(PACK):
-                for s in range(PASSES):
+            for s in range(PASSES):
+                for t in range(PACK):
                     nc.tensor.matmul_mx(acc[:, t * P : (t + 1) * P], **row_set("c", s, t),
                                         rhs=x_code[s, half][:, at : at + BLOCK].bitcast(FP8X4), rhs_scale=x_scale[s, half][:, at : at + BLOCK],
-                                        start=s == 0, stop=s == PASSES - 1)
+                                        start=(s, t) == (0, 0), stop=(s, t) == (PASSES - 1, PACK - 1))
             return acc
 
         def add_c(j0, acc, dst):
@@ -266,22 +273,29 @@ def tile_list_octant_voxel_fusion_kernel(tc, xT, wgt, offs, wa, ba, wb_words, wb
             nc.vector.tensor_tensor(dst.rearrange("p (c l t) -> p c t l", l=LINE, t=PACK), acc[:].rearrange("p (t c l) -> p c t l", l=LINE, t=PACK),
                                     gated[half][:, :, at : at + BLOCK].rearrange("p t (c l) -> p c t l", l=LINE), ALU.add)
 
-        def quantise_h(width, h_round):
-            h_code = sb([P, width], U32, "h_code", bufs=3)
+        def quantise_h(j0, width, h_round):
+            if j0 == 0:
+                h_code = sb([P, width], U32, "h_code_first", tag=f"b_copy{PACK - 1}")
+            else:
+                h_code = sb([P, width], U32, "h_code", bufs=3)
             h_scale = sb([P, width], U8, "h_scale", bufs=3)
             nc.vector.quantize_mx(h_code[:].bitcast(FP8X4), h_scale[:], h_round[:])
             return h_code, h_scale
 
         def finish(j0, width, h_code, h_scale):
             acc = bank()
-            result = sb([P, N // P, width], F32, "result", bufs=len(STORES))
+            accs = [acc[:, :width], bank()[:] if width == HALF else acc[:, width : 2 * width]]
+            result = sb([P, N // P, width], F32, f"result{j0}")
             for u in range(N // P):
-                nc.tensor.matmul_mx(acc[:, u * width : (u + 1) * width], lhsT=wo_code[:, PACK * u * P : PACK * (u + 1) * P].bitcast(FP8X4),
+                nc.tensor.matmul_mx(accs[u], lhsT=wo_code[:, PACK * u * P : PACK * (u + 1) * P].bitcast(FP8X4),
                                     lhsT_scale=wo_scale[:, u * P : (u + 1) * P], rhs=h_code[:].bitcast(FP8X4), rhs_scale=h_scale[:],
                                     start=True, stop=True)
             for u in range(N // P):
-                nc.scalar.activation(result[:, u, :], acc[:, u * width : (u + 1) * width], ACT.Identity, bias=bo_sb[:, u : u + 1])
-            nc.sync.dma_start(out.rearrange("(u p) j -> p u j", p=P)[:, :, j0 : j0 + width], result[:])
+                nc.scalar.activation(result[:, u, :], accs[u], ACT.Identity, bias=bo_sb[:, u : u + 1])
+                if width == HALF:
+                    nc.sync.dma_start(out[u * P : (u + 1) * P, j0 : j0 + width], result[:, u, :])
+            if width < HALF:
+                nc.sync.dma_start(out.rearrange("(u p) j -> p u j", p=P)[:, :, j0 : j0 + width], result[:])
 
         blocks = S // BLOCK
         store_of, completed_by = {}, {}
@@ -296,12 +310,12 @@ def tile_list_octant_voxel_fusion_kernel(tc, xT, wgt, offs, wa, ba, wb_words, wb
             if b < blocks:
                 j0, width = store_of[b]
                 if j0 not in h_rounds:
-                    h_rounds[j0] = sb([P, width * PACK], BF16, "h_round", bufs=3)
+                    h_rounds[j0] = sb([P, width * PACK], BF16, f"h_round{j0}")
                 at = (b * BLOCK - j0) * PACK
                 add_c(b * BLOCK, c_banks[b], h_rounds[j0][:, at : at + BLOCK * PACK])
             if b - 1 in completed_by:
                 j0, width = completed_by[b - 1]
-                h_quantised[j0] = quantise_h(width, h_rounds[j0])
+                h_quantised[j0] = quantise_h(j0, width, h_rounds[j0])
             if b + C_AHEAD < blocks:
                 c_banks[b + C_AHEAD] = product_c((b + C_AHEAD) * BLOCK)
             if b - 2 in completed_by:

@@ -24,6 +24,7 @@ PASSES = K // K_PASS
 GROUP = 16
 HALF = 512
 HALVES = S // HALF
+QUARTER = HALF // 2
 BLOCK = 128
 LINE = 4
 PIECES = (256, 256, 512)
@@ -65,10 +66,6 @@ def tile_list_octant_voxel_fusion_kernel(tc, xT, wgt, offs, wa, ba, wb_words, wb
         x_rows = xT.rearrange("(s p i) t -> s i p t", s=PASSES, i=PACK)
         planes, w_raw = {}, {}
 
-        def load_plane(s, i):
-            planes[s, i] = sb([P, T], F32, f"plane{s}{i}")
-            nc.sync.dma_start(planes[s, i][:], x_rows[s, i])
-
         def load_weight(name, w, s):
             w_raw[name, s] = sb([P, PACK, H], F32, f"raw_{name}{s}")
             nc.sync.dma_start(w_raw[name, s][:], w[s * K_PASS : (s + 1) * K_PASS, :].rearrange("(p i) c -> p i c", i=PACK))
@@ -81,16 +78,14 @@ def tile_list_octant_voxel_fusion_kernel(tc, xT, wgt, offs, wa, ba, wb_words, wb
                               wb_scales[:, 4 * q : 4 * q + 4, :].rearrange("s r e -> r s e").bitcast(I32))
         for s in range(PASSES):
             for i in range(PACK):
-                if (s, i) == (PASSES - 1, PACK - 1):
+                if (s, i) == (1, 2):
                     load_weight("a", wa, 0)
-                load_plane(s, i)
+                planes[s, i] = sb([P, T], F32, f"plane{s}{i}")
+                nc.sync.dma_start(planes[s, i][:], x_rows[s, i])
         load_weight("a", wa, 1)
         nc.sync.dma_start(ba_sb[:], ba.rearrange("(p t) -> p t", t=PACK))
-        c_half = []
-        for u in range(2):
-            c_half.append(sb([P, PACK, H // 2], F32, f"raw_c0{u}"))
-            nc.sync.dma_start(c_half[u][:], wc[:K_PASS, u * H // 2 : (u + 1) * H // 2].rearrange("(p i) c -> p i c", i=PACK))
-        load_weight("c", wc, 1)
+        for s in range(PASSES):
+            load_weight("c", wc, s)
         nc.sync.dma_start(wo_code[:].bitcast(I32), wo_words[0].rearrange("p e i -> p (e i)").bitcast(I32))
         for q in range(4):
             nc.sync.dma_start(wo_scale[32 * q : 32 * q + 4, :].bitcast(I32), wo_scales[0, 4 * q : 4 * q + 4, :].bitcast(I32))
@@ -103,6 +98,7 @@ def tile_list_octant_voxel_fusion_kernel(tc, xT, wgt, offs, wa, ba, wb_words, wb
             return sb(shape, F32, name, tag="scratch", bufs=3)
 
         runs = S // P
+        weight_piece = {}
         by_column = bank()
         nc.tensor.transpose(by_column[:, :P], two_rows[:], ident[:])
         by_run = by_column[:, :P].rearrange("j (g d c) -> j c g d", d=2, c=runs)
@@ -115,9 +111,9 @@ def tile_list_octant_voxel_fusion_kernel(tc, xT, wgt, offs, wa, ba, wb_words, wb
             for c in range(count):
                 nc.tensor.transpose(back[:, c * P : (c + 1) * P], repeated[:, c, :], ident[:])
             nc.scalar.copy(weight[:, j0 : j0 + width], back[:, :width])
-            if j0 == starts[1]:
-                weight_piece = sb([P, width], F32, "weight_piece")
-                nc.scalar.copy(weight_piece[:], back[:, :width])
+            if j0 < HALF:
+                weight_piece[j0] = sb([P, width], F32, f"weight_piece{j0}")
+                nc.scalar.copy(weight_piece[j0][:], back[:, :width])
 
         wb_code = sb([P, PASSES, 2 * H], U8, "wb_code")
         wb_scale = sb([P, PASSES, H], U8, "wb_scale")
@@ -126,78 +122,48 @@ def tile_list_octant_voxel_fusion_kernel(tc, xT, wgt, offs, wa, ba, wb_words, wb
         nc.vector.tensor_copy(wb_scale[:].rearrange("p s (t m) -> p s t m", t=PACK),
                               wb_scales_raw[:].rearrange("p s (m t) -> p s t m", t=PACK))
 
-        shared = sb([P, 3072], F32, "shared")
-        picked0 = sb([P, PACK, S], F32, "picked0")
-        picked1_row = sb([P, PACK * S], F32, "picked1")
-        picked1 = [picked1_row[:].rearrange("p (i j) -> p i j", i=PACK)[:, :, j0 : j0 + width] for j0, width in zip(starts, PIECES)]
+        picked = [sb([P, PACK * S], F32, f"picked{s}") for s in range(PASSES)]
         x_code, x_scale, w_code, w_scale, w_round = {}, {}, {}, {}, {}
+        pair_width = 2 * P * PACK
 
-        def gather(dst, s, i, j0, width):
-            nc.vector.tensor_tensor(dst, planes[s, i][:].indirect(offsets[:, j0 // GROUP : (j0 + width) // GROUP]),
-                                    weight_piece[:] if (s, i, j0) == (1, PACK - 1, starts[1]) else weight[:, j0 : j0 + width], ALU.mult)
+        gated = [sb([P, PACK * HALF], F32, f"gated{half}") for half in range(HALVES)]
 
-        def round_x(src, width, last=False):
-            if last:
-                x_round = shared[:, 1920:2944].bitcast(BF16).rearrange("p (c i) -> p c i", i=PACK)
-            else:
-                x_round = sb([P, width, PACK], BF16, "x_round", bufs=4)
-            nc.scalar.copy(x_round[:].rearrange("p (c l) i -> p c i l", l=LINE), src.rearrange("p i (c l) -> p c i l", l=LINE))
-            return x_round
+        def gather(s, i, j0, width, factor=None):
+            nc.vector.tensor_tensor(picked[s][:, i * S + j0 : i * S + j0 + width],
+                                    planes[s, i][:].indirect(offsets[:, j0 // GROUP : (j0 + width) // GROUP]),
+                                    weight[:, j0 : j0 + width] if factor is None else factor, ALU.mult)
 
-        def quantise_x(s, j0, width, x_round):
+        def round_planes(s, i, j0, width, dst):
+            nc.scalar.copy(dst.rearrange("p (c l i) -> p c i l", l=LINE, i=PACK)[:, :, i : i + 2, :],
+                           picked[s][:].rearrange("p (i j) -> p i j", i=PACK)[:, i : i + 2, j0 : j0 + width].rearrange("p i (c l) -> p c i l", l=LINE))
+
+        def quantise_x(s, j0, width, x_round, tag=None):
             half, at = divmod(j0, HALF)
             if at == 0:
-                x_code[s, half] = sb([P, HALF], U32, f"x_code{s}{half}", tag="raw_c00" if (s, half) == (1, 1) else None)
+                x_code[s, half] = sb([P, HALF], U32, f"x_code{s}{half}", tag=tag)
                 x_scale[s, half] = sb([P, HALF], U8, f"x_scale{s}{half}")
-            nc.vector.quantize_mx(x_code[s, half][:, at : at + width].bitcast(FP8X4), x_scale[s, half][:, at : at + width],
-                                  x_round[:].rearrange("p c i -> p (c i)"))
+            nc.vector.quantize_mx(x_code[s, half][:, at : at + width].bitcast(FP8X4), x_scale[s, half][:, at : at + width], x_round)
 
-        def round_w(copy, name, s, pair):
-            w_round[name, s, pair] = sb([P, 2, P, PACK], BF16, f"w_round{name}{s}{pair}")
-            copy(w_round[name, s, pair][:].rearrange("p t m i -> p m i t"),
+        def round_w(copy, name, s, pair, dst=None):
+            w_round[name, s, pair] = sb([P, pair_width], BF16, f"w_round{name}{s}{pair}")[:] if dst is None else dst
+            copy(w_round[name, s, pair].rearrange("p (t m i) -> p m i t", t=2, i=PACK),
                  w_raw[name, s][:].rearrange("p i (m t) -> p m i t", t=PACK)[:, :, :, 2 * pair : 2 * pair + 2])
 
-        def quantise_w(name, s, pair):
-            w_code[name, s, pair] = sb([P, 2 * P], U32, f"w_code{name}{s}{pair}", tag="weight_piece" if (name, s, pair) == ("a", 0, 1) else None)
-            w_scale[name, s, pair] = sb([P, 2 * P], U8, f"w_scale{name}{s}{pair}")
-            nc.vector.quantize_mx(w_code[name, s, pair][:].bitcast(FP8X4), w_scale[name, s, pair][:],
-                                  w_round[name, s, pair][:].rearrange("p t m i -> p (t m i)"))
+        def quantise_w(name, s, pair, tag=None):
+            w_code[name, s, pair] = sb([P, 2 * P], U32, f"w_code{name}{s}{pair}", tag=tag)[:]
+            w_scale[name, s, pair] = sb([P, 2 * P], U8, f"w_scale{name}{s}{pair}")[:]
+            nc.vector.quantize_mx(w_code[name, s, pair].bitcast(FP8X4), w_scale[name, s, pair], w_round[name, s, pair])
+
+        def quantise_two(name, both, rounded, tag=None):
+            code, scale = sb([P, H], U32, f"w_code{name}", tag=tag), sb([P, H], U8, f"w_scale{name}")
+            for n, (s, pair) in enumerate(both):
+                w_code[name[0], s, pair] = code[:, n * 2 * P : (n + 1) * 2 * P]
+                w_scale[name[0], s, pair] = scale[:, n * 2 * P : (n + 1) * 2 * P]
+            nc.vector.quantize_mx(code[:].bitcast(FP8X4), scale[:], rounded)
 
         def row_set(name, s, t):
             cols = slice(t % 2 * P, (t % 2 + 1) * P)
             return dict(lhsT=w_code[name, s, t // 2][:, cols].bitcast(FP8X4), lhsT_scale=w_scale[name, s, t // 2][:, cols])
-
-        for j0, width in zip(starts, PIECES):
-            gather(picked0[:, 0, j0 : j0 + width], 0, 0, j0, width)
-        for i in range(1, PACK):
-            gather(picked0[:, i, :], 0, i, 0, S)
-        rounded0 = [round_x(picked0[:, :, half * HALF : (half + 1) * HALF], HALF) for half in range(HALVES)]
-
-        for i in range(PACK - 1):
-            gather(picked1_row[:, i * S : (i + 1) * S], 1, i, 0, S)
-            if i < HALVES:
-                quantise_x(0, i * HALF, HALF, rounded0[i])
-        for pair in range(2):
-            round_w(nc.scalar.copy, "a", 0, pair)
-        quantise_w("a", 0, 0)
-        rounded1 = []
-        for n, width in enumerate(PIECES):
-            gather(picked1[n][:, PACK - 1, :], 1, PACK - 1, starts[n], width)
-            if n == 1:
-                quantise_w("a", 0, 1)
-            rounded1.append(round_x(picked1[n], width, n == len(PIECES) - 1))
-        for n, width in enumerate(PIECES):
-            quantise_x(1, starts[n], width, rounded1[n])
-            if n < 2:
-                round_w(nc.vector.tensor_copy, "a", 1, n)
-                quantise_w("a", 1, n)
-            if n == 1:
-                quarter = 2 * P * PACK
-                late = shared[:, 1024:].bitcast(BF16)
-                first = late[:, : 2 * quarter].rearrange("p (t m i) -> p m i t", t=PACK, i=PACK)
-                for pair in range(2):
-                    nc.vector.tensor_copy(first[:, : P // 2, :, 2 * pair : 2 * pair + 2],
-                                          c_half[0][:].rearrange("p i (m t) -> p m i t", t=PACK)[:, :, :, 2 * pair : 2 * pair + 2])
 
         def product_a(half, t, s, acc):
             nc.tensor.matmul_mx(acc[:], **row_set("a", s, t), rhs=x_code[s, half][:].bitcast(FP8X4), rhs_scale=x_scale[s, half][:],
@@ -208,42 +174,67 @@ def tile_list_octant_voxel_fusion_kernel(tc, xT, wgt, offs, wa, ba, wb_words, wb
                                 lhsT_scale=wb_scale[:, s, t * P : (t + 1) * P],
                                 rhs=x_code[s, half][:].bitcast(FP8X4), rhs_scale=x_scale[s, half][:], start=s == 0, stop=s == PASSES - 1)
 
-        gated = [sb([P, PACK, HALF], F32, "gated0"), shared[:, 512:2560].rearrange("p (t j) -> p t j", t=PACK)]
+        rounded0 = [sb([P, HALF * PACK], BF16, f"x_round0{half}")[:] for half in range(HALVES)]
+        for i in range(PACK):
+            for j0, width in zip(starts, PIECES) if i == 0 else [(0, S)]:
+                gather(0, i, j0, width)
+            if i % 2:
+                for half in range(HALVES):
+                    round_planes(0, i - 1, half * HALF, HALF, rounded0[half])
 
-        def round_rest(pair):
-            nc.scalar.copy(first[:, P // 2 :, :, 2 * pair : 2 * pair + 2],
-                           c_half[1][:].rearrange("p i (m t) -> p m i t", t=PACK)[:, :, :, 2 * pair : 2 * pair + 2])
+        for pair in range(2):
+            round_w(nc.scalar.copy, "a", 0, pair)
+        fence = sb([P, 5 * pair_width], BF16, "fence", tag="raw_a0")
+        rounded1 = [fence[:, 3 * pair_width :], fence[:, pair_width : 3 * pair_width]]
+        for i in range(PACK - 1):
+            gather(1, i, 0, S)
+            if i < HALVES:
+                quantise_x(0, i * HALF, HALF, rounded0[i], tag=f"plane1{i}")
+            if i == 1:
+                for half in range(HALVES):
+                    round_planes(1, 0, half * HALF, HALF, rounded1[half])
+        for j0 in range(0, S, QUARTER):
+            gather(1, PACK - 1, j0, QUARTER, weight_piece[j0][:] if j0 < HALF else None)
+            if j0 < HALF:
+                quantise_w("a", 0, j0 // QUARTER, tag=f"weight_piece{j0}")
+        for j0 in range(0, S, QUARTER):
+            half, at = divmod(j0, HALF)
+            round_planes(1, 2, j0, QUARTER, rounded1[half][:, at * PACK : (at + QUARTER) * PACK])
+        round_w(nc.scalar.copy, "a", 1, 1, fence[:, :pair_width])
+
+        quantise_x(1, 0, HALF, rounded1[0])
+        round_w(nc.vector.tensor_copy, "a", 1, 0)
+        quantise_w("a", 1, 0)
+        quantise_x(1, HALF, HALF, rounded1[1], tag="w_rounda10")
+        quantise_w("a", 1, 1)
 
         def gate_times_b(half, t, acc_a, acc_b):
             gate = scratch([P, HALF], "gate")
             nc.scalar.activation(gate[:], acc_a[:], ACT.Sigmoid, bias=ba_sb[:, t : t + 1])
             mine = HALF if half == 0 or t < PACK - 2 else (HALF // 2 if t == PACK - 2 else 0)
+            dst = gated[half][:, t * HALF : (t + 1) * HALF]
             if mine:
-                nc.vector.tensor_tensor(gated[half][:, t, :mine], acc_b[:, :mine], gate[:, :mine], ALU.mult)
+                nc.vector.tensor_tensor(dst[:, :mine], acc_b[:, :mine], gate[:, :mine], ALU.mult)
             if mine < HALF:
-                b_copy = sb([P, HALF - mine], F32, f"b_copy{t}")
+                b_copy = sb([P, HALF - mine], F32, f"b_copy{t}", tag="raw_c0" if mine else None)
                 nc.scalar.copy(b_copy[:], acc_b[:, mine:])
-                nc.gpsimd.tensor_tensor(gated[half][:, t, mine:], b_copy[:], gate[:, mine:], ALU.mult)
+                nc.gpsimd.tensor_tensor(dst[:, mine:], b_copy[:], gate[:, mine:], ALU.mult)
 
-        open_banks = []
+        banks_b = [bank() for t in range(PACK)]
+        banks_a = [bank() for t in range(PACK)]
         for t in range(PACK):
-            open_banks.append((bank(), bank()))
-            product_a(0, t, 0, open_banks[t][0])
-            product_b(0, t, 0, open_banks[t][1])
+            product_b(0, t, 0, banks_b[t])
         for t in range(PACK):
-            product_a(0, t, 1, open_banks[t][0])
-            product_b(0, t, 1, open_banks[t][1])
-            gate_times_b(0, t, *open_banks[t])
-            if t == 2:
-                round_rest(0)
-        nc.gpsimd.tensor_scalar(late[:, 2 * quarter :].rearrange("p (t m i) -> p m t i", t=PACK, i=PACK),
-                                w_raw["c", 1][:].rearrange("p i (m t) -> p m t i", t=PACK), 1.0, 0.0, ALU.mult, ALU.add)
-        late_code = [sb([P, 4 * P], U32, "late_code0", tag="raw_c1"), sb([P, 4 * P], U32, "late_code1")]
-        late_scale = [sb([P, 4 * P], U8, f"late_scale{s}") for s in range(PASSES)]
-        for s in range(PASSES):
-            for pair in range(2):
-                w_code["c", s, pair] = late_code[s][:, pair * 2 * P : (pair + 1) * 2 * P]
-                w_scale["c", s, pair] = late_scale[s][:, pair * 2 * P : (pair + 1) * 2 * P]
+            product_a(0, t, 0, banks_a[t])
+        for product, banks in ((product_b, banks_b), (product_a, banks_a)):
+            for t in range(PACK):
+                product(0, t, 1, banks[t])
+        for t in range(PACK):
+            gate_times_b(0, t, banks_a[t], banks_b[t])
+
+        nc.gpsimd.tensor_scalar(fence[:, : 2 * pair_width].rearrange("p (t m i) -> p m t i", t=PACK, i=PACK),
+                                w_raw["c", 0][:].rearrange("p i (m t) -> p m t i", t=PACK), 1.0, 0.0, ALU.mult, ALU.add)
+        late = sb([P, 2 * pair_width], BF16, "late", tag="raw_c0")
 
         for t in range(PACK):
             acc_a, acc_b = bank(), bank()
@@ -253,10 +244,10 @@ def tile_list_octant_voxel_fusion_kernel(tc, xT, wgt, offs, wa, ba, wb_words, wb
                 product_b(1, t, s, acc_b)
             gate_times_b(1, t, acc_a, acc_b)
             if t == 0:
-                round_rest(1)
-            if t == 0:
-                for s in range(PASSES):
-                    nc.vector.quantize_mx(late_code[s][:].bitcast(FP8X4), late_scale[s][:], late[:, s * 2 * quarter : (s + 1) * 2 * quarter])
+                round_w(nc.scalar.copy, "c", 1, 1, late[:, pair_width:])
+                round_w(nc.vector.tensor_copy, "c", 1, 0, late[:, :pair_width])
+                quantise_two("c0", ((0, 0), (0, 1)), fence[:, : 2 * pair_width])
+                quantise_two("c1", ((1, 0), (1, 1)), late[:])
 
         def product_c(j0):
             half, at = divmod(j0, HALF)
@@ -271,7 +262,7 @@ def tile_list_octant_voxel_fusion_kernel(tc, xT, wgt, offs, wa, ba, wb_words, wb
         def add_c(j0, acc, dst):
             half, at = divmod(j0, HALF)
             nc.vector.tensor_tensor(dst.rearrange("p (c l t) -> p c t l", l=LINE, t=PACK), acc[:].rearrange("p (t c l) -> p c t l", l=LINE, t=PACK),
-                                    gated[half][:, :, at : at + BLOCK].rearrange("p t (c l) -> p c t l", l=LINE), ALU.add)
+                                    gated[half][:].rearrange("p (t j) -> p t j", t=PACK)[:, :, at : at + BLOCK].rearrange("p t (c l) -> p c t l", l=LINE), ALU.add)
 
         def quantise_h(j0, width, h_round):
             if j0 == 0:

@@ -78,14 +78,17 @@ def tile_list_octant_voxel_fusion_kernel(tc, xT, wgt, offs, wa, ba, wb_words, wb
                               wb_scales[:, 4 * q : 4 * q + 4, :].rearrange("s r e -> r s e").bitcast(I32))
         for s in range(PASSES):
             for i in range(PACK):
-                if (s, i) == (1, 2):
+                if (s, i) == (PASSES - 1, PACK - 1):
                     load_weight("a", wa, 0)
                 planes[s, i] = sb([P, T], F32, f"plane{s}{i}")
                 nc.sync.dma_start(planes[s, i][:], x_rows[s, i])
         load_weight("a", wa, 1)
         nc.sync.dma_start(ba_sb[:], ba.rearrange("(p t) -> p t", t=PACK))
-        for s in range(PASSES):
-            load_weight("c", wc, s)
+        c_half = []
+        for u in range(2):
+            c_half.append(sb([P, PACK, H // 2], F32, f"raw_c0{u}"))
+            nc.sync.dma_start(c_half[u][:], wc[:K_PASS, u * H // 2 : (u + 1) * H // 2].rearrange("(p i) c -> p i c", i=PACK))
+        load_weight("c", wc, 1)
         nc.sync.dma_start(wo_code[:].bitcast(I32), wo_words[0].rearrange("p e i -> p (e i)").bitcast(I32))
         for q in range(4):
             nc.sync.dma_start(wo_scale[32 * q : 32 * q + 4, :].bitcast(I32), wo_scales[0, 4 * q : 4 * q + 4, :].bitcast(I32))
@@ -111,7 +114,7 @@ def tile_list_octant_voxel_fusion_kernel(tc, xT, wgt, offs, wa, ba, wb_words, wb
             for c in range(count):
                 nc.tensor.transpose(back[:, c * P : (c + 1) * P], repeated[:, c, :], ident[:])
             nc.scalar.copy(weight[:, j0 : j0 + width], back[:, :width])
-            if j0 < HALF:
+            if j0 == QUARTER:
                 weight_piece[j0] = sb([P, width], F32, f"weight_piece{j0}")
                 nc.scalar.copy(weight_piece[j0][:], back[:, :width])
 
@@ -133,9 +136,9 @@ def tile_list_octant_voxel_fusion_kernel(tc, xT, wgt, offs, wa, ba, wb_words, wb
                                     planes[s, i][:].indirect(offsets[:, j0 // GROUP : (j0 + width) // GROUP]),
                                     weight[:, j0 : j0 + width] if factor is None else factor, ALU.mult)
 
-        def round_planes(s, i, j0, width, dst):
-            nc.scalar.copy(dst.rearrange("p (c l i) -> p c i l", l=LINE, i=PACK)[:, :, i : i + 2, :],
-                           picked[s][:].rearrange("p (i j) -> p i j", i=PACK)[:, i : i + 2, j0 : j0 + width].rearrange("p i (c l) -> p c i l", l=LINE))
+        def round_x(s, j0, width, dst):
+            nc.scalar.copy(dst.rearrange("p (c l i) -> p c i l", l=LINE, i=PACK),
+                           picked[s][:].rearrange("p (i j) -> p i j", i=PACK)[:, :, j0 : j0 + width].rearrange("p i (c l) -> p c i l", l=LINE))
 
         def quantise_x(s, j0, width, x_round, tag=None):
             half, at = divmod(j0, HALF)
@@ -178,35 +181,39 @@ def tile_list_octant_voxel_fusion_kernel(tc, xT, wgt, offs, wa, ba, wb_words, wb
         for i in range(PACK):
             for j0, width in zip(starts, PIECES) if i == 0 else [(0, S)]:
                 gather(0, i, j0, width)
-            if i % 2:
-                for half in range(HALVES):
-                    round_planes(0, i - 1, half * HALF, HALF, rounded0[half])
+        for half in range(HALVES):
+            round_x(0, half * HALF, HALF, rounded0[half])
 
-        for pair in range(2):
-            round_w(nc.scalar.copy, "a", 0, pair)
-        fence = sb([P, 5 * pair_width], BF16, "fence", tag="raw_a0")
-        rounded1 = [fence[:, 3 * pair_width :], fence[:, pair_width : 3 * pair_width]]
+        fence = sb([P, 2 * pair_width], BF16, "fence")
+        rounded1 = [sb([P, HALF * PACK], BF16, "x_round10")[:], fence[:]]
         for i in range(PACK - 1):
             gather(1, i, 0, S)
             if i < HALVES:
-                quantise_x(0, i * HALF, HALF, rounded0[i], tag=f"plane1{i}")
-            if i == 1:
-                for half in range(HALVES):
-                    round_planes(1, 0, half * HALF, HALF, rounded1[half])
-        for j0 in range(0, S, QUARTER):
-            gather(1, PACK - 1, j0, QUARTER, weight_piece[j0][:] if j0 < HALF else None)
-            if j0 < HALF:
-                quantise_w("a", 0, j0 // QUARTER, tag=f"weight_piece{j0}")
-        for j0 in range(0, S, QUARTER):
+                quantise_x(0, i * HALF, HALF, rounded0[i])
+        for pair in range(2):
+            round_w(nc.scalar.copy, "a", 0, pair)
+        quantise_w("a", 0, 0)
+        for j0, width in zip(starts, PIECES):
+            gather(1, PACK - 1, j0, width, weight_piece[j0][:] if j0 == QUARTER else None)
+            if j0 == QUARTER:
+                quantise_w("a", 0, 1, tag=f"weight_piece{j0}")
             half, at = divmod(j0, HALF)
-            round_planes(1, 2, j0, QUARTER, rounded1[half][:, at * PACK : (at + QUARTER) * PACK])
-        round_w(nc.scalar.copy, "a", 1, 1, fence[:, :pair_width])
+            round_x(1, j0, width, rounded1[half][:, at * PACK : (at + width) * PACK])
 
-        quantise_x(1, 0, HALF, rounded1[0])
         round_w(nc.vector.tensor_copy, "a", 1, 0)
+        quantise_x(1, 0, HALF, rounded1[0])
         quantise_w("a", 1, 0)
-        quantise_x(1, HALF, HALF, rounded1[1], tag="w_rounda10")
+        round_w(nc.vector.tensor_copy, "a", 1, 1)
+        first_c = gated[1][:, HALF : 3 * HALF].bitcast(BF16)
+
+        def round_first_c(copy, u, pair):
+            copy(first_c.rearrange("p (t m i) -> p m i t", t=PACK, i=PACK)[:, u * P // 2 : (u + 1) * P // 2, :, 2 * pair : 2 * pair + 2],
+                 c_half[u][:].rearrange("p i (m t) -> p m i t", t=PACK)[:, :, :, 2 * pair : 2 * pair + 2])
+
+        for pair in range(2):
+            round_first_c(nc.vector.tensor_copy, 0, pair)
         quantise_w("a", 1, 1)
+        quantise_x(1, HALF, HALF, rounded1[1], tag="raw_c00")
 
         def gate_times_b(half, t, acc_a, acc_b):
             gate = scratch([P, HALF], "gate")
@@ -216,25 +223,26 @@ def tile_list_octant_voxel_fusion_kernel(tc, xT, wgt, offs, wa, ba, wb_words, wb
             if mine:
                 nc.vector.tensor_tensor(dst[:, :mine], acc_b[:, :mine], gate[:, :mine], ALU.mult)
             if mine < HALF:
-                b_copy = sb([P, HALF - mine], F32, f"b_copy{t}", tag="raw_c0" if mine else None)
+                b_copy = sb([P, HALF - mine], F32, f"b_copy{t}", tag="fence" if mine else None)
                 nc.scalar.copy(b_copy[:], acc_b[:, mine:])
                 nc.gpsimd.tensor_tensor(dst[:, mine:], b_copy[:], gate[:, mine:], ALU.mult)
 
-        banks_b = [bank() for t in range(PACK)]
-        banks_a = [bank() for t in range(PACK)]
+        banks_a, banks_b = [], []
         for t in range(PACK):
+            banks_a.append(bank())
+            banks_b.append(bank())
+            product_a(0, t, 0, banks_a[t])
             product_b(0, t, 0, banks_b[t])
         for t in range(PACK):
-            product_a(0, t, 0, banks_a[t])
-        for product, banks in ((product_b, banks_b), (product_a, banks_a)):
-            for t in range(PACK):
-                product(0, t, 1, banks[t])
+            product_b(0, t, 1, banks_b[t])
+            product_a(0, t, 1, banks_a[t])
         for t in range(PACK):
             gate_times_b(0, t, banks_a[t], banks_b[t])
+            if t == 2:
+                round_first_c(nc.scalar.copy, 1, 0)
 
         nc.gpsimd.tensor_scalar(fence[:, : 2 * pair_width].rearrange("p (t m i) -> p m t i", t=PACK, i=PACK),
-                                w_raw["c", 0][:].rearrange("p i (m t) -> p m t i", t=PACK), 1.0, 0.0, ALU.mult, ALU.add)
-        late = sb([P, 2 * pair_width], BF16, "late", tag="raw_c0")
+                                w_raw["c", 1][:].rearrange("p i (m t) -> p m t i", t=PACK), 1.0, 0.0, ALU.mult, ALU.add)
 
         for t in range(PACK):
             acc_a, acc_b = bank(), bank()
@@ -244,10 +252,9 @@ def tile_list_octant_voxel_fusion_kernel(tc, xT, wgt, offs, wa, ba, wb_words, wb
                 product_b(1, t, s, acc_b)
             gate_times_b(1, t, acc_a, acc_b)
             if t == 0:
-                round_w(nc.scalar.copy, "c", 1, 1, late[:, pair_width:])
-                round_w(nc.vector.tensor_copy, "c", 1, 0, late[:, :pair_width])
-                quantise_two("c0", ((0, 0), (0, 1)), fence[:, : 2 * pair_width])
-                quantise_two("c1", ((1, 0), (1, 1)), late[:])
+                round_first_c(nc.scalar.copy, 1, 1)
+                quantise_two("c0", ((0, 0), (0, 1)), first_c, tag="raw_c1")
+                quantise_two("c1", ((1, 0), (1, 1)), fence[:])
 
         def product_c(j0):
             half, at = divmod(j0, HALF)

@@ -25,6 +25,7 @@ GROUP = 16
 HALF = 512
 HALVES = S // HALF
 QUARTER = HALF // 2
+SPACED = HALF + QUARTER
 BLOCK = 128
 LINE = 4
 PIECES = (256, 256, 512)
@@ -46,14 +47,15 @@ def tile_list_octant_voxel_fusion_kernel(tc, xT, wgt, offs, wa, ba, wb_words, wb
 
         offsets = keep.tile([P, S // GROUP], U16, name="offsets")
 
+        wb_scales_raw = sb([P, PASSES, H], U8, "wb_scales_raw")
+        nc.vector.memset(wb_scales_raw[:].rearrange("p s e -> p (s e)").bitcast(I32), 0)
+
         warm = sb([P, 8], F32, "warm")
         nc.vector.memset(warm[:, 0:1], 0.0)
         nc.scalar.activation(warm[:, 4:5], warm[:, 0:1], ACT.Sigmoid)
 
         wb_words_raw = sb([P, PASSES, 2 * H], U8, "wb_words_raw")
-        wb_scales_raw = sb([P, PASSES, H], U8, "wb_scales_raw")
         wo_scale = sb([P, N], U8, "wo_scale")
-        nc.vector.memset(wb_scales_raw[:].rearrange("p s e -> p (s e)").bitcast(I32), 0)
         nc.vector.memset(wo_scale[:].bitcast(I32), 0)
         weight = sb([P, S], F32, "weight")
         ba_sb = sb([P, PACK], F32, "ba_sb")
@@ -84,11 +86,8 @@ def tile_list_octant_voxel_fusion_kernel(tc, xT, wgt, offs, wa, ba, wb_words, wb
                 nc.sync.dma_start(planes[s, i][:], x_rows[s, i])
         load_weight("a", wa, 1)
         nc.sync.dma_start(ba_sb[:], ba.rearrange("(p t) -> p t", t=PACK))
-        c_half = []
-        for u in range(2):
-            c_half.append(sb([P, PACK, H // 2], F32, f"raw_c0{u}"))
-            nc.sync.dma_start(c_half[u][:], wc[:K_PASS, u * H // 2 : (u + 1) * H // 2].rearrange("(p i) c -> p i c", i=PACK))
-        load_weight("c", wc, 1)
+        for s in range(PASSES):
+            load_weight("c", wc, s)
         nc.sync.dma_start(wo_code[:].bitcast(I32), wo_words[0].rearrange("p e i -> p (e i)").bitcast(I32))
         for q in range(4):
             nc.sync.dma_start(wo_scale[32 * q : 32 * q + 4, :].bitcast(I32), wo_scales[0, 4 * q : 4 * q + 4, :].bitcast(I32))
@@ -114,7 +113,7 @@ def tile_list_octant_voxel_fusion_kernel(tc, xT, wgt, offs, wa, ba, wb_words, wb
             for c in range(count):
                 nc.tensor.transpose(back[:, c * P : (c + 1) * P], repeated[:, c, :], ident[:])
             nc.scalar.copy(weight[:, j0 : j0 + width], back[:, :width])
-            if j0 == QUARTER:
+            if j0 == 0:
                 weight_piece[j0] = sb([P, width], F32, f"weight_piece{j0}")
                 nc.scalar.copy(weight_piece[j0][:], back[:, :width])
 
@@ -129,7 +128,8 @@ def tile_list_octant_voxel_fusion_kernel(tc, xT, wgt, offs, wa, ba, wb_words, wb
         x_code, x_scale, w_code, w_scale, w_round = {}, {}, {}, {}, {}
         pair_width = 2 * P * PACK
 
-        gated = [sb([P, PACK * HALF], F32, f"gated{half}") for half in range(HALVES)]
+        row = sb([P, PACK * SPACED], F32, "row")
+        gated = [sb([P, PACK, HALF], F32, "gated0")[:], row[:].rearrange("p (t j) -> p t j", t=PACK)[:, :, :HALF]]
 
         def gather(s, i, j0, width, factor=None):
             nc.vector.tensor_tensor(picked[s][:, i * S + j0 : i * S + j0 + width],
@@ -184,8 +184,8 @@ def tile_list_octant_voxel_fusion_kernel(tc, xT, wgt, offs, wa, ba, wb_words, wb
         for half in range(HALVES):
             round_x(0, half * HALF, HALF, rounded0[half])
 
-        fence = sb([P, 2 * pair_width], BF16, "fence")
-        rounded1 = [sb([P, HALF * PACK], BF16, "x_round10")[:], fence[:]]
+        fence = row[:, 2 * SPACED + QUARTER : 3 * SPACED + HALF].bitcast(BF16)
+        rounded1 = [sb([P, HALF * PACK], BF16, "x_round10")[:], row[:, SPACED + HALF : 3 * SPACED].bitcast(BF16)]
         for i in range(PACK - 1):
             gather(1, i, 0, S)
             if i < HALVES:
@@ -194,9 +194,9 @@ def tile_list_octant_voxel_fusion_kernel(tc, xT, wgt, offs, wa, ba, wb_words, wb
             round_w(nc.scalar.copy, "a", 0, pair)
         quantise_w("a", 0, 0)
         for j0, width in zip(starts, PIECES):
-            gather(1, PACK - 1, j0, width, weight_piece[j0][:] if j0 == QUARTER else None)
+            gather(1, PACK - 1, j0, width, weight_piece[j0][:] if j0 == 0 else None)
             if j0 == QUARTER:
-                quantise_w("a", 0, 1, tag=f"weight_piece{j0}")
+                quantise_w("a", 0, 1, tag="weight_piece0")
             half, at = divmod(j0, HALF)
             round_x(1, j0, width, rounded1[half][:, at * PACK : (at + width) * PACK])
 
@@ -204,26 +204,29 @@ def tile_list_octant_voxel_fusion_kernel(tc, xT, wgt, offs, wa, ba, wb_words, wb
         quantise_x(1, 0, HALF, rounded1[0])
         quantise_w("a", 1, 0)
         round_w(nc.vector.tensor_copy, "a", 1, 1)
-        first_c = gated[1][:, HALF : 3 * HALF].bitcast(BF16)
+        first_c = row[:, SPACED : 2 * SPACED + QUARTER].bitcast(BF16)
 
-        def round_first_c(copy, u, pair):
-            copy(first_c.rearrange("p (t m i) -> p m i t", t=PACK, i=PACK)[:, u * P // 2 : (u + 1) * P // 2, :, 2 * pair : 2 * pair + 2],
-                 c_half[u][:].rearrange("p i (m t) -> p m i t", t=PACK)[:, :, :, 2 * pair : 2 * pair + 2])
+        def round_second_pair(copy, u):
+            columns = slice(u * P // 2, (u + 1) * P // 2)
+            copy(first_c[:, pair_width:].rearrange("p (t m i) -> p m i t", t=2, i=PACK)[:, columns],
+                 w_raw["c", 0][:].rearrange("p i (m t) -> p m i t", t=PACK)[:, columns, :, 2:])
 
-        for pair in range(2):
-            round_first_c(nc.vector.tensor_copy, 0, pair)
+        def one_port_copy(dst, src):
+            nc.vector.tensor_reduce(dst, src.unsqueeze(4), mybir.AxisListType.X, ALU.max)
+
+        round_w(nc.vector.tensor_copy, "c", 0, 0, first_c[:, :pair_width])
         quantise_w("a", 1, 1)
-        quantise_x(1, HALF, HALF, rounded1[1], tag="raw_c00")
+        quantise_x(1, HALF, HALF, rounded1[1])
 
         def gate_times_b(half, t, acc_a, acc_b):
             gate = scratch([P, HALF], "gate")
             nc.scalar.activation(gate[:], acc_a[:], ACT.Sigmoid, bias=ba_sb[:, t : t + 1])
             mine = HALF if half == 0 or t < PACK - 2 else (HALF // 2 if t == PACK - 2 else 0)
-            dst = gated[half][:, t * HALF : (t + 1) * HALF]
+            dst = gated[half][:, t, :]
             if mine:
                 nc.vector.tensor_tensor(dst[:, :mine], acc_b[:, :mine], gate[:, :mine], ALU.mult)
             if mine < HALF:
-                b_copy = sb([P, HALF - mine], F32, f"b_copy{t}", tag="fence" if mine else None)
+                b_copy = sb([P, HALF - mine], F32, f"b_copy{t}")
                 nc.scalar.copy(b_copy[:], acc_b[:, mine:])
                 nc.gpsimd.tensor_tensor(dst[:, mine:], b_copy[:], gate[:, mine:], ALU.mult)
 
@@ -238,10 +241,9 @@ def tile_list_octant_voxel_fusion_kernel(tc, xT, wgt, offs, wa, ba, wb_words, wb
             product_a(0, t, 1, banks_a[t])
         for t in range(PACK):
             gate_times_b(0, t, banks_a[t], banks_b[t])
-            if t == 2:
-                round_first_c(nc.scalar.copy, 1, 0)
+        round_second_pair(one_port_copy, 0)
 
-        nc.gpsimd.tensor_scalar(fence[:, : 2 * pair_width].rearrange("p (t m i) -> p m t i", t=PACK, i=PACK),
+        nc.gpsimd.tensor_scalar(fence.rearrange("p (t m i) -> p m t i", t=PACK, i=PACK),
                                 w_raw["c", 1][:].rearrange("p i (m t) -> p m t i", t=PACK), 1.0, 0.0, ALU.mult, ALU.add)
 
         for t in range(PACK):
@@ -252,9 +254,9 @@ def tile_list_octant_voxel_fusion_kernel(tc, xT, wgt, offs, wa, ba, wb_words, wb
                 product_b(1, t, s, acc_b)
             gate_times_b(1, t, acc_a, acc_b)
             if t == 0:
-                round_first_c(nc.scalar.copy, 1, 1)
+                round_second_pair(nc.scalar.copy, 1)
                 quantise_two("c0", ((0, 0), (0, 1)), first_c, tag="raw_c1")
-                quantise_two("c1", ((1, 0), (1, 1)), fence[:])
+                quantise_two("c1", ((1, 0), (1, 1)), fence)
 
         def product_c(j0):
             half, at = divmod(j0, HALF)
@@ -269,7 +271,7 @@ def tile_list_octant_voxel_fusion_kernel(tc, xT, wgt, offs, wa, ba, wb_words, wb
         def add_c(j0, acc, dst):
             half, at = divmod(j0, HALF)
             nc.vector.tensor_tensor(dst.rearrange("p (c l t) -> p c t l", l=LINE, t=PACK), acc[:].rearrange("p (t c l) -> p c t l", l=LINE, t=PACK),
-                                    gated[half][:].rearrange("p (t j) -> p t j", t=PACK)[:, :, at : at + BLOCK].rearrange("p t (c l) -> p c t l", l=LINE), ALU.add)
+                                    gated[half][:, :, at : at + BLOCK].rearrange("p t (c l) -> p c t l", l=LINE), ALU.add)
 
         def quantise_h(j0, width, h_round):
             if j0 == 0:
@@ -288,7 +290,10 @@ def tile_list_octant_voxel_fusion_kernel(tc, xT, wgt, offs, wa, ba, wb_words, wb
                 nc.tensor.matmul_mx(accs[u], lhsT=wo_code[:, PACK * u * P : PACK * (u + 1) * P].bitcast(FP8X4),
                                     lhsT_scale=wo_scale[:, u * P : (u + 1) * P], rhs=h_code[:].bitcast(FP8X4), rhs_scale=h_scale[:],
                                     start=True, stop=True)
-            for u in range(N // P):
+            if j0 + width == S:
+                nc.vector.tensor_tensor(result[:], acc[:, : 2 * width].rearrange("p (u j) -> p u j", u=N // P),
+                                        bo_sb[:].unsqueeze(2).to_broadcast([P, N // P, width]), ALU.add)
+            for u in range(N // P if j0 + width < S else 0):
                 nc.scalar.activation(result[:, u, :], accs[u], ACT.Identity, bias=bo_sb[:, u : u + 1])
                 if width == HALF:
                     nc.sync.dma_start(out[u * P : (u + 1) * P, j0 : j0 + width], result[:, u, :])

@@ -26,6 +26,7 @@ HALF = 512
 HALVES = S // HALF
 QUARTER = HALF // 2
 SPACED = HALF + QUARTER
+POOL_COLUMNS = 112
 BLOCK = 128
 LINE = 4
 PIECES = (256, 256, 512)
@@ -243,8 +244,8 @@ def tile_list_octant_voxel_fusion_kernel(tc, xT, wgt, offs, wa, ba, wb_words, wb
             gate_times_b(0, t, banks_a[t], banks_b[t])
         round_second_pair(one_port_copy, 0)
 
-        nc.gpsimd.tensor_scalar(fence.rearrange("p (t m i) -> p m t i", t=PACK, i=PACK),
-                                w_raw["c", 1][:].rearrange("p i (m t) -> p m t i", t=PACK), 1.0, 0.0, ALU.mult, ALU.add)
+        nc.gpsimd.tensor_scalar(fence.rearrange("p (t m i) -> p m t i", t=PACK, i=PACK)[:, :POOL_COLUMNS],
+                                w_raw["c", 1][:].rearrange("p i (m t) -> p m t i", t=PACK)[:, :POOL_COLUMNS], 1.0, 0.0, ALU.mult, ALU.add)
 
         for t in range(PACK):
             acc_a, acc_b = bank(), bank()
@@ -255,6 +256,8 @@ def tile_list_octant_voxel_fusion_kernel(tc, xT, wgt, offs, wa, ba, wb_words, wb
             gate_times_b(1, t, acc_a, acc_b)
             if t == 0:
                 round_second_pair(nc.scalar.copy, 1)
+                nc.scalar.copy(fence.rearrange("p (t m i) -> p m i t", t=PACK, i=PACK)[:, POOL_COLUMNS:],
+                               w_raw["c", 1][:].rearrange("p i (m t) -> p m i t", t=PACK)[:, POOL_COLUMNS:])
                 quantise_two("c0", ((0, 0), (0, 1)), first_c, tag="raw_c1")
                 quantise_two("c1", ((1, 0), (1, 1)), fence)
 

@@ -75,16 +75,16 @@ def tile_list_octant_voxel_fusion_kernel(tc, xT, wgt, offs, wa, ba, wb_words, wb
 
         nc.sync.dma_start(two_rows[:], wgt.rearrange("(u r) (c j) -> u (r c) j", r=GROUP // 2, j=P)[:, 0 : S // P, :])
         nc.sync.dma_start(offsets[:], offs)
-        nc.sync.dma_start(wb_words_raw[:].bitcast(I32), wb_words.rearrange("s p e -> p s e").bitcast(I32))
-        for q in range(4):
-            nc.sync.dma_start(wb_scales_raw[32 * q : 32 * q + 4, :, :].bitcast(I32),
-                              wb_scales[:, 4 * q : 4 * q + 4, :].rearrange("s r e -> r s e").bitcast(I32))
+        staged = sb([4, PASSES * 4, H], U8, "staged")
+        nc.sync.dma_start(staged[:].bitcast(I32), wb_scales.rearrange("s (q r) e -> r (s q) e", r=4).bitcast(I32))
         for s in range(PASSES):
             for i in range(PACK):
                 if (s, i) == (PASSES - 1, PACK - 1):
                     load_weight("a", wa, 0)
                 planes[s, i] = sb([P, T], F32, f"plane{s}{i}")
                 nc.sync.dma_start(planes[s, i][:], x_rows[s, i])
+                if (s, i) == (0, 0):
+                    nc.sync.dma_start(wb_words_raw[:].bitcast(I32), wb_words.rearrange("s p e -> p s e").bitcast(I32))
         load_weight("a", wa, 1)
         nc.sync.dma_start(ba_sb[:], ba.rearrange("(p t) -> p t", t=PACK))
         for s in range(PASSES):
@@ -107,7 +107,8 @@ def tile_list_octant_voxel_fusion_kernel(tc, xT, wgt, offs, wa, ba, wb_words, wb
         by_run = by_column[:, :P].rearrange("j (g d c) -> j c g d", d=2, c=runs)
         for j0, width in zip(starts, PIECES):
             first, count = j0 // P, width // P
-            repeated = scratch([P, count, P], f"repeated{first}")
+            last = j0 + width == S
+            repeated = sb([P, count, P], F32, "repeated_last") if last else scratch([P, count, P], f"repeated{first}")
             nc.scalar.copy(repeated[:].rearrange("j c (g d e) -> j c g d e", d=2, e=GROUP // 2),
                            by_run[:, first : first + count, :, :].unsqueeze(4).to_broadcast([P, count, P // GROUP, 2, GROUP // 2]))
             back = bank()
@@ -118,10 +119,13 @@ def tile_list_octant_voxel_fusion_kernel(tc, xT, wgt, offs, wa, ba, wb_words, wb
                 weight_piece[j0] = sb([P, width], F32, f"weight_piece{j0}")
                 nc.scalar.copy(weight_piece[j0][:], back[:, :width])
 
-        wb_code = sb([P, PASSES, 2 * H], U8, "wb_code")
+        wb_code = sb([P, PASSES, 2 * H], U8, "wb_code", tag="repeated_last")
         wb_scale = sb([P, PASSES, H], U8, "wb_scale")
-        nc.vector.tensor_copy(wb_code[:].bitcast(U16).rearrange("p s (t m) -> p s t m", t=PACK),
-                              wb_words_raw[:].bitcast(U16).rearrange("p s (m t) -> p s t m", t=PACK))
+        nc.scalar.copy(wb_code[:].bitcast(U16).rearrange("p s (t m) -> p s m t", t=PACK),
+                       wb_words_raw[:].bitcast(U16).rearrange("p s (m t) -> p s m t", t=PACK))
+        for q in range(4):
+            nc.vector.tensor_copy(wb_scales_raw[32 * q : 32 * q + 4, :, :].bitcast(I32),
+                                  staged[:].rearrange("r (s q) e -> r s q e", q=4)[:, :, q, :].bitcast(I32))
         nc.vector.tensor_copy(wb_scale[:].rearrange("p s (t m) -> p s t m", t=PACK),
                               wb_scales_raw[:].rearrange("p s (m t) -> p s t m", t=PACK))
 

@@ -29,6 +29,7 @@ SPACED = HALF + QUARTER
 POOL_COLUMNS = 112
 BLOCK = 128
 LINE = 4
+PAIR = 2
 PIECES = (256, 256, 512)
 STORES = (512, 256, 128, 128)
 C_AHEAD = 4
@@ -142,8 +143,8 @@ def tile_list_octant_voxel_fusion_kernel(tc, xT, wgt, offs, wa, ba, wb_words, wb
                                     weight[:, j0 : j0 + width] if factor is None else factor, ALU.mult)
 
         def round_x(s, j0, width, dst):
-            nc.scalar.copy(dst.rearrange("p (c l i) -> p c i l", l=LINE, i=PACK),
-                           picked[s][:].rearrange("p (i j) -> p i j", i=PACK)[:, :, j0 : j0 + width].rearrange("p i (c l) -> p c i l", l=LINE))
+            nc.scalar.copy(dst.rearrange("p (c l i) -> p c i l", l=PAIR, i=PACK),
+                           picked[s][:].rearrange("p (i j) -> p i j", i=PACK)[:, :, j0 : j0 + width].rearrange("p i (c l) -> p c i l", l=PAIR))
 
         def quantise_x(s, j0, width, x_round, tag=None):
             half, at = divmod(j0, HALF)

@@ -28,7 +28,6 @@ QUARTER = HALF // 2
 SPACED = HALF + QUARTER
 POOL_COLUMNS = 112
 BLOCK = 128
-LINE = 4
 PAIR = 2
 PIECES = (256, 256, 512)
 STORES = (512, 256, 128, 128)
@@ -99,7 +98,7 @@ def tile_list_octant_voxel_fusion_kernel(tc, xT, wgt, offs, wa, ba, wb_words, wb
         starts = [sum(PIECES[:n]) for n in range(len(PIECES))]
 
         def scratch(shape, name):
-            return sb(shape, F32, name, tag="scratch", bufs=3)
+            return sb(shape, F32, name, tag="scratch", bufs=2)
 
         runs = S // P
         weight_piece = {}
@@ -225,7 +224,7 @@ def tile_list_octant_voxel_fusion_kernel(tc, xT, wgt, offs, wa, ba, wb_words, wb
         quantise_x(1, HALF, HALF, rounded1[1])
 
         def gate_times_b(half, t, acc_a, acc_b):
-            gate = scratch([P, HALF], "gate")
+            gate = sb([P, HALF], F32, f"gate{half}{t}", tag=f"plane{half}{t}")
             nc.scalar.activation(gate[:], acc_a[:], ACT.Sigmoid, bias=ba_sb[:, t : t + 1])
             mine = HALF if half == 0 or t < PACK - 2 else (HALF // 2 if t == PACK - 2 else 0)
             dst = gated[half][:, t, :]
@@ -278,8 +277,8 @@ def tile_list_octant_voxel_fusion_kernel(tc, xT, wgt, offs, wa, ba, wb_words, wb
 
         def add_c(j0, acc, dst):
             half, at = divmod(j0, HALF)
-            nc.vector.tensor_tensor(dst.rearrange("p (c l t) -> p c t l", l=LINE, t=PACK), acc[:].rearrange("p (t c l) -> p c t l", l=LINE, t=PACK),
-                                    gated[half][:, :, at : at + BLOCK].rearrange("p t (c l) -> p c t l", l=LINE), ALU.add)
+            nc.vector.tensor_tensor(dst.rearrange("p (c l t) -> p c t l", l=PAIR, t=PACK), acc[:].rearrange("p (t c l) -> p c t l", l=PAIR, t=PACK),
+                                    gated[half][:, :, at : at + BLOCK].rearrange("p t (c l) -> p c t l", l=PAIR), ALU.add)
 
         def quantise_h(j0, width, h_round):
             if j0 == 0:

@@ -190,7 +190,7 @@ def tile_list_octant_voxel_fusion_kernel(tc, xT, wgt, offs, wa, ba, wb_words, wb
             round_x(0, half * HALF, HALF, rounded0[half])
 
         fence = row[:, 2 * SPACED + QUARTER : 3 * SPACED + HALF].bitcast(BF16)
-        rounded1 = [sb([P, HALF * PACK], BF16, "x_round10")[:], row[:, SPACED + HALF : 3 * SPACED].bitcast(BF16)]
+        rounded1 = [sb([P, HALF * PACK], BF16, "x_round10")[:], fence]
         for i in range(PACK - 1):
             gather(1, i, 0, S)
             if i < HALVES:
@@ -211,42 +211,35 @@ def tile_list_octant_voxel_fusion_kernel(tc, xT, wgt, offs, wa, ba, wb_words, wb
         round_w(nc.vector.tensor_copy, "a", 1, 1)
         first_c = row[:, SPACED : 2 * SPACED + QUARTER].bitcast(BF16)
 
-        def round_second_pair(copy, u):
-            columns = slice(u * P // 2, (u + 1) * P // 2)
-            copy(first_c[:, pair_width:].rearrange("p (t m i) -> p m i t", t=2, i=PACK)[:, columns],
-                 w_raw["c", 0][:].rearrange("p i (m t) -> p m i t", t=PACK)[:, columns, :, 2:])
-
-        def one_port_copy(dst, src):
-            nc.vector.tensor_reduce(dst, src.unsqueeze(4), mybir.AxisListType.X, ALU.max)
-
         round_w(nc.vector.tensor_copy, "c", 0, 0, first_c[:, :pair_width])
         quantise_w("a", 1, 1)
         quantise_x(1, HALF, HALF, rounded1[1])
 
         def gate_times_b(half, t, acc_a, acc_b):
-            gate = sb([P, HALF], F32, f"gate{half}{t}", tag=f"plane{half}{t}")
-            nc.scalar.activation(gate[:], acc_a[:], ACT.Sigmoid, bias=ba_sb[:, t : t + 1])
+            if (half, t) == (0, 1):
+                gate = row[:, SPACED + HALF : 2 * SPACED + QUARTER]
+            else:
+                gate = sb([P, HALF], F32, f"gate{half}{t}", tag=f"plane{half}{t}")[:]
+            nc.scalar.activation(gate, acc_a[:], ACT.Sigmoid, bias=ba_sb[:, t : t + 1])
             mine = HALF if half == 0 or t < PACK - 2 else (HALF // 2 if t == PACK - 2 else 0)
             dst = gated[half][:, t, :]
-            if mine:
-                nc.vector.tensor_tensor(dst[:, :mine], acc_b[:, :mine], gate[:, :mine], ALU.mult)
             if mine < HALF:
                 b_copy = sb([P, HALF - mine], F32, f"b_copy{t}")
                 nc.scalar.copy(b_copy[:], acc_b[:, mine:])
                 nc.gpsimd.tensor_tensor(dst[:, mine:], b_copy[:], gate[:, mine:], ALU.mult)
+            if mine:
+                nc.vector.tensor_tensor(dst[:, :mine], acc_b[:, :mine], gate[:, :mine], ALU.mult)
 
         banks_a, banks_b = [], []
-        for t in range(PACK):
-            banks_a.append(bank())
-            banks_b.append(bank())
-            product_a(0, t, 0, banks_a[t])
-            product_b(0, t, 0, banks_b[t])
+        for banks, product in ((banks_a, product_a), (banks_b, product_b)):
+            for t in range(PACK):
+                banks.append(bank())
+                product(0, t, 0, banks[t])
         for t in range(PACK):
             product_b(0, t, 1, banks_b[t])
             product_a(0, t, 1, banks_a[t])
         for t in range(PACK):
             gate_times_b(0, t, banks_a[t], banks_b[t])
-        round_second_pair(one_port_copy, 0)
 
         nc.gpsimd.tensor_scalar(fence.rearrange("p (t m i) -> p m t i", t=PACK, i=PACK)[:, :POOL_COLUMNS],
                                 w_raw["c", 1][:].rearrange("p i (m t) -> p m t i", t=PACK)[:, :POOL_COLUMNS], 1.0, 0.0, ALU.mult, ALU.add)
@@ -259,7 +252,7 @@ def tile_list_octant_voxel_fusion_kernel(tc, xT, wgt, offs, wa, ba, wb_words, wb
                 product_b(1, t, s, acc_b)
             gate_times_b(1, t, acc_a, acc_b)
             if t == 0:
-                round_second_pair(nc.scalar.copy, 1)
+                round_w(nc.scalar.copy, "c", 0, 1, first_c[:, pair_width:])
                 nc.scalar.copy(fence.rearrange("p (t m i) -> p m i t", t=PACK, i=PACK)[:, POOL_COLUMNS:],
                                w_raw["c", 1][:].rearrange("p i (m t) -> p m i t", t=PACK)[:, POOL_COLUMNS:])
                 quantise_two("c0", ((0, 0), (0, 1)), first_c, tag="raw_c1")

@@ -177,10 +177,11 @@ def tile_list_octant_voxel_fusion_kernel(tc, xT, wgt, offs, wa, ba, wb_words, wb
             nc.tensor.matmul_mx(acc[:], **row_set("a", s, t), rhs=x_code[s, half][:].bitcast(FP8X4), rhs_scale=x_scale[s, half][:],
                                 start=s == 0, stop=s == PASSES - 1)
 
-        def product_b(half, t, s, acc):
-            nc.tensor.matmul_mx(acc[:], lhsT=wb_code[:, s, 2 * t * P : 2 * (t + 1) * P].bitcast(FP4X4),
+        def product_b(half, t, s, acc, at=0, width=HALF):
+            nc.tensor.matmul_mx(acc[:, at : at + width], lhsT=wb_code[:, s, 2 * t * P : 2 * (t + 1) * P].bitcast(FP4X4),
                                 lhsT_scale=wb_scale[:, s, t * P : (t + 1) * P],
-                                rhs=x_code[s, half][:].bitcast(FP8X4), rhs_scale=x_scale[s, half][:], start=s == 0, stop=s == PASSES - 1)
+                                rhs=x_code[s, half][:, at : at + width].bitcast(FP8X4), rhs_scale=x_scale[s, half][:, at : at + width],
+                                start=s == 0, stop=s == PASSES - 1 and at + width == HALF)
 
         rounded0 = [sb([P, HALF * PACK], BF16, f"x_round0{half}")[:] for half in range(HALVES)]
         for i in range(PACK):
@@ -205,8 +206,9 @@ def tile_list_octant_voxel_fusion_kernel(tc, xT, wgt, offs, wa, ba, wb_words, wb
             half, at = divmod(j0, HALF)
             round_x(1, j0, width, rounded1[half][:, at * PACK : (at + width) * PACK])
 
+        quantise_x(1, 0, QUARTER, rounded1[0][:, : QUARTER * PACK])
         round_w(nc.vector.tensor_copy, "a", 1, 0)
-        quantise_x(1, 0, HALF, rounded1[0])
+        quantise_x(1, QUARTER, QUARTER, rounded1[0][:, QUARTER * PACK :])
         quantise_w("a", 1, 0)
         round_w(nc.vector.tensor_copy, "a", 1, 1)
         first_c = row[:, SPACED : 2 * SPACED + QUARTER].bitcast(BF16)
@@ -216,12 +218,12 @@ def tile_list_octant_voxel_fusion_kernel(tc, xT, wgt, offs, wa, ba, wb_words, wb
         quantise_x(1, HALF, HALF, rounded1[1])
 
         def gate_times_b(half, t, acc_a, acc_b):
-            if (half, t) == (0, 1):
+            if (half, t) == (0, 0):
                 gate = row[:, SPACED + HALF : 2 * SPACED + QUARTER]
             else:
                 gate = sb([P, HALF], F32, f"gate{half}{t}", tag=f"plane{half}{t}")[:]
             nc.scalar.activation(gate, acc_a[:], ACT.Sigmoid, bias=ba_sb[:, t : t + 1])
-            mine = HALF if half == 0 or t < PACK - 2 else (HALF // 2 if t == PACK - 2 else 0)
+            mine = HALF if half == 0 or t < PACK - 2 else 0
             dst = gated[half][:, t, :]
             if mine < HALF:
                 b_copy = sb([P, HALF - mine], F32, f"b_copy{t}")
@@ -236,8 +238,12 @@ def tile_list_octant_voxel_fusion_kernel(tc, xT, wgt, offs, wa, ba, wb_words, wb
                 banks.append(bank())
                 product(0, t, 0, banks[t])
         for t in range(PACK):
-            product_b(0, t, 1, banks_b[t])
-            product_a(0, t, 1, banks_a[t])
+            product_b(0, t, 1, banks_b[t], 0, QUARTER)
+        for pair in range(2):
+            for t in (2 * pair, 2 * pair + 1):
+                product_b(0, t, 1, banks_b[t], QUARTER, QUARTER)
+            for t in (2 * pair, 2 * pair + 1):
+                product_a(0, t, 1, banks_a[t])
         for t in range(PACK):
             gate_times_b(0, t, banks_a[t], banks_b[t])
 

@@ -26,7 +26,6 @@ HALF = 512
 HALVES = S // HALF
 QUARTER = HALF // 2
 SPACED = HALF + QUARTER
-POOL_COLUMNS = 112
 BLOCK = 128
 PAIR = 2
 PIECES = (256, 256, 512)
@@ -43,8 +42,11 @@ def tile_list_octant_voxel_fusion_kernel(tc, xT, wgt, offs, wa, ba, wb_words, wb
         def sb(shape, dtype, name, tag=None, bufs=1):
             return keep.tile(shape, dtype, name=name, tag=tag or name, bufs=bufs, align_bytes=64)
 
+        taken = []
+
         def bank():
-            return psum.tile([P, HALF], F32, name="bank", tag="bank", bufs=8)
+            taken.append(psum.tile([P, HALF], F32, name="bank", tag=f"bank{len(taken) % 8}"))
+            return taken[-1]
 
         offsets = keep.tile([P, S // GROUP], U16, name="offsets")
 
@@ -86,9 +88,9 @@ def tile_list_octant_voxel_fusion_kernel(tc, xT, wgt, offs, wa, ba, wb_words, wb
                 if (s, i) == (0, 0):
                     nc.sync.dma_start(wb_words_raw[:].bitcast(I32), wb_words.rearrange("s p e -> p s e").bitcast(I32))
         load_weight("a", wa, 1)
+        load_weight("c", wc, 0)
         nc.sync.dma_start(ba_sb[:], ba.rearrange("(p t) -> p t", t=PACK))
-        for s in range(PASSES):
-            load_weight("c", wc, s)
+        load_weight("c", wc, 1)
         nc.sync.dma_start(wo_code[:].bitcast(I32), wo_words[0].rearrange("p e i -> p (e i)").bitcast(I32))
         for q in range(4):
             nc.sync.dma_start(wo_scale[32 * q : 32 * q + 4, :].bitcast(I32), wo_scales[0, 4 * q : 4 * q + 4, :].bitcast(I32))
@@ -221,9 +223,9 @@ def tile_list_octant_voxel_fusion_kernel(tc, xT, wgt, offs, wa, ba, wb_words, wb
             if (half, t) == (0, 0):
                 gate = row[:, SPACED + HALF : 2 * SPACED + QUARTER]
             else:
-                gate = sb([P, HALF], F32, f"gate{half}{t}", tag=f"plane{half}{t}")[:]
+                gate = sb([P, HALF], F32, f"gate{half}{t}", tag="raw_c0" if (half, t) == (1, 1) else f"plane{half}{t}")[:]
             nc.scalar.activation(gate, acc_a[:], ACT.Sigmoid, bias=ba_sb[:, t : t + 1])
-            mine = HALF if half == 0 or t < PACK - 2 else 0
+            mine = HALF if half == 0 or t < PACK - 2 else (HALF // 2 if t == PACK - 2 else 0)
             dst = gated[half][:, t, :]
             if mine < HALF:
                 b_copy = sb([P, HALF - mine], F32, f"b_copy{t}")
@@ -247,8 +249,8 @@ def tile_list_octant_voxel_fusion_kernel(tc, xT, wgt, offs, wa, ba, wb_words, wb
         for t in range(PACK):
             gate_times_b(0, t, banks_a[t], banks_b[t])
 
-        nc.gpsimd.tensor_scalar(fence.rearrange("p (t m i) -> p m t i", t=PACK, i=PACK)[:, :POOL_COLUMNS],
-                                w_raw["c", 1][:].rearrange("p i (m t) -> p m t i", t=PACK)[:, :POOL_COLUMNS], 1.0, 0.0, ALU.mult, ALU.add)
+        nc.gpsimd.tensor_scalar(fence.rearrange("p (t m i) -> p m t i", t=PACK, i=PACK),
+                                w_raw["c", 1][:].rearrange("p i (m t) -> p m t i", t=PACK), 1.0, 0.0, ALU.mult, ALU.add)
 
         for t in range(PACK):
             acc_a, acc_b = bank(), bank()
@@ -259,8 +261,6 @@ def tile_list_octant_voxel_fusion_kernel(tc, xT, wgt, offs, wa, ba, wb_words, wb
             gate_times_b(1, t, acc_a, acc_b)
             if t == 0:
                 round_w(nc.scalar.copy, "c", 0, 1, first_c[:, pair_width:])
-                nc.scalar.copy(fence.rearrange("p (t m i) -> p m i t", t=PACK, i=PACK)[:, POOL_COLUMNS:],
-                               w_raw["c", 1][:].rearrange("p i (m t) -> p m i t", t=PACK)[:, POOL_COLUMNS:])
                 quantise_two("c0", ((0, 0), (0, 1)), first_c, tag="raw_c1")
                 quantise_two("c1", ((1, 0), (1, 1)), fence)
 

@@ -40,7 +40,7 @@ def tile_list_octant_voxel_fusion_kernel(tc, xT, wgt, offs, wa, ba, wb_words, wb
         psum = ctx.enter_context(tc.psum_pool(name="psum", bufs=1))
 
         def sb(shape, dtype, name, tag=None, bufs=1):
-            return keep.tile(shape, dtype, name=name, tag=tag or name, bufs=bufs, align_bytes=64)
+            return keep.tile(shape, dtype, name=name, tag=tag or name, bufs=bufs, align_bytes=256)
 
         taken = []
 
@@ -225,7 +225,7 @@ def tile_list_octant_voxel_fusion_kernel(tc, xT, wgt, offs, wa, ba, wb_words, wb
             else:
                 gate = sb([P, HALF], F32, f"gate{half}{t}", tag="raw_c0" if (half, t) == (1, 1) else f"plane{half}{t}")[:]
             nc.scalar.activation(gate, acc_a[:], ACT.Sigmoid, bias=ba_sb[:, t : t + 1])
-            mine = HALF if half == 0 or t < PACK - 2 else (HALF // 2 if t == PACK - 2 else 0)
+            mine = HALF if half == 0 or t < PACK - 2 else 0
             dst = gated[half][:, t, :]
             if mine < HALF:
                 b_copy = sb([P, HALF - mine], F32, f"b_copy{t}")
@@ -291,7 +291,7 @@ def tile_list_octant_voxel_fusion_kernel(tc, xT, wgt, offs, wa, ba, wb_words, wb
         def finish(j0, width, h_code, h_scale):
             acc = bank()
             accs = [acc[:, :width], bank()[:] if width == HALF else acc[:, width : 2 * width]]
-            result = sb([P, N // P, width], F32, f"result{j0}")
+            result = sb([P, N // P, width], F32, f"result{j0}", tag=f"raw_a{j0 // HALF}" if j0 % HALF == 0 else None)
             for u in range(N // P):
                 nc.tensor.matmul_mx(accs[u], lhsT=wo_code[:, PACK * u * P : PACK * (u + 1) * P].bitcast(FP8X4),
                                     lhsT_scale=wo_scale[:, u * P : (u + 1) * P], rhs=h_code[:].bitcast(FP8X4), rhs_scale=h_scale[:],

from contextlib import ExitStack

import concourse.mybir as mybir
from concourse.masks import make_identity

K, T, S, H, N = 1024, 2048, 1024, 512, 256
FLOPS = 2 * S * (3 * K * H + H * N)

F32 = mybir.dt.float32
BF16 = mybir.dt.bfloat16
I32 = mybir.dt.int32
U32 = mybir.dt.uint32
U16 = mybir.dt.uint16
U8 = mybir.dt.uint8
FP8X4 = mybir.dt.float8_e4m3fn_x4
FP4X4 = mybir.dt.float4_e2m1fn_x4
ALU = mybir.AluOpType
ACT = mybir.ActivationFunctionType

P = 128
PACK = 4
K_PASS = P * PACK
PASSES = K // K_PASS
GROUP = 16
HALF = 512
HALVES = S // HALF
QUARTER = HALF // 2
SPACED = HALF + QUARTER
BLOCK = 128
PAIR = 2
PIECES = (256, 256, 512)
STORES = (512, 256, 128, 128)
C_AHEAD = 4


def tile_list_octant_voxel_fusion_kernel(tc, xT, wgt, offs, wa, ba, wb_words, wb_scales, wc, wo_words, wo_scales, bo, out):
    nc = tc.nc
    with ExitStack() as ctx:
        keep = ctx.enter_context(tc.tile_pool(name="keep", bufs=1))
        psum = ctx.enter_context(tc.psum_pool(name="psum", bufs=1))

        def sb(shape, dtype, name, tag=None, bufs=1):
            return keep.tile(shape, dtype, name=name, tag=tag or name, bufs=bufs, align_bytes=256)

        taken = []

        def bank():
            taken.append(psum.tile([P, HALF], F32, name="bank", tag=f"bank{len(taken) % 8}"))
            return taken[-1]

        offsets = keep.tile([P, S // GROUP], U16, name="offsets")

        wb_scales_raw = sb([P, PASSES, H], U8, "wb_scales_raw")
        nc.vector.memset(wb_scales_raw[:].rearrange("p s e -> p (s e)").bitcast(I32), 0)

        warm = sb([P, 8], F32, "warm")
        nc.vector.memset(warm[:, 0:1], 0.0)
        nc.scalar.activation(warm[:, 4:5], warm[:, 0:1], ACT.Sigmoid)

        wb_words_raw = sb([P, PASSES, 2 * H], U8, "wb_words_raw")
        wo_scale = sb([P, N], U8, "wo_scale")
        nc.vector.memset(wo_scale[:].bitcast(I32), 0)
        weight = sb([P, S], F32, "weight")
        ba_sb = sb([P, PACK], F32, "ba_sb")
        bo_sb = sb([P, N // P], F32, "bo_sb")
        wo_code = sb([P, PACK * N], U8, "wo_code")
        ident = sb([P, P], F32, "ident")
        make_identity(nc, ident[:])
        two_rows = sb([P, P], F32, "two_rows")

        x_rows = xT.rearrange("(s p i) t -> s i p t", s=PASSES, i=PACK)
        planes, w_raw = {}, {}

        def load_weight(name, w, s):
            w_raw[name, s] = sb([P, PACK, H], F32, f"raw_{name}{s}")
            nc.sync.dma_start(w_raw[name, s][:], w[s * K_PASS : (s + 1) * K_PASS, :].rearrange("(p i) c -> p i c", i=PACK))

        nc.sync.dma_start(two_rows[:], wgt.rearrange("(u r) (c j) -> u (r c) j", r=GROUP // 2, j=P)[:, 0 : S // P, :])
        nc.sync.dma_start(offsets[:], offs)
        staged = sb([4, PASSES * 4, H], U8, "staged")
        nc.sync.dma_start(staged[:].bitcast(I32), wb_scales.rearrange("s (q r) e -> r (s q) e", r=4).bitcast(I32))
        for s in range(PASSES):
            for i in range(PACK):
                if (s, i) == (PASSES - 1, PACK - 1):
                    load_weight("a", wa, 0)
                planes[s, i] = sb([P, T], F32, f"plane{s}{i}")
                nc.sync.dma_start(planes[s, i][:], x_rows[s, i])
                if (s, i) == (0, 0):
                    nc.sync.dma_start(wb_words_raw[:].bitcast(I32), wb_words.rearrange("s p e -> p s e").bitcast(I32))
        load_weight("a", wa, 1)
        load_weight("c", wc, 0)
        nc.sync.dma_start(ba_sb[:], ba.rearrange("(p t) -> p t", t=PACK))
        load_weight("c", wc, 1)
        nc.sync.dma_start(wo_code[:].bitcast(I32), wo_words[0].rearrange("p e i -> p (e i)").bitcast(I32))
        for q in range(4):
            nc.sync.dma_start(wo_scale[32 * q : 32 * q + 4, :].bitcast(I32), wo_scales[0, 4 * q : 4 * q + 4, :].bitcast(I32))
        with nc.allow_non_contiguous_dma(reason="one bias value a partition"):
            nc.sync.dma_start(bo_sb[:], bo.rearrange("(u p) -> p u", p=P))

        starts = [sum(PIECES[:n]) for n in range(len(PIECES))]

        def scratch(shape, name):
            return sb(shape, F32, name, tag="scratch", bufs=2)

        runs = S // P
        weight_piece = {}
        by_column = bank()
        nc.tensor.transpose(by_column[:, :P], two_rows[:], ident[:])
        by_run = by_column[:, :P].rearrange("j (g d c) -> j c g d", d=2, c=runs)
        for j0, width in zip(starts, PIECES):
            first, count = j0 // P, width // P
            last = j0 + width == S
            repeated = sb([P, count, P], F32, "repeated_last") if last else scratch([P, count, P], f"repeated{first}")
            nc.scalar.copy(repeated[:].rearrange("j c (g d e) -> j c g d e", d=2, e=GROUP // 2),
                           by_run[:, first : first + count, :, :].unsqueeze(4).to_broadcast([P, count, P // GROUP, 2, GROUP // 2]))
            back = bank()
            for c in range(count):
                nc.tensor.transpose(back[:, c * P : (c + 1) * P], repeated[:, c, :], ident[:])
            nc.scalar.copy(weight[:, j0 : j0 + width], back[:, :width])
            if j0 == 0:
                weight_piece[j0] = sb([P, width], F32, f"weight_piece{j0}")
                nc.scalar.copy(weight_piece[j0][:], back[:, :width])

        wb_code = sb([P, PASSES, 2 * H], U8, "wb_code", tag="repeated_last")
        wb_scale = sb([P, PASSES, H], U8, "wb_scale")
        nc.scalar.copy(wb_code[:].bitcast(U16).rearrange("p s (t m) -> p s m t", t=PACK),
                       wb_words_raw[:].bitcast(U16).rearrange("p s (m t) -> p s m t", t=PACK))
        for q in range(4):
            nc.vector.tensor_copy(wb_scales_raw[32 * q : 32 * q + 4, :, :].bitcast(I32),
                                  staged[:].rearrange("r (s q) e -> r s q e", q=4)[:, :, q, :].bitcast(I32))
        nc.vector.tensor_copy(wb_scale[:].rearrange("p s (t m) -> p s t m", t=PACK),
                              wb_scales_raw[:].rearrange("p s (m t) -> p s t m", t=PACK))

        picked = [sb([P, PACK * S], F32, f"picked{s}") for s in range(PASSES)]
        x_code, x_scale, w_code, w_scale, w_round = {}, {}, {}, {}, {}
        pair_width = 2 * P * PACK

        row = sb([P, PACK * SPACED], F32, "row")
        gated = [sb([P, PACK, HALF], F32, "gated0")[:], row[:].rearrange("p (t j) -> p t j", t=PACK)[:, :, :HALF]]

        def gather(s, i, j0, width, factor=None):
            nc.vector.tensor_tensor(picked[s][:, i * S + j0 : i * S + j0 + width],
                                    planes[s, i][:].indirect(offsets[:, j0 // GROUP : (j0 + width) // GROUP]),
                                    weight[:, j0 : j0 + width] if factor is None else factor, ALU.mult)

        def round_x(s, j0, width, dst):
            nc.scalar.copy(dst.rearrange("p (c l i) -> p c i l", l=PAIR, i=PACK),
                           picked[s][:].rearrange("p (i j) -> p i j", i=PACK)[:, :, j0 : j0 + width].rearrange("p i (c l) -> p c i l", l=PAIR))

        def quantise_x(s, j0, width, x_round, tag=None):
            half, at = divmod(j0, HALF)
            if at == 0:
                x_code[s, half] = sb([P, HALF], U32, f"x_code{s}{half}", tag=tag)
                x_scale[s, half] = sb([P, HALF], U8, f"x_scale{s}{half}")
            nc.vector.quantize_mx(x_code[s, half][:, at : at + width].bitcast(FP8X4), x_scale[s, half][:, at : at + width], x_round)

        def round_w(copy, name, s, pair, dst=None):
            w_round[name, s, pair] = sb([P, pair_width], BF16, f"w_round{name}{s}{pair}")[:] if dst is None else dst
            copy(w_round[name, s, pair].rearrange("p (t m i) -> p m i t", t=2, i=PACK),
                 w_raw[name, s][:].rearrange("p i (m t) -> p m i t", t=PACK)[:, :, :, 2 * pair : 2 * pair + 2])

        def quantise_w(name, s, pair, tag=None):
            w_code[name, s, pair] = sb([P, 2 * P], U32, f"w_code{name}{s}{pair}", tag=tag)[:]
            w_scale[name, s, pair] = sb([P, 2 * P], U8, f"w_scale{name}{s}{pair}")[:]
            nc.vector.quantize_mx(w_code[name, s, pair].bitcast(FP8X4), w_scale[name, s, pair], w_round[name, s, pair])

        def quantise_two(name, both, rounded, tag=None):
            code, scale = sb([P, H], U32, f"w_code{name}", tag=tag), sb([P, H], U8, f"w_scale{name}")
            for n, (s, pair) in enumerate(both):
                w_code[name[0], s, pair] = code[:, n * 2 * P : (n + 1) * 2 * P]
                w_scale[name[0], s, pair] = scale[:, n * 2 * P : (n + 1) * 2 * P]
            nc.vector.quantize_mx(code[:].bitcast(FP8X4), scale[:], rounded)

        def row_set(name, s, t):
            cols = slice(t % 2 * P, (t % 2 + 1) * P)
            return dict(lhsT=w_code[name, s, t // 2][:, cols].bitcast(FP8X4), lhsT_scale=w_scale[name, s, t // 2][:, cols])

        def product_a(half, t, s, acc):
            nc.tensor.matmul_mx(acc[:], **row_set("a", s, t), rhs=x_code[s, half][:].bitcast(FP8X4), rhs_scale=x_scale[s, half][:],
                                start=s == 0, stop=s == PASSES - 1)

        def product_b(half, t, s, acc, at=0, width=HALF):
            nc.tensor.matmul_mx(acc[:, at : at + width], lhsT=wb_code[:, s, 2 * t * P : 2 * (t + 1) * P].bitcast(FP4X4),
                                lhsT_scale=wb_scale[:, s, t * P : (t + 1) * P],
                                rhs=x_code[s, half][:, at : at + width].bitcast(FP8X4), rhs_scale=x_scale[s, half][:, at : at + width],
                                start=s == 0, stop=s == PASSES - 1 and at + width == HALF)

        rounded0 = [sb([P, HALF * PACK], BF16, f"x_round0{half}")[:] for half in range(HALVES)]
        for i in range(PACK):
            for j0, width in zip(starts, PIECES) if i == 0 else [(0, S)]:
                gather(0, i, j0, width)
        for half in range(HALVES):
            round_x(0, half * HALF, HALF, rounded0[half])

        fence = row[:, 2 * SPACED + QUARTER : 3 * SPACED + HALF].bitcast(BF16)
        rounded1 = [sb([P, HALF * PACK], BF16, "x_round10")[:], fence]
        for i in range(PACK - 1):
            gather(1, i, 0, S)
            if i < HALVES:
                quantise_x(0, i * HALF, HALF, rounded0[i])
        for pair in range(2):
            round_w(nc.scalar.copy, "a", 0, pair)
        quantise_w("a", 0, 0)
        for j0, width in zip(starts, PIECES):
            gather(1, PACK - 1, j0, width, weight_piece[j0][:] if j0 == 0 else None)
            if j0 == QUARTER:
                quantise_w("a", 0, 1, tag="weight_piece0")
            half, at = divmod(j0, HALF)
            round_x(1, j0, width, rounded1[half][:, at * PACK : (at + width) * PACK])

        quantise_x(1, 0, QUARTER, rounded1[0][:, : QUARTER * PACK])
        round_w(nc.vector.tensor_copy, "a", 1, 0)
        quantise_x(1, QUARTER, QUARTER, rounded1[0][:, QUARTER * PACK :])
        quantise_w("a", 1, 0)
        round_w(nc.vector.tensor_copy, "a", 1, 1)
        first_c = row[:, SPACED : 2 * SPACED + QUARTER].bitcast(BF16)

        round_w(nc.vector.tensor_copy, "c", 0, 0, first_c[:, :pair_width])
        quantise_w("a", 1, 1)
        quantise_x(1, HALF, HALF, rounded1[1])

        def gate_times_b(half, t, acc_a, acc_b):
            if (half, t) == (0, 0):
                gate = row[:, SPACED + HALF : 2 * SPACED + QUARTER]
            else:
                gate = sb([P, HALF], F32, f"gate{half}{t}", tag="raw_c0" if (half, t) == (1, 1) else f"plane{half}{t}")[:]
            nc.scalar.activation(gate, acc_a[:], ACT.Sigmoid, bias=ba_sb[:, t : t + 1])
            mine = HALF if half == 0 or t < PACK - 2 else 0
            dst = gated[half][:, t, :]
            if mine < HALF:
                b_copy = sb([P, HALF - mine], F32, f"b_copy{t}")
                nc.scalar.copy(b_copy[:], acc_b[:, mine:])
                nc.gpsimd.tensor_tensor(dst[:, mine:], b_copy[:], gate[:, mine:], ALU.mult)
            if mine:
                nc.vector.tensor_tensor(dst[:, :mine], acc_b[:, :mine], gate[:, :mine], ALU.mult)

        banks_a, banks_b = [], []
        for banks, product in ((banks_a, product_a), (banks_b, product_b)):
            for t in range(PACK):
                banks.append(bank())
                product(0, t, 0, banks[t])
        for t in range(PACK):
            product_b(0, t, 1, banks_b[t], 0, QUARTER)
        for pair in range(2):
            for t in (2 * pair, 2 * pair + 1):
                product_b(0, t, 1, banks_b[t], QUARTER, QUARTER)
            for t in (2 * pair, 2 * pair + 1):
                product_a(0, t, 1, banks_a[t])
        for t in range(PACK):
            gate_times_b(0, t, banks_a[t], banks_b[t])

        nc.gpsimd.tensor_scalar(fence.rearrange("p (t m i) -> p m t i", t=PACK, i=PACK),
                                w_raw["c", 1][:].rearrange("p i (m t) -> p m t i", t=PACK), 1.0, 0.0, ALU.mult, ALU.add)

        for t in range(PACK):
            acc_a, acc_b = bank(), bank()
            for s in range(PASSES):
                product_a(1, t, s, acc_a)
            for s in range(PASSES):
                product_b(1, t, s, acc_b)
            gate_times_b(1, t, acc_a, acc_b)
            if t == 0:
                round_w(nc.scalar.copy, "c", 0, 1, first_c[:, pair_width:])
                quantise_two("c0", ((0, 0), (0, 1)), first_c, tag="raw_c1")
                quantise_two("c1", ((1, 0), (1, 1)), fence)

        def product_c(j0):
            half, at = divmod(j0, HALF)
            acc = bank()
            for s in range(PASSES):
                for t in range(PACK):
                    nc.tensor.matmul_mx(acc[:, t * P : (t + 1) * P], **row_set("c", s, t),
                                        rhs=x_code[s, half][:, at : at + BLOCK].bitcast(FP8X4), rhs_scale=x_scale[s, half][:, at : at + BLOCK],
                                        start=(s, t) == (0, 0), stop=(s, t) == (PASSES - 1, PACK - 1))
            return acc

        def add_c(j0, acc, dst):
            half, at = divmod(j0, HALF)
            nc.vector.tensor_tensor(dst.rearrange("p (c l t) -> p c t l", l=PAIR, t=PACK), acc[:].rearrange("p (t c l) -> p c t l", l=PAIR, t=PACK),
                                    gated[half][:, :, at : at + BLOCK].rearrange("p t (c l) -> p c t l", l=PAIR), ALU.add)

        def quantise_h(j0, width, h_round):
            if j0 == 0:
                h_code = sb([P, width], U32, "h_code_first", tag=f"b_copy{PACK - 1}")
            else:
                h_code = sb([P, width], U32, "h_code", bufs=3)
            h_scale = sb([P, width], U8, "h_scale", bufs=3)
            nc.vector.quantize_mx(h_code[:].bitcast(FP8X4), h_scale[:], h_round[:])
            return h_code, h_scale

        def finish(j0, width, h_code, h_scale):
            acc = bank()
            accs = [acc[:, :width], bank()[:] if width == HALF else acc[:, width : 2 * width]]
            result = sb([P, N // P, width], F32, f"result{j0}", tag=f"raw_a{j0 // HALF}" if j0 % HALF == 0 else None)
            for u in range(N // P):
                nc.tensor.matmul_mx(accs[u], lhsT=wo_code[:, PACK * u * P : PACK * (u + 1) * P].bitcast(FP8X4),
                                    lhsT_scale=wo_scale[:, u * P : (u + 1) * P], rhs=h_code[:].bitcast(FP8X4), rhs_scale=h_scale[:],
                                    start=True, stop=True)
            if j0 + width == S:
                nc.vector.tensor_tensor(result[:], acc[:, : 2 * width].rearrange("p (u j) -> p u j", u=N // P),
                                        bo_sb[:].unsqueeze(2).to_broadcast([P, N // P, width]), ALU.add)
            for u in range(N // P if j0 + width < S else 0):
                nc.scalar.activation(result[:, u, :], accs[u], ACT.Identity, bias=bo_sb[:, u : u + 1])
                if width == HALF:
                    nc.sync.dma_start(out[u * P : (u + 1) * P, j0 : j0 + width], result[:, u, :])
            if width < HALF:
                nc.sync.dma_start(out.rearrange("(u p) j -> p u j", p=P)[:, :, j0 : j0 + width], result[:])

        blocks = S // BLOCK
        store_of, completed_by = {}, {}
        for n, width in enumerate(STORES):
            j0 = sum(STORES[:n])
            for b in range(j0 // BLOCK, (j0 + width) // BLOCK):
                store_of[b] = (j0, width)
            completed_by[(j0 + width) // BLOCK - 1] = (j0, width)
        c_banks = {b: product_c(b * BLOCK) for b in range(C_AHEAD)}
        h_rounds, h_quantised = {}, {}
        for b in range(blocks + 2):
            if b < blocks:
                j0, width = store_of[b]
                if j0 not in h_rounds:
                    h_rounds[j0] = sb([P, width * PACK], BF16, f"h_round{j0}")
                at = (b * BLOCK - j0) * PACK
                add_c(b * BLOCK, c_banks[b], h_rounds[j0][:, at : at + BLOCK * PACK])
            if b - 1 in completed_by:
                j0, width = completed_by[b - 1]
                h_quantised[j0] = quantise_h(j0, width, h_rounds[j0])
            if b + C_AHEAD < blocks:
                c_banks[b + C_AHEAD] = product_c((b + C_AHEAD) * BLOCK)
            if b - 2 in completed_by:
                j0, width = completed_by[b - 2]
                finish(j0, width, *h_quantised[j0])
